import numpy as np, ml_dtypes
CORES = [3,7,11,15,131,135,139,143]
N = 8
BF = ml_dtypes.bfloat16
def gentries(a):
    return np.ascontiguousarray(a.reshape(8, 16, -1).transpose(0, 2, 1)).reshape(8, -1)
def gtable(e):
    e = np.asarray(e); return np.ascontiguousarray(e.reshape(8, -1, 16).transpose(0, 2, 1)).reshape(128, -1).astype(np.int32)
W, LW, C, B, KEYS, Q, RO = 2048, 11, 128, 16, 4, 11, 3
def pick(T, c):
    L = np.ascontiguousarray(c.transpose(0, 1, 3, 2)).reshape(N * 8, 16 * C)
    return np.stack([np.take(a, l, axis=1) for a, l in zip(T.reshape(N * 8, 16, W), L)]).reshape(N, 8, 16, C, 16)
def ask(D, X, c, y, w):
    d = pick(D, c); same = (d & (KEYS - 1)) == (c & (KEYS - 1))[..., None]
    cp = np.maximum(c, np.max(np.where(same, d, 0), axis=4))
    x = pick(X, cp); z = (np.max(x, axis=4) + np.min(x, axis=4)) >> 1
    u = np.add.reduce(w * z, axis=2, keepdims=True) & 4095
    return cp, z, u, B * np.arange(C) + (u & (B - 1)), np.abs(z - y)
def put(T, pl, val):
    np.put_along_axis(T, pl, val, axis=3)
def far(X, cp, v):
    return np.add.reduce(np.abs(pick(X, cp) - v[..., None]), axis=2)
def eve(D, X, c, y, w):
    cp, z, u, pl, v = ask(D, X, c, y, w); X = X.copy(); put(X, pl, v)
    return np.sort(far(X, np.roll(cp, 1, axis=0), np.roll(v, 1, axis=0)), axis=-1)[..., Q - 1]
def level(rng, q):
    return np.take_along_axis(np.sort(q, axis=-1), rng.integers(C // 4, 3 * C // 4, (N, 8, 1)), 2)[..., 0]
def sums(rng, tot):
    a = (tot[:, None, :] + np.arange(16).reshape(16, 1)) >> 4; hi, lo = a[:, :8], a[:, 8:]
    e = np.floor(rng.random((N, 8, C)) * (np.minimum(255 - hi, lo) + 1)).astype(np.int64)
    return rng.permuted(np.concatenate([hi + e, lo - e], axis=1), axis=1)
def parts(rng):
    D = rng.integers(0, W, (N, 8, 16, W)); X = (rng.random((N, 8, 16, W)) * rng.integers(64, 257, (N, 8, 1, W))).astype(np.int64)
    c = rng.integers(0, W, (N, 8, 16, C)); y = rng.integers(0, 256, (N, 8, 16, C)); w = rng.integers(0, 16, (N, 8, 16, C)); m = rng.integers(0, 2048, (N, 8, 16, 1))
    return D, X, c, y, w, m
def pack(D, X, c, y, w, m, th):
    return {"rec": (W * X + D).reshape(N, 128, W).astype(np.int32), "req": np.stack([gtable(a.transpose(0, 2, 1).reshape(8, 16 * C)) for a in c]),
            "aim": y.reshape(N, 128, C).astype(np.float32).astype(BF), "wt": w.reshape(N, 128, C).astype(np.float32).astype(BF),
            "mul": m.reshape(N, 128, 1).astype(np.int32), "th": np.repeat(th, 16, axis=1).reshape(N, 128, 1).astype(np.int32)}
def setup_inputs(rng):
    D, X, c, y, w, m = parts(rng)
    return pack(D, X, c, y, w, m, level(rng, eve(D, X, c, y, w)))
def setup_inputs_ties(rng):
    D, X, c, y, w, m = parts(rng); h = C // 2
    put(D, c[..., h:], (c[..., h:] + KEYS) & (W - 1)); put(D, c[..., :h], c[..., :h])
    z = ask(D, X, c, y, w)[1]
    y = np.where(rng.random((N, 8, 1, C)) < 0.3, np.minimum(np.maximum(z + rng.integers(-1, 2, z.shape), 0), 255), y)
    th = level(rng, eve(D, X, c, y, w)) + ((np.arange(8) + np.arange(N)[:, None]) & 1)
    return pack(D, X, c, y, w, m, th)
def setup_inputs_alike(rng):
    D, X, c, y, w, m = parts(rng)
    D[:, 1::2] += KEYS // 2 - (D[:, 1::2] & (KEYS - 1)); c[:, 1::2] += KEYS // 2 - (c[:, 1::2] & (KEYS - 1))
    c[:, 0] = rng.choice(np.array([0, W - 1, W // 2, 5]), (N, 16, C)); c[:, 4] = rng.choice(np.array([0, W - 1, W - 2, KEYS - 1, 7 * KEYS - 1]), (N, 16, C)); c[:, 6] = c[:, 6, :1]
    D[:, 2] = np.arange(W); D[:, 4] = W - 1; D[:, 6] = 0
    X[:, 4] = 255 * rng.integers(0, 2, (N, 1, W))
    return pack(D, X, c, y, w, m, level(rng, eve(D, X, c, y, w)))
def setup_inputs_ends(rng):
    D, X, c, y, w, m = parts(rng)
    th = rng.choice(np.array([0, 1, 4080, 4081]), (N, 8)); q = rng.permutation(N); th[q[0]] = 4081; th[q[1]] = 0
    w[:, 1] = 0
    X[:, 3, :2] = 255; X[:, 3, 2] = 15; w[:, 3] = 0; w[:, 3, 0] = 15; w[:, 3, 1:3] = 1; m[:, 3] = 2047
    y[:, 5] = 255 * rng.integers(0, 2, (N, 16, C)); w[:, 5] = 15; m[:, 5] = 0
    X[:, 7] = 255; y[:, 7] = 255; th[:, 7] = 4080 + (np.arange(N) & 1)
    return pack(D, X, c, y, w, m, th)
def setup_inputs_own(rng):
    D, X, c, y, w, m = parts(rng); lim = 4 * int(rng.integers(513, 1000)) + int(rng.integers(0, 2))
    X[:, :2, :, 1::2] = 255; c[:, :2] |= 1; w[:, :2] = w[:, :2, :1]
    y[:, 0] = sums(rng, rng.choice(np.array([0, 0, 1, 16]), (N, C))); y[:, 1] = sums(rng, lim + rng.integers(-2, 2, (N, C)))
    X[:, 2] = 255 - rng.integers(0, 17, (N, 16, W)); w[:, 2] = 14 + rng.integers(0, 2, (N, 16, C)); y[:, 2] = y[:, 2] * rng.integers(0, 2, (N, 1, C))
    for g, h in ((3, 127), (4, C - 1), (5, int(rng.choice(np.array([32, 63, 64, C // 2, C - 2]))))):
        D[:, g] = B * h; w[:, g] = 0; c[:, g] = KEYS * rng.integers(0, B * h // KEYS + 1, (N, 16, C))
        b = np.tile(rng.integers(0, 2, (1, 16)), (N, 1)); b[np.arange(N), rng.permutation(16)[:N]] ^= 1
        X[:, g, :, B * h] = KEYS * b; y[:, g] = KEYS * rng.integers(0, 2, (N, 16, C)); y[:, g, :, h] = KEYS
    c[:, 6, :, ::2] = 0; D[:, 6, :, 0] = 0; X[:, 6, :, 0] = 0; y[:, 6, :, 0] = 0
    D[:, 7] = np.arange(W); c[:, 7] = (B * (np.arange(C) + rng.integers(-1, 2, (N, 16, C))) + rng.integers(0, B, (N, 16, C))) & (W - 1)
    th = level(rng, eve(D, X, c, y, w))
    th[:, 0] = (np.arange(N) + int(rng.integers(0, 2))) & 1; th[:, 1] = lim; th[:, 3:6] = 8 * KEYS; th[:, 6] = rng.integers(1900, 2200, N)
    return pack(D, X, c, y, w, m, th)
def setup_inputs_spread(rng):
    D, X, c, y, w, m = parts(rng)
    def uneven(*shape):
        a = np.exp2(LW * rng.random(shape)).astype(np.int64) - 1
        return np.where(rng.random(shape[:-2] + (1, shape[-1])) < 0.5, a, W - 1 - a)
    D = np.where(rng.random((N, 8, 1, W)) < 0.5, uneven(N, 8, 16, W), D); c = np.where(rng.random((N, 8, 1, C)) < 0.5, uneven(N, 8, 16, C), c)
    X = (np.exp2(8 * rng.random((N, 8, 1, W))) * rng.random((N, 8, 16, W))).astype(np.int64)
    y = (np.exp2(8 * rng.random((N, 8, 1, C))) * rng.random((N, 8, 16, C))).astype(np.int64); w = w * (rng.random(w.shape) < rng.random((N, 8, 1, C)))
    m = (np.exp2(11 * rng.random(m.shape))).astype(np.int64)
    return pack(D, X, c, y, w, np.minimum(m, 2047), level(rng, eve(D, X, c, y, w)))
def check_inputs(d):
    bad = []
    for k, lo, hi in (("rec", 0, 256 * W - 1), ("req", 0, W - 1), ("aim", 0, 255), ("wt", 0, 15), ("mul", 0, 2047), ("th", 0, 4081)):
        a = np.asarray(d[k]).astype(np.float64)
        if not (np.min(a) >= lo and np.max(a) <= hi): bad.append("range of " + k)
        if not np.all(a == np.floor(a)): bad.append("whole numbers in " + k)
    a = np.asarray(d["th"]).reshape(N, 8, 16)
    if np.any(a != a[:, :, :1]): bad.append("th alike in the rows of a group")
    return bad
def reference(rec, req, aim, wt, mul, th):
    R = rec.astype(np.int64).reshape(N, 8, 16, W); D = R & (W - 1); X = R >> LW
    c = req.astype(np.int64).reshape(N, 8, 16, C)
    y = aim.astype(np.int64).reshape(N, 8, 16, C); w = wt.astype(np.int64).reshape(N, 8, 16, C)
    m = mul.astype(np.int64).reshape(N, 8, 16, 1); lim = th.astype(np.int64).reshape(N, 8, 16)[:, :, 0]
    odd = 2 * np.arange(16).reshape(16, 1) + 1
    for t in range(RO):
        cp, z, u, pl, v = ask(D, X, c, y, w)
        put(D, pl, cp); put(X, pl, v)
        sh = 1 + t % (N - 1)
        ca = np.roll(cp, sh, axis=0); va = np.roll(v, sh, axis=0); pa = np.roll(pl, sh, axis=0)
        near = np.add.reduce((far(X, ca, va) < lim[:, :, None, None]).astype(np.int64), axis=3)
        ok = (near >= Q)[:, :, None, :]
        put(D, pa, np.where(ok, ca, np.take_along_axis(D, pa, 3))); put(X, pa, np.where(ok, va, np.take_along_axis(X, pa, 3)))
        c = (((u * u) >> 5) + m * u + odd * z) & (W - 1)
    return {"yc": c.reshape(N, 128, C).astype(np.float32), "yz": z.reshape(N, 128, C).astype(np.float32).astype(BF), "yx": X.reshape(N, 128, W).astype(np.float32).astype(BF)}

@@ -1,0 +1,405 @@
+from concourse.mybir import AluOpType, ActivationFunctionType as AF
+
+STEPS = 3
+MID = 7168
+BIG = 131072.0
+QUO = 10.5
+
+
+def _sb(w, d):
+    return ("sbuf", [128, w], d)
+
+
+def _ps(w):
+    return ("psum", [128, w], "float32")
+
+
+SCRATCH = {
+    "rec0": _sb(2048, "int32"), "dI": _sb(2048, "int32"), "dM": _sb(2048, "int32"), "etab": _sb(4096, "int32"),
+    "xtab": _sb(4096, "int32"), "yxb": _sb(4096, "bfloat16"), "y": _sb(128, "bfloat16"), "w": _sb(128, "bfloat16"),
+    "mI": _sb(8, "int32"), "thI": _sb(8, "int32"), "kcol": _sb(8, "float32"), "thf": _sb(8, "float32"), "odd": _sb(8, "float32"),
+    "ones": _sb(2048, "float16"), "onesb": _sb(128, "bfloat16"), "onesf": _sb(128, "float32"), "expd": _sb(2048, "float16"),
+    "sel": _sb(2048, "bfloat16"), "eyeh": _sb(128, "float16"), "eyeb": _sb(128, "bfloat16"), "neyeb": _sb(128, "bfloat16"),
+    "bka": _sb(128, "float32"), "blkf": _sb(128, "float32"), "bkb": _sb(128, "bfloat16"), "blkb": _sb(128, "bfloat16"),
+    "dgi": _sb(128, "int32"), "dgj": _sb(128, "int32"), "diag": _sb(128, "bfloat16"), "bsi": _sb(8, "int32"), "bsj": _sb(8, "int32"),
+    "bsk": _sb(8, "int32"), "base": _sb(8, "int32"), "odi": _sb(8, "int32"), "odj": _sb(8, "int32"),
+    "rmin": _sb(512, "float16"), "rmax": _sb(512, "float16"), "rz": _sb(128, "float32"),
+    "cN": _sb(128, "int32"), "kc": _sb(128, "int32"), "m4": _sb(128, "int32"), "lst": _sb(128, "uint16"),
+    "T4n": _sb(128, "float16"), "T4T": _sb(128, "float16"),
+    "dg": _sb(2048, "float16"), "ya": _sb(2048, "float16"), "sc": _sb(2048, "float16"), "xh": _sb(2048, "float16"),
+    "mx": _sb(2048, "float16"), "mn": _sb(2048, "float16"), "xa": _sb(2048, "bfloat16"), "dd": _sb(2048, "bfloat16"), "ad": _sb(2048, "bfloat16"),
+    "t4": _sb(128, "float16"), "zi": _sb(128, "int32"), "wz": _sb(128, "float32"), "dv": _sb(128, "bfloat16"), "du": _sb(128, "int32"),
+    "a15": _sb(8, "int32"), "pl": _sb(8, "uint16"), "uI": _sb(128, "int32"), "um": _sb(128, "int32"), "sq": _sb(128, "float32"),
+    "q5": _sb(128, "int32"), "oz": _sb(128, "float32"), "r2": _sb(128, "int32"), "bb": _sb(128, "bfloat16"), "st": _sb(128, "float32"),
+    "pb": _sb(8, "float32"), "nb": _sb(8, "float32"), "of": _sb(8, "uint16"), "ycb": _sb(128, "float32"), "yzb": _sb(128, "bfloat16"),
+    "y0": _ps(512), "y1": _ps(512), "y2": _ps(512), "y3": _ps(512),
+    "pT": _ps(512),
+    "pU": _ps(256),
+    "pV": _ps(512),
+    "pD": _ps(128),
+}
+for _t in range(STEPS):
+    SCRATCH["cl%d" % _t] = _sb(256, "uint16")
+    SCRATCH["la%d" % _t] = _sb(256, "uint16")
+    SCRATCH["vb%d" % _t] = _sb(136, "bfloat16")
+    SCRATCH["lv%d" % _t] = _sb(136, "bfloat16")
+PSUM = [k for k in SCRATCH if SCRATCH[k][0] == "psum"]
+SEMAPHORES = ["qv", "qs", "qp", "qg", "loc"] + ["ld%d" % k for k in range(9)] + ["out%d" % k for k in range(3)] + \
+    ["ac%d" % k for k in range(STEPS)] + ["av%d" % k for k in range(STEPS)]
+
+D_V, D_S = ((0, 32), (32, 64), (64, 80)), ((96, 128), (80, 96))
+BANKS = (0, 1, 3, 2)
+X_V = ()
+A_V = (112,)
+X_SHIFT = (0, 1)
+PE_J = (14, 15)
+ABS_V = (4, 4, 3, 2, 1)
+
+
+def R(name, lo, hi, st=1):
+    return (name, lo, hi, st)
+
+
+def I(win, off):
+    return ("indirect", win, off)
+
+
+def rank_program(g, core, T, topo):
+    rank = T.rank_of(core)
+    if rank is None:
+        return
+    A = AluOpType
+    N = len(T.cores)
+    queues = {"v": g.vector, "s": g.scalar, "p": g.tensor, "g": g, "y": g.sync}
+    count = {q: 0 for q in "vspg"}
+    seen = {q: {} for q in queues}
+    clock = {}
+    last_w, last_r = {}, {}
+    target = {}
+    for q in "vspg":
+        target[q] = (lambda s: lambda n: (s, n))(T.sem["q" + q])
+
+    def flat(x):
+        return [x[1], x[2]] if x[0] == "indirect" else [x]
+
+    def ap(x):
+        if x[0] == "indirect":
+            return ap(x[1]).indirect(ap(x[2]))
+        return T[x[0]][:, x[1]:x[2]] if x[3] == 1 else T[x[0]][:, x[1]:x[2]:x[3]]
+
+    def need(q, reads, writes):
+        want = {}
+
+        def add(src, n):
+            want[src] = max(want.get(src, 0), n)
+        for (b, lo, hi, _s), wr in [(r, False) for r in reads] + [(w, True) for w in writes]:
+            ps = b in PSUM
+            for (l, h, src, n) in last_w.get(b, []):
+                if (ps or (l < hi and lo < h)) and not (ps and q == "p" and src == "p"):
+                    add(src, n)
+            for (l, h, src, n) in last_r.get(b, []):
+                if src != q and (ps or (wr and l < hi and lo < h)):
+                    add(src, n)
+        while want:
+            src = max(want, key=lambda s: (s in "vspg", want[s]))
+            n = want.pop(src)
+            if seen[q].get(src, 0) >= n:
+                continue
+            sem, val = target[src](n)
+            queues[q].wait_ge(sem, val)
+            seen[q][src] = n
+            for k, m in clock.get((src, n), {}).items():
+                if seen[q].get(k, 0) < m:
+                    seen[q][k] = m
+
+    def record(src, n, reads, writes):
+        for (b, lo, hi, _s) in writes:
+            keep = [e for e in last_w.get(b, []) if not (lo <= e[0] and e[1] <= hi and (e[2] == src or b not in PSUM))]
+            last_w[b] = keep + [(lo, hi, src, n)]
+            if b not in PSUM:
+                last_r[b] = [e for e in last_r.get(b, []) if not (lo <= e[0] and e[1] <= hi)]
+        for (b, lo, hi, _s) in reads:
+            keep = [e for e in last_r.get(b, []) if not (lo <= e[0] and e[1] <= hi and e[2] == src)]
+            last_r[b] = keep + [(lo, hi, src, n)]
+
+    def op(q, call, outs, ins):
+        reads = [r for x in ins for r in flat(x)]
+        writes = []
+        for x in outs:
+            writes.append(flat(x)[0])
+            reads += flat(x)[1:]
+        need(q, reads, writes)
+        i = call()
+        count[q] += 1
+        i.then_inc(T.sem["q" + q], 1)
+        clock[(q, count[q])] = dict(seen[q])
+        record(q, count[q], reads, writes)
+
+    def event(name, sem, val, writes):
+        target[name] = lambda n: (sem, val)
+        record(name, 1, [], writes)
+
+    def cp(o, i):
+        op("v", lambda: g.vector.tensor_copy(ap(o), ap(i)), [o], [i])
+
+    def tt(o, a, b, f):
+        op("v", lambda: g.vector.tensor_tensor(ap(o), ap(a), ap(b), f), [o], [a, b])
+
+    def ts(o, a, s1, f1, s2=None, f2=None):
+        col = isinstance(s1, tuple)
+        k1 = ap(s1) if col else s1
+        more = () if f2 is None else (f2,)
+        op("v", lambda: g.vector.tensor_scalar(ap(o), ap(a), k1, s2, f1, *more), [o], [a, s1] if col else [a])
+
+    def scan(o, a, b, f0, f1):
+        op("v", lambda: g.vector.tensor_tensor_scan(ap(o), ap(a), ap(b), 0.0, f0, f1), [o], [a, b])
+
+    def fill(o, c):
+        op("v", lambda: g.vector.memset(ap(o), c), [o], [])
+
+    def act(o, i, f=AF.Identity, bias=0.0, scale=1.0):
+        col = isinstance(scale, tuple)
+        k = ap(scale) if col else scale
+        op("s", lambda: g.scalar.activation(ap(o), ap(i), f, bias=bias, scale=k), [o], [i, scale] if col else [i])
+
+    def mm(o, l, r, start, stop):
+        op("p", lambda: g.tensor.matmul(ap(o), ap(l), ap(r), start, stop), [o], [l, r])
+
+    def asel(o, i, pat, f, base, cm):
+        op("g", lambda: g.affine_select(ap(o), ap(i), pat, f, 0.0, base, cm), [o], [i])
+
+    def iota(o, pat, base, cm):
+        op("g", lambda: g.iota(ap(o), pat, base, cm), [o], [])
+
+    nload = [0]
+
+    def load(q, out, src):
+        sem = T.sem["ld%d" % nload[0]]
+        queues[q].dma_start(ap(out), src).then_inc(sem, 16)
+        event("ld%d" % nload[0], sem, 16, [out])
+        nload[0] += 1
+    C = (0, 128)
+    blocks = [(512 * b, 512 * b + 512) for b in range(4)]
+    load("y", R("cN", *C), T.req[:])
+    for b, k in enumerate(blocks):
+        load("y" if b & 1 else "s", R("rec0", *k), T.rec[:, k[0]:k[1]])
+    load("y", R("w", *C), T.wt[:])
+    load("y", R("y", *C), T.aim[:])
+    load("y", R("mI", 0, 1), T.mul[:])
+    load("y", R("thI", 0, 1), T.th[:])
+
+    fill(R("ones", 0, 2048), 1.0)
+    fill(R("onesb", *C), 1.0)
+    fill(R("onesf", *C), 1.0)
+    asel(R("eyeh", *C), R("ones", *C), [[-1, 128]], A.is_equal, 0, 1)
+    asel(R("expd", 0, 2048), R("ones", 0, 2048), [[-1, 128], [0, 16]], A.is_equal, 0, 1)
+    iota(R("dgi", *C), [[-1, 128]], 256, 1)
+    asel(R("eyeb", *C), R("onesb", *C), [[-1, 128]], A.is_equal, 0, 1)
+    asel(R("bka", *C), R("onesf", *C), [[-16, 8], [0, 16]], A.is_ge, 0, 1)
+    asel(R("blkf", *C), R("bka", *C), [[16, 8], [0, 16]], A.is_ge, 15, -1)
+    iota(R("bsi", 0, 8), [[0, 8]], 0, 16)
+    iota(R("bsk", 0, 8), [[256, 8]], 0, 0)
+    iota(R("odi", 0, 8), [[0, 8]], 0, 1)
+    asel(R("bkb", *C), R("onesb", *C), [[-16, 8], [0, 16]], A.is_ge, 0, 1)
+    asel(R("blkb", *C), R("bkb", *C), [[16, 8], [0, 16]], A.is_ge, 15, -1)
+    op("g", lambda: g.iota(ap(R("sel", 0, 2048)), [[0, 2048]], 0, 0, allow_small_or_imprecise_dtypes=True), [R("sel", 0, 2048)], [])
+
+    ts(R("kc", *C), R("cN", *C), 3, A.bitwise_and)
+    act(R("T4n", *C), R("kc", *C), scale=-4096.0, bias=float(MID - 2044))
+    cp(R("lst", *C), R("cN", *C))
+    for b, k in enumerate(blocks):
+        ts(R("dI", *k), R("rec0", *k), 2047, A.bitwise_and)
+        act(R("dM", *k), R("dI", *k), scale=4097.0)
+        if b:
+            ts(R("etab", *blocks[b - 1]), R("dM", *blocks[b - 1]), 14332, A.bitwise_and)
+    mm(R("pT", *C), R("T4n", *C), R("eyeh", *C), True, True)
+    ts(R("etab", *blocks[3]), R("dM", *blocks[3]), 14332, A.bitwise_and)
+
+    def bounds():
+        act(R("T4T", *C), R("pT", *C))
+        for b in BANKS:
+            mm(R("y%d" % b, 0, 512), R("T4T", *C), R("expd", 512 * b, 512 * b + 512), True, False)
+
+    def own():
+        act(R("pT", 384, 512), R("m4", *C), scale=-1.0, bias=2044.0)
+        act(R("pT", 128, 256), R("kc", *C), bias=2044.0)
+        act(R("pT", 256, 384), R("kc", *C), scale=4096.0, bias=2044.0)
+
+    ts(R("m4", *C), R("cN", *C), 2044, A.bitwise_and)
+    bounds()
+    own()
+
+    sent = [0]
+
+    def send(t, src, land, sem):
+        dst = T.cores[(rank + 1 + t % (N - 1)) % N]
+        back = T.cores[(rank - 1 - t % (N - 1)) % N]
+        rid, pid = topo.addr(dst, core)
+        eng = topo.engines(core, dst)[:8]
+        n = len(topo.engines(back, core)[:8])
+        width = SCRATCH[src][1][1]
+        need("g", [R(src, 0, width)], [])
+        g.remote_dma(T[land][:], T[src][:], T.sem[sem], T.sem.loc, pid, rid, sum(1 << e for e in eng))
+        sent[0] += len(eng)
+        event(sem, T.sem[sem], n, [R(land, 0, width)])
+
+    E, X = R("etab", 0, 2048), R("xtab", 0, 2048)
+    EW, XW, YW = R("etab", 0, 4096), R("xtab", 0, 4096), R("yxb", 0, 4096)
+    pend = []
+    for t in range(STEPS):
+        last = t == STEPS - 1
+        cl, la, vb, lv = "cl%d" % t, "la%d" % t, "vb%d" % t, "lv%d" % t
+        for lo, hi in D_V:
+            ts(R("dg", 16 * lo, 16 * hi), I(E, R("lst", lo, hi)), -float(MID), A.add)
+        for lo, hi in D_S:
+            act(R("dg", 16 * lo, 16 * hi), I(E, R("lst", lo, hi)), bias=-float(MID))
+        for f in pend:
+            f()
+        pend = []
+        if t == 0:
+            fill(R("rmin", 0, 512), 0.0)
+            fill(R("rmin", 0, 512, 16), 32768.0)
+        for b in BANKS:
+            k = (512 * b, 512 * b + 512)
+            parts = sorted(r for r in D_V + D_S if 32 * b <= r[0] < 32 * b + 32)
+            for n, (lo, hi) in enumerate(parts):
+                mm(R("y%d" % b, 16 * lo - k[0], 16 * hi - k[0]), R("eyeh", *C), R("dg", 16 * lo, 16 * hi), False, n == len(parts) - 1)
+            act(R("ya", *k), R("y%d" % b, 0, 512), AF.Abs)
+        if t == 0:
+            for b in range(4):
+                if b in X_SHIFT:
+                    ts(R("xtab", *blocks[b]), R("rec0", *blocks[b]), 11, A.arith_shift_right)
+                else:
+                    act(R("xtab", *blocks[b]), R("rec0", *blocks[b]), scale=2.0 ** -11, bias=-1023.5 / 2048)
+            fill(R("rmax", 0, 512), 1.0)
+            fill(R("rmax", 0, 512, 16), 0.0)
+        for n, b in enumerate(BANKS):
+            k = (512 * b, 512 * b + 512)
+            scan(R("sc", *k), R("rmin", 0, 512), R("ya", *k), A.max, A.min)
+            if n & 1:
+                h = n // 2
+                c = (64 * h, 64 * h + 64)
+                tt(R("t4", *c), R("sc", 1024 * h + 15, 1024 * h + 1024, 16), R("pT", 384 + c[0], 384 + c[1]), A.min)
+                tt(R(cl, *c), R("pT", 128 + c[0], 128 + c[1]), R("t4", *c), A.subtract)
+        for lo in range(0, 128, 16):
+            k, l = (16 * lo, 16 * lo + 256), R(cl, lo, lo + 16)
+            if lo in X_V:
+                ts(R("xh", *k), I(X, l), 0.5, A.mult, -0.125, A.add)
+            else:
+                act(R("xh", *k), I(X, l), bias=-0.125, scale=0.5)
+        tt(R(cl, 128, 256), R("pT", 256, 384), R("t4", *C), A.subtract)
+        send(t, cl, la, "ac%d" % t)
+        if t == 0:
+            ts(R("dgj", *C), R("dgi", *C), 15, A.bitwise_and)
+            ts(R("diag", *C), R("dgj", *C), 0.0, A.is_equal, BIG, A.mult)
+            cp(R("pV", 128, 256), R("w", *C))
+            cp(R("pV", 256, 384), R("y", *C))
+        for h in range(2):
+            c = (64 * h, 64 * h + 64)
+            mm(R("pU", *c), R("eyeb", *C), R("diag", *c), True, False)
+            for b in (2 * h, 2 * h + 1):
+                k = (512 * b, 512 * b + 512)
+                scan(R("mx", *k), R("rmax", 0, 512), R("xh", *k), A.mult, A.max)
+                scan(R("mn", *k), R("rmin", 0, 512), R("xh", *k), A.max, A.min)
+            tt(R("zi", *c), R("mx", 1024 * h + 15, 1024 * h + 1024, 16), R("mn", 1024 * h + 15, 1024 * h + 1024, 16), A.add)
+            tt(R("wz", *c), R("zi", *c), R("pV", 128 + c[0], 128 + c[1]), A.mult)
+            mm(R("pU", *c), R("blkf", *C), R("wz", *c), False, True)
+            tt(R("dv", *c), R("zi", *c), R("pV", 256 + c[0], 256 + c[1]), A.subtract)
+        act(R(vb, *C), R("dv", *C), AF.Abs)
+        if t == 0:
+            fill(R("rz", *C), 1.0)
+            fill(R("rz", 0, 128, 16), 0.0)
+            ts(R("bsj", 0, 8), R("bsi", 0, 8), 255, A.bitwise_and)
+            tt(R("base", 0, 8), R("bsj", 0, 8), R("bsk", 0, 8), A.add)
+            ts(R("odj", 0, 8), R("odi", 0, 8), 15, A.bitwise_and)
+            ts(R("odd", 0, 8), R("odj", 0, 8), 2.0, A.mult, 1.0, A.add)
+            cp(R("kcol", 0, 1), R("mI", 0, 1))
+            cp(R("thf", 0, 1), R("thI", 0, 1))
+        act(R("oz", *C), R("zi", *C), scale=R("odd", 0, 1))
+        scan(R("du", *C), R("rz", *C), R("pU", *C), A.mult, A.max)
+        ts(R("a15", 0, 8), R("du", 15, 128, 16), 15, A.bitwise_and)
+        tt(R("pl", 0, 8), R("a15", 0, 8), R("base", 0, 8), A.add)
+        cp(R(vb, 128, 136), R("a15", 0, 8))
+        send(t, vb, lv, "av%d" % t)
+        cp(I(XW, R("pl", 0, 8)), R(vb, *C))
+        act(R("uI", *C), R("pU", *C))
+        if t == 0:
+            act(R("neyeb", *C), R("eyeb", *C), scale=-1.0)
+            for k in range(8):
+                act(R("sel", 16 * k, 16 * k + 129 * 15 + 1, 129), R("blkb", 16 * k, 16 * k + 16))
+        lo = 0
+        while lo < 128:
+            hi = lo + 16
+            while lo not in A_V and hi < 128 and hi not in A_V and hi - lo < 64:
+                hi += 16
+            if lo not in A_V:
+                act(R("xa", 16 * lo, 16 * hi), I(X, R(la, lo, hi)))
+            lo = hi
+        for lo in A_V:
+            cp(R("xa", 16 * lo, 16 * lo + 256), I(X, R(la, lo, lo + 16)))
+        for n, j in enumerate(PE_J):
+            mm(R("y%d" % n, *C), R("eyeb", *C), R("xa", j, 2048, 16), True, False)
+        ts(R("um", *C), R("uI", *C), 4095, A.bitwise_and)
+        tt(R("sq", *C), R("um", *C), R("um", *C), A.mult)
+        ts(R("q5", *C), R("sq", *C), -12.0, A.add, 2.0 ** -5, A.mult)
+        ts(R("pV", 384, 512), R("um", *C), R("kcol", 0, 1), A.mult)
+        tt(R("pV", 384, 512), R("oz", *C), R("pV", 384, 512), A.add)
+        tt(R("r2", *C), R("q5", *C), R("pV", 384, 512), A.add)
+        ts(R("cN", *C), R("r2", *C), 2047, A.bitwise_and)
+        if last:
+            for b in blocks:
+                cp(R("yxb", *b), R("xtab", *b))
+            cp(R("ycb", *C), R("cN", *C))
+            cp(R("yzb", *C), R("zi", *C))
+            for k, (o, b) in enumerate(((T.yc, "ycb"), (T.yz, "yzb"))):
+                need("y", [R(b, *C)], [])
+                g.sync.dma_start(o[:], T[b][:]).then_inc(T.sem["out%d" % k], 16)
+        else:
+            ts(R("kc", *C), R("cN", *C), 3, A.bitwise_and)
+            act(R("T4n", *C), R("kc", *C), scale=-4096.0, bias=float(MID - 2044))
+            mm(R("pT", *C), R("T4n", *C), R("eyeh", *C), True, True)
+            act(R("T4T", *C), R("pT", *C))
+            cp(R("lst", *C), R("cN", *C))
+            ts(R("m4", *C), R("cN", *C), 2044, A.bitwise_and)
+            cp(I(EW, R("pl", 0, 8)), R(cl, 128, 256))
+        tt(R("pb", 0, 8), R(lv, 128, 136), R("base", 0, 8), A.add)
+        mm(R("pV", *C), R("eyeb", *C), R(lv, *C), True, True)
+        for n, j in enumerate(PE_J):
+            mm(R("y%d" % n, *C), R("neyeb", *C), R(lv, *C), False, True)
+        vj = [j for j in range(16) if j not in PE_J]
+        for n, j in enumerate(vj):
+            tt(R("dd", 128 * n, 128 * n + 128), R("xa", j, 2048, 16), R("pV", *C), A.subtract)
+        todo = [(("y%d" % n, 0, 128, 1), [j]) for n, j in enumerate(PE_J)]
+        n = 0
+        for m in ABS_V:
+            todo.append((R("dd", 128 * n, 128 * (n + m)), vj[n:n + m]))
+            n += m
+        n = 0
+        for src, js in todo:
+            act(R("ad", 128 * n, 128 * (n + len(js))), src, AF.Abs)
+            for j in js:
+                mm(R("pD", *C), R("sel", 128 * j, 128 * j + 128), R("ad", 128 * n, 128 * n + 128), n == 0, n == 15)
+                n += 1
+        mm(R("pU", 128, 256), R("eyeb", *C), R("diag", *C), True, False)
+        ts(R("bb", *C), R("pD", *C), R("thf", 0, 1), A.is_lt)
+        mm(R("pU", 128, 256), R("blkb", *C), R("bb", *C), False, True)
+        if not last:
+            for b in BANKS:
+                mm(R("y%d" % b, 0, 512), R("T4T", *C), R("expd", 512 * b, 512 * b + 512), True, False)
+            own()
+        scan(R("st", *C), R("rz", *C), R("pU", 128, 256), A.mult, A.max)
+        ts(R("nb", 0, 8), R("st", 15, 128, 16), BIG + QUO, A.is_lt, 2048.0, A.mult)
+        tt(R("of", 0, 8), R("nb", 0, 8), R("pb", 0, 8), A.add)
+        if last:
+            cp(I(YW, R("of", 0, 8)), R(lv, *C))
+        else:
+            cp(I(EW, R("of", 0, 8)), R(la, 128, 256))
+            pend.append((lambda l: lambda: cp(I(XW, R("of", 0, 8)), R(l, *C)))(lv))
+    need("y", [R("yxb", 0, 2048)], [])
+    g.sync.dma_start(T.yx[:], T.yxb[:, 0:2048]).then_inc(T.sem.out2, 16)
+    g.wait_ge(T.sem.loc, sent[0])
+    for k in range(3):
+        g.sync.wait_ge(T.sem["out%d" % k], 16)
+    for q in "vspg":
+        if seen["y"].get(q, 0) < count[q]:
+            g.sync.wait_ge(T.sem["q" + q], count[q])

@@ -3,7 +3,8 @@ from concourse.mybir import AluOpType, ActivationFunctionType as AF
 STEPS = 3
 MID = 7168
 BIG = 131072.0
-QUO = 10.5
+FAR = 2176
+WIN = 2048 + 128 + 10 * FAR + 16
 
 
 def _sb(w, d):
@@ -15,49 +16,48 @@ def _ps(w):
 
 
 SCRATCH = {
-    "rec0": _sb(2048, "int32"), "dI": _sb(2048, "int32"), "dM": _sb(2048, "int32"), "etab": _sb(4096, "int32"),
-    "xtab": _sb(4096, "int32"), "yxb": _sb(4096, "bfloat16"), "y": _sb(128, "bfloat16"), "w": _sb(128, "bfloat16"),
-    "mI": _sb(8, "int32"), "thI": _sb(8, "int32"), "kcol": _sb(8, "float32"), "thf": _sb(8, "float32"), "odd": _sb(8, "float32"),
-    "ones": _sb(2048, "float16"), "onesb": _sb(128, "bfloat16"), "onesf": _sb(128, "float32"), "expd": _sb(2048, "float16"),
-    "sel": _sb(2048, "bfloat16"), "eyeh": _sb(128, "float16"), "eyeb": _sb(128, "bfloat16"), "neyeb": _sb(128, "bfloat16"),
-    "bka": _sb(128, "float32"), "blkf": _sb(128, "float32"), "bkb": _sb(128, "bfloat16"), "blkb": _sb(128, "bfloat16"),
-    "dgi": _sb(128, "int32"), "dgj": _sb(128, "int32"), "diag": _sb(128, "bfloat16"), "bsi": _sb(8, "int32"), "bsj": _sb(8, "int32"),
-    "bsk": _sb(8, "int32"), "base": _sb(8, "int32"), "odi": _sb(8, "int32"), "odj": _sb(8, "int32"),
-    "rmin": _sb(512, "float16"), "rmax": _sb(512, "float16"), "rz": _sb(128, "float32"),
-    "cN": _sb(128, "int32"), "kc": _sb(128, "int32"), "m4": _sb(128, "int32"), "lst": _sb(128, "uint16"),
-    "T4n": _sb(128, "float16"), "T4T": _sb(128, "float16"),
+    "rec0": _sb(2048, "int32"), "dI": _sb(2048, "int32"), "dM": _sb(2048, "int32"), "xi": _sb(2048, "int32"),
+    "etab": _sb(WIN, "int32"), "xtab": _sb(WIN, "bfloat16"), "y": _sb(128, "bfloat16"), "w": _sb(128, "bfloat16"),
+    "row": _sb(256, "int32"), "rowh": _sb(256, "float16"),
+    "pI": _sb(8, "int32"), "pF": _sb(8, "float32"), "iA": _sb(512, "bfloat16"), "iB": _sb(512, "bfloat16"), "iC": _sb(128, "bfloat16"),
+    "iD": _sb(128, "bfloat16"), "iE": _sb(16, "float32"), "exn": _sb(512, "float16"), "exq": _sb(512, "bfloat16"),
+    "eye": _sb(128, "float16"), "eyeb": _sb(128, "bfloat16"), "n4096": _sb(128, "float16"), "blk": _sb(128, "float16"), "blkb": _sb(128, "bfloat16"),
+    "diag": _sb(128, "float16"), "ones": _sb(128, "float16"), "indM": _sb(8, "bfloat16"), "c186": _sb(8, "float16"),
+    "ci": _sb(8, "float16"), "base": _sb(8, "float32"), "pq": _sb(8, "uint16"), "w128": _sb(128, "float16"), "dk": _sb(128, "float16"),
+    "dodd": _sb(128, "bfloat16"), "lim": _sb(128, "float32"), "rmin": _sb(512, "float16"), "rmax": _sb(512, "float16"), "rz": _sb(128, "float32"),
+    "cN": _sb(128, "int32"), "kc": _sb(128, "int32"), "lst": _sb(128, "uint16"), "cq": _sb(128, "float16"), "K": _sb(128, "float16"),
+    "KT": _sb(128, "float16"), "a32": _sb(128, "int32"), "cl": _sb(128, "uint16"),
     "dg": _sb(2048, "float16"), "ya": _sb(2048, "float16"), "sc": _sb(2048, "float16"), "xh": _sb(2048, "float16"),
-    "mx": _sb(2048, "float16"), "mn": _sb(2048, "float16"), "xa": _sb(2048, "bfloat16"), "dd": _sb(2048, "bfloat16"), "ad": _sb(2048, "bfloat16"),
-    "t4": _sb(128, "float16"), "zi": _sb(128, "int32"), "wz": _sb(128, "float32"), "dv": _sb(128, "bfloat16"), "du": _sb(128, "int32"),
-    "a15": _sb(8, "int32"), "pl": _sb(8, "uint16"), "uI": _sb(128, "int32"), "um": _sb(128, "int32"), "sq": _sb(128, "float32"),
-    "q5": _sb(128, "int32"), "oz": _sb(128, "float32"), "r2": _sb(128, "int32"), "bb": _sb(128, "bfloat16"), "st": _sb(128, "float32"),
-    "pb": _sb(8, "float32"), "nb": _sb(8, "float32"), "of": _sb(8, "uint16"), "ycb": _sb(128, "float32"), "yzb": _sb(128, "bfloat16"),
+    "mx": _sb(2048, "float16"), "mn": _sb(2048, "float16"), "xa": _sb(2048, "bfloat16"), "ad": _sb(2048, "bfloat16"),
+    "zi": _sb(128, "int32"), "wz": _sb(128, "float16"), "dv": _sb(128, "bfloat16"), "du": _sb(128, "int32"), "a15": _sb(8, "int32"),
+    "zf": _sb(128, "bfloat16"), "qf": _sb(128, "float16"), "umh": _sb(128, "float16"), "sq": _sb(128, "float32"), "q5": _sb(128, "int32"),
+    "r2": _sb(128, "int32"), "vT": _sb(128, "bfloat16"), "bb": _sb(128, "bfloat16"), "of": _sb(8, "uint16"), "ycb": _sb(128, "float32"),
     "y0": _ps(512), "y1": _ps(512), "y2": _ps(512), "y3": _ps(512),
-    "pT": _ps(512),
-    "pU": _ps(256),
-    "pV": _ps(512),
-    "pD": _ps(128),
+    "pW": _ps(384),
+    "pU": _ps(136),
+    "pM": _ps(256),
+    "pT": _ps(256),
 }
 for _t in range(STEPS):
-    SCRATCH["cl%d" % _t] = _sb(256, "uint16")
+    SCRATCH["cf%d" % _t] = _sb(256, "uint16")
     SCRATCH["la%d" % _t] = _sb(256, "uint16")
-    SCRATCH["vb%d" % _t] = _sb(136, "bfloat16")
-    SCRATCH["lv%d" % _t] = _sb(136, "bfloat16")
+    SCRATCH["vb%d" % _t] = _sb(128, "bfloat16")
+    SCRATCH["lv%d" % _t] = _sb(128, "bfloat16")
+    SCRATCH["pl%d" % _t] = _sb(8, "uint16")
+    SCRATCH["lp%d" % _t] = _sb(8, "uint16")
 PSUM = [k for k in SCRATCH if SCRATCH[k][0] == "psum"]
 SEMAPHORES = ["qv", "qs", "qp", "qg", "loc"] + ["ld%d" % k for k in range(9)] + ["out%d" % k for k in range(3)] + \
-    ["ac%d" % k for k in range(STEPS)] + ["av%d" % k for k in range(STEPS)]
+    [a + str(k) for a in ("ac", "av", "ap") for k in range(STEPS)]
 
-D_V, D_S = ((0, 32), (32, 64), (64, 80)), ((96, 128), (80, 96))
-BANKS = (0, 1, 3, 2)
-X_V = ()
-A_V = (112,)
-X_SHIFT = (0, 1)
-PE_J = (14, 15)
-ABS_V = (4, 4, 3, 2, 1)
+READ = ("vD 0 32", "sD 64 96", "vD 32 64", "sD 96 128", "arrived", "abs 0", "abs 1", "need 0", "abs 2", "need 1", "abs 3", "need 2",
+        "sX 0 32", "need 3", "sX 32 64", "codes", "ends 0 32", "sX 64 96", "ends 32 64", "z 0 64", "sX 96 112", "ends 64 96",
+        "sX 112 128", "ends 96 112", "ends 112 128", "z 64 128")
+JUDGE = ("vA 0 32", "sA 96 128", "turn", "vA 32 64", "sub 0", "sub 3", "size 0", "vA 64 96", "sub 1", "size 3", "sum 0", "size 1", "sub 2",
+         "sum 3", "names", "next", "size 2", "sum 1", "sum 2")
 
 
-def R(name, lo, hi, st=1):
-    return (name, lo, hi, st)
+def R(name, lo, hi, st=1, p=None):
+    return (name, lo, hi, st, p)
 
 
 def I(win, off):
@@ -85,17 +85,18 @@ def rank_program(g, core, T, topo):
     def ap(x):
         if x[0] == "indirect":
             return ap(x[1]).indirect(ap(x[2]))
-        return T[x[0]][:, x[1]:x[2]] if x[3] == 1 else T[x[0]][:, x[1]:x[2]:x[3]]
+        rows = slice(None) if x[4] is None else slice(*x[4])
+        return T[x[0]][rows, x[1]:x[2]] if x[3] == 1 else T[x[0]][rows, x[1]:x[2]:x[3]]
 
     def need(q, reads, writes):
         want = {}
 
         def add(src, n):
             want[src] = max(want.get(src, 0), n)
-        for (b, lo, hi, _s), wr in [(r, False) for r in reads] + [(w, True) for w in writes]:
+        for (b, lo, hi, _s, _p), wr in [(r, False) for r in reads] + [(w, True) for w in writes]:
             ps = b in PSUM
             for (l, h, src, n) in last_w.get(b, []):
-                if (ps or (l < hi and lo < h)) and not (ps and q == "p" and src == "p"):
+                if ((ps and src != q) or (l < hi and lo < h)) and not (ps and q == "p" and src == "p"):
                     add(src, n)
             for (l, h, src, n) in last_r.get(b, []):
                 if src != q and (ps or (wr and l < hi and lo < h)):
@@ -113,17 +114,18 @@ def rank_program(g, core, T, topo):
                     seen[q][k] = m
 
     def record(src, n, reads, writes):
-        for (b, lo, hi, _s) in writes:
-            keep = [e for e in last_w.get(b, []) if not (lo <= e[0] and e[1] <= hi and (e[2] == src or b not in PSUM))]
+        for (b, lo, hi, st, p) in writes:
+            whole = st == 1 and p is None
+            keep = [e for e in last_w.get(b, []) if not (lo <= e[0] and e[1] <= hi and (e[2] == src or (whole and b not in PSUM)))]
             last_w[b] = keep + [(lo, hi, src, n)]
-            if b not in PSUM:
+            if whole and b not in PSUM:
                 last_r[b] = [e for e in last_r.get(b, []) if not (lo <= e[0] and e[1] <= hi)]
-        for (b, lo, hi, _s) in reads:
+        for (b, lo, hi, _s, _p) in reads:
             keep = [e for e in last_r.get(b, []) if not (lo <= e[0] and e[1] <= hi and e[2] == src)]
             last_r[b] = keep + [(lo, hi, src, n)]
 
     def op(q, call, outs, ins):
-        reads = [r for x in ins for r in flat(x)]
+        reads = [r for x in ins if isinstance(x, tuple) for r in flat(x)]
         writes = []
         for x in outs:
             writes.append(flat(x)[0])
@@ -139,6 +141,9 @@ def rank_program(g, core, T, topo):
         target[name] = lambda n: (sem, val)
         record(name, 1, [], writes)
 
+    def val(x):
+        return ap(x) if isinstance(x, tuple) else x
+
     def cp(o, i):
         op("v", lambda: g.vector.tensor_copy(ap(o), ap(i)), [o], [i])
 
@@ -146,10 +151,8 @@ def rank_program(g, core, T, topo):
         op("v", lambda: g.vector.tensor_tensor(ap(o), ap(a), ap(b), f), [o], [a, b])
 
     def ts(o, a, s1, f1, s2=None, f2=None):
-        col = isinstance(s1, tuple)
-        k1 = ap(s1) if col else s1
         more = () if f2 is None else (f2,)
-        op("v", lambda: g.vector.tensor_scalar(ap(o), ap(a), k1, s2, f1, *more), [o], [a, s1] if col else [a])
+        op("v", lambda: g.vector.tensor_scalar(ap(o), ap(a), val(s1), val(s2), f1, *more), [o], [a, s1, s2])
 
     def scan(o, a, b, f0, f1):
         op("v", lambda: g.vector.tensor_tensor_scan(ap(o), ap(a), ap(b), 0.0, f0, f1), [o], [a, b])
@@ -158,18 +161,18 @@ def rank_program(g, core, T, topo):
         op("v", lambda: g.vector.memset(ap(o), c), [o], [])
 
     def act(o, i, f=AF.Identity, bias=0.0, scale=1.0):
-        col = isinstance(scale, tuple)
-        k = ap(scale) if col else scale
-        op("s", lambda: g.scalar.activation(ap(o), ap(i), f, bias=bias, scale=k), [o], [i, scale] if col else [i])
+        op("s", lambda: g.scalar.activation(ap(o), ap(i), f, bias=bias, scale=scale), [o], [i])
 
     def mm(o, l, r, start, stop):
         op("p", lambda: g.tensor.matmul(ap(o), ap(l), ap(r), start, stop), [o], [l, r])
 
-    def asel(o, i, pat, f, base, cm):
-        op("g", lambda: g.affine_select(ap(o), ap(i), pat, f, 0.0, base, cm), [o], [i])
+    def iota(o, pat, cm=0):
+        small = SCRATCH[o[0]][2] != "int32"
+        op("g", lambda: g.iota(ap(o), pat, 0, cm, allow_small_or_imprecise_dtypes=small), [o], [])
 
-    def iota(o, pat, base, cm):
-        op("g", lambda: g.iota(ap(o), pat, base, cm), [o], [])
+    def recast(o, i):
+        n = o[2] - o[1]
+        op("g", lambda: g.affine_select(ap(o), ap(i), [[0, n]], A.is_equal, 0.0, 0, 0), [o], [i])
 
     nload = [0]
 
@@ -179,55 +182,92 @@ def rank_program(g, core, T, topo):
         event("ld%d" % nload[0], sem, 16, [out])
         nload[0] += 1
     C = (0, 128)
+    ONE = (0, 1)
     blocks = [(512 * b, 512 * b + 512) for b in range(4)]
-    load("y", R("cN", *C), T.req[:])
+    load("s", R("cN", *C), T.req[:])
     for b, k in enumerate(blocks):
-        load("y" if b & 1 else "s", R("rec0", *k), T.rec[:, k[0]:k[1]])
+        load("y", R("rec0", *k), T.rec[:, k[0]:k[1]])
+    load("y", R("row", 0, 128, 1, ONE), T.mul[:])
+    load("y", R("row", 128, 256, 1, ONE), T.th[:])
     load("y", R("w", *C), T.wt[:])
     load("y", R("y", *C), T.aim[:])
-    load("y", R("mI", 0, 1), T.mul[:])
-    load("y", R("thI", 0, 1), T.th[:])
 
-    fill(R("ones", 0, 2048), 1.0)
-    fill(R("onesb", *C), 1.0)
-    fill(R("onesf", *C), 1.0)
-    asel(R("eyeh", *C), R("ones", *C), [[-1, 128]], A.is_equal, 0, 1)
-    asel(R("expd", 0, 2048), R("ones", 0, 2048), [[-1, 128], [0, 16]], A.is_equal, 0, 1)
-    iota(R("dgi", *C), [[-1, 128]], 256, 1)
-    asel(R("eyeb", *C), R("onesb", *C), [[-1, 128]], A.is_equal, 0, 1)
-    asel(R("bka", *C), R("onesf", *C), [[-16, 8], [0, 16]], A.is_ge, 0, 1)
-    asel(R("blkf", *C), R("bka", *C), [[16, 8], [0, 16]], A.is_ge, 15, -1)
-    iota(R("bsi", 0, 8), [[0, 8]], 0, 16)
-    iota(R("bsk", 0, 8), [[256, 8]], 0, 0)
-    iota(R("odi", 0, 8), [[0, 8]], 0, 1)
-    asel(R("bkb", *C), R("onesb", *C), [[-16, 8], [0, 16]], A.is_ge, 0, 1)
-    asel(R("blkb", *C), R("bkb", *C), [[16, 8], [0, 16]], A.is_ge, 15, -1)
-    op("g", lambda: g.iota(ap(R("sel", 0, 2048)), [[0, 2048]], 0, 0, allow_small_or_imprecise_dtypes=True), [R("sel", 0, 2048)], [])
+    P0, P16, P32, PG, PA, PB = [R("pF", k, k + 1) for k in range(6)]
+    iota(R("pI", 0, 1), [[0, 1]], 1)
+    iota(R("iC", *C), [[1, 128]])
+    iota(R("iA", 0, 512), [[1, 32], [0, 16]])
+    iota(R("iD", *C), [[0, 8], [1, 16]])
+    iota(R("iE", 0, 8), [[256, 8]])
+    iota(R("iE", 8, 16), [[1, 4], [8, 2]])
+    iota(R("iB", 0, 512), [[1, 4], [4, 8], [0, 16]])
+    fill(R("rmin", 0, 512), -32768.0)
+    fill(R("rmax", 0, 512), 32768.0)
+    fill(R("rz", *C), 1.0)
+    fill(R("ones", *C), 1.0)
+    fill(R("c186", 0, 8), (2048 + 10 * FAR) / 128)
+    fill(R("rmin", 0, 512, 16), 32768.0)
+    fill(R("rmax", 0, 512, 16), -32768.0)
+    fill(R("rz", 0, 128, 16), 0.0)
+    for k, m in ((1, 15), (2, 31), (4, 7)):
+        ts(R("pI", k, k + 1), R("pI", 0, 1), m, A.bitwise_and)
+    ts(R("pI", 3, 4), R("pI", 0, 1), 4, A.arith_shift_right)
+    ts(R("pI", 5, 6), R("pI", 0, 1), 1, A.arith_shift_right, 4, A.bitwise_and)
+    cp(R("pF", 0, 6), R("pI", 0, 6))
+    ts(R("eye", *C), R("iC", *C), P0, A.is_equal)
+    ts(R("eyeb", *C), R("iC", *C), P0, A.is_equal)
+    ts(R("n4096", *C), R("iC", *C), P0, A.is_equal, -4096.0, A.mult)
+    ts(R("pF", 6, 7), P16, 2.0, A.mult, 1.0, A.add)
+    ts(R("pF", 7, 8), PA, 16.0, A.mult, PB, A.add)
+    ts(R("exn", 0, 512), R("iA", 0, 512), P32, A.is_equal, -4096.0, A.mult)
+    ts(R("dodd", *C), R("iC", *C), P0, A.is_equal, R("pF", 6, 7), A.mult)
+    ts(R("blk", *C), R("iA", *C), PG, A.is_equal)
+    ts(R("blkb", *C), R("iA", *C), PG, A.is_equal)
+    ts(R("indM", 0, 8), R("iA", 0, 128, 16), PG, A.is_equal, -float(FAR), A.mult)
 
-    ts(R("kc", *C), R("cN", *C), 3, A.bitwise_and)
-    act(R("T4n", *C), R("kc", *C), scale=-4096.0, bias=float(MID - 2044))
-    cp(R("lst", *C), R("cN", *C))
-    for b, k in enumerate(blocks):
-        ts(R("dI", *k), R("rec0", *k), 2047, A.bitwise_and)
-        act(R("dM", *k), R("dI", *k), scale=4097.0)
-        if b:
-            ts(R("etab", *blocks[b - 1]), R("dM", *blocks[b - 1]), 14332, A.bitwise_and)
-    mm(R("pT", *C), R("T4n", *C), R("eyeh", *C), True, True)
-    ts(R("etab", *blocks[3]), R("dM", *blocks[3]), 14332, A.bitwise_and)
+    def lists():
+        act(R("lst", *C), R("cN", *C))
+
+    def keys():
+        act(R("K", *C), R("kc", *C), bias=2044.0)
+        mm(R("pT", *C), R("K", *C), R("eye", *C), True, True)
+        act(R("KT", *C), R("pT", *C))
 
     def bounds():
-        act(R("T4T", *C), R("pT", *C))
-        for b in BANKS:
-            mm(R("y%d" % b, 0, 512), R("T4T", *C), R("expd", 512 * b, 512 * b + 512), True, False)
+        for b in range(4):
+            rows = (32 * b, 32 * b + 32)
+            mm(R("y%d" % b, 0, 512), R("KT", 0, 128, 1, rows), R("exn", 0, 512, 1, rows), True, False)
 
-    def own():
-        act(R("pT", 384, 512), R("m4", *C), scale=-1.0, bias=2044.0)
-        act(R("pT", 128, 256), R("kc", *C), bias=2044.0)
-        act(R("pT", 256, 384), R("kc", *C), scale=4096.0, bias=2044.0)
+    def later():
+        act(R("pW", 256, 384), R("kc", *C), scale=4095.0)
+        act(R("cq", *C), I(R("cN", *C), R("pq", 0, 8)))
 
-    ts(R("m4", *C), R("cN", *C), 2044, A.bitwise_and)
+    ts(R("kc", *C), R("cN", *C), 3, A.bitwise_and)
+    lists()
+    keys()
     bounds()
-    own()
+    ts(R("diag", *C), R("iD", *C), P16, A.is_equal, -BIG / 4096, A.mult)
+    ts(R("ci", 0, 8), R("iE", 0, 8), 0.0625, A.mult, P16, A.add)
+    ts(R("pq", 0, 8), R("iE", 8, 16), R("pF", 7, 8), A.add)
+    ts(R("base", 0, 8), R("ci", 0, 8), 16.0, A.mult)
+    ts(R("exq", 0, 512), R("iB", 0, 512), P32, A.is_equal)
+    for b, k in enumerate(blocks):
+        ts(R("dI", *k), R("rec0", *k), 2047, A.bitwise_and)
+        act(R("xi", *k), R("rec0", *k), scale=2.0 ** -11, bias=-1023.5 / 2048)
+        act(R("dM", *k), R("dI", *k), scale=4097.0)
+        recast(R("xtab", *k), R("xi", *k))
+        if b:
+            ts(R("etab", *blocks[b - 1]), R("dM", *blocks[b - 1]), 14332, A.bitwise_and)
+    ts(R("etab", *blocks[3]), R("dM", *blocks[3]), 14332, A.bitwise_and)
+    later()
+
+    def rest():
+        ts(R("rowh", 0, 256, 1, ONE), R("row", 0, 256, 1, ONE), -2048.0, A.add)
+        mm(R("pM", 0, 256), R("ones", 0, 128, 1, ONE), R("rowh", 0, 256, 1, ONE), True, True)
+        tt(R("dk", *C), R("eye", *C), R("pM", *C), A.mult)
+        ts(R("lim", *C), R("pM", 128, 256), 2048.0, A.add)
+        ts(R("w128", *C), R("w", *C), 128.0, A.mult)
+        cp(R("pW", *C), R("w", *C))
+        ts(R("pW", 128, 256), R("y", *C), -128.0, A.add)
 
     sent = [0]
 
@@ -244,159 +284,129 @@ def rank_program(g, core, T, topo):
         event(sem, T.sem[sem], n, [R(land, 0, width)])
 
     E, X = R("etab", 0, 2048), R("xtab", 0, 2048)
-    EW, XW, YW = R("etab", 0, 4096), R("xtab", 0, 4096), R("yxb", 0, 4096)
-    pend = []
+    EW, XW = R("etab", 0, WIN), R("xtab", 0, WIN)
     for t in range(STEPS):
         last = t == STEPS - 1
-        cl, la, vb, lv = "cl%d" % t, "la%d" % t, "vb%d" % t, "lv%d" % t
-        for lo, hi in D_V:
-            ts(R("dg", 16 * lo, 16 * hi), I(E, R("lst", lo, hi)), -float(MID), A.add)
-        for lo, hi in D_S:
-            act(R("dg", 16 * lo, 16 * hi), I(E, R("lst", lo, hi)), bias=-float(MID))
-        for f in pend:
-            f()
-        pend = []
-        if t == 0:
-            fill(R("rmin", 0, 512), 0.0)
-            fill(R("rmin", 0, 512, 16), 32768.0)
-        for b in BANKS:
-            k = (512 * b, 512 * b + 512)
-            parts = sorted(r for r in D_V + D_S if 32 * b <= r[0] < 32 * b + 32)
-            for n, (lo, hi) in enumerate(parts):
-                mm(R("y%d" % b, 16 * lo - k[0], 16 * hi - k[0]), R("eyeh", *C), R("dg", 16 * lo, 16 * hi), False, n == len(parts) - 1)
-            act(R("ya", *k), R("y%d" % b, 0, 512), AF.Abs)
-        if t == 0:
-            for b in range(4):
-                if b in X_SHIFT:
-                    ts(R("xtab", *blocks[b]), R("rec0", *blocks[b]), 11, A.arith_shift_right)
+        cf, la, vb, lv, pl, lp = [a + str(t) for a in ("cf", "la", "vb", "lv", "pl", "lp")]
+        done = [0] * 4
+
+        def sums(o):
+            mm(o, R("n4096", *C), R("diag", *C), True, False)
+            mm(o, R("blk", *C), R("w128", *C), False, False)
+
+        for word in READ:
+            name, lo, hi = (word.split() + [0, 0])[:3]
+            lo, hi = int(lo), int(hi)
+            k = (16 * lo, 16 * hi)
+            if name[1:] == "D":
+                if name[0] == "v":
+                    ts(R("dg", *k), I(E, R("lst", lo, hi)), -float(MID), A.add)
                 else:
-                    act(R("xtab", *blocks[b]), R("rec0", *blocks[b]), scale=2.0 ** -11, bias=-1023.5 / 2048)
-            fill(R("rmax", 0, 512), 1.0)
-            fill(R("rmax", 0, 512, 16), 0.0)
-        for n, b in enumerate(BANKS):
-            k = (512 * b, 512 * b + 512)
-            scan(R("sc", *k), R("rmin", 0, 512), R("ya", *k), A.max, A.min)
-            if n & 1:
-                h = n // 2
-                c = (64 * h, 64 * h + 64)
-                tt(R("t4", *c), R("sc", 1024 * h + 15, 1024 * h + 1024, 16), R("pT", 384 + c[0], 384 + c[1]), A.min)
-                tt(R(cl, *c), R("pT", 128 + c[0], 128 + c[1]), R("t4", *c), A.subtract)
-        for lo in range(0, 128, 16):
-            k, l = (16 * lo, 16 * lo + 256), R(cl, lo, lo + 16)
-            if lo in X_V:
-                ts(R("xh", *k), I(X, l), 0.5, A.mult, -0.125, A.add)
-            else:
-                act(R("xh", *k), I(X, l), bias=-0.125, scale=0.5)
-        tt(R(cl, 128, 256), R("pT", 256, 384), R("t4", *C), A.subtract)
-        send(t, cl, la, "ac%d" % t)
-        if t == 0:
-            ts(R("dgj", *C), R("dgi", *C), 15, A.bitwise_and)
-            ts(R("diag", *C), R("dgj", *C), 0.0, A.is_equal, BIG, A.mult)
-            cp(R("pV", 128, 256), R("w", *C))
-            cp(R("pV", 256, 384), R("y", *C))
-        for h in range(2):
-            c = (64 * h, 64 * h + 64)
-            mm(R("pU", *c), R("eyeb", *C), R("diag", *c), True, False)
-            for b in (2 * h, 2 * h + 1):
-                k = (512 * b, 512 * b + 512)
-                scan(R("mx", *k), R("rmax", 0, 512), R("xh", *k), A.mult, A.max)
-                scan(R("mn", *k), R("rmin", 0, 512), R("xh", *k), A.max, A.min)
-            tt(R("zi", *c), R("mx", 1024 * h + 15, 1024 * h + 1024, 16), R("mn", 1024 * h + 15, 1024 * h + 1024, 16), A.add)
-            tt(R("wz", *c), R("zi", *c), R("pV", 128 + c[0], 128 + c[1]), A.mult)
-            mm(R("pU", *c), R("blkf", *C), R("wz", *c), False, True)
-            tt(R("dv", *c), R("zi", *c), R("pV", 256 + c[0], 256 + c[1]), A.subtract)
+                    act(R("dg", *k), I(E, R("lst", lo, hi)), bias=-float(MID))
+                b = lo // 32
+                done[b] += hi - lo
+                mm(R("y%d" % b, k[0] - 512 * b, k[1] - 512 * b), R("eye", *C), R("dg", *k), False, done[b] == 32)
+            elif name == "arrived":
+                if t:
+                    cp(I(XW, R("of", 0, 8)), R("lv%d" % (t - 1), *C))
+                else:
+                    rest()
+            elif name == "abs":
+                act(R("ya", *blocks[lo]), R("y%d" % lo, 0, 512), AF.Abs, bias=float(MID + 4095 * 2044))
+            elif name == "need":
+                c = (32 * lo, 32 * lo + 32)
+                scan(R("sc", *blocks[lo]), R("rmin", 0, 512), R("ya", *blocks[lo]), A.max, A.min)
+                tt(R("a32", *c), R("K", *c), R("sc", 512 * lo + 15, 512 * lo + 512, 16), A.subtract)
+                tt(R("cl", *c), R("a32", *c), R("lst", *c), A.max)
+            elif name == "codes":
+                tt(R(cf, *C), I(R("a32", *C), R("pq", 0, 8)), R("cq", *C), A.max)
+                tt(R(cf, 128, 256), R("cl", *C), R("pW", 256, 384), A.add)
+                send(t, cf, la, "ac%d" % t)
+                sums(R("pU", *C))
+                sums(R("pM", *C))
+            elif name[1:] == "X":
+                if name[0] == "v":
+                    ts(R("xh", *k), I(X, R("cl", lo, hi)), 0.5, A.mult, -64.125, A.add)
+                else:
+                    act(R("xh", *k), I(X, R("cl", lo, hi)), bias=-64.125, scale=0.5)
+            elif name == "ends":
+                scan(R("mx", *k), R("rmax", 0, k[1] - k[0]), R("xh", *k), A.min, A.max)
+                scan(R("mn", *k), R("rmin", 0, k[1] - k[0]), R("xh", *k), A.max, A.min)
+            elif name == "z":
+                tt(R("zi", lo, hi), R("mx", k[0] + 15, k[1], 16), R("mn", k[0] + 15, k[1], 16), A.add)
+                tt(R("wz", lo, hi), R("zi", lo, hi), R("pW", lo, hi), A.mult)
+                mm(R("pU", lo, hi), R("blk", *C), R("wz", lo, hi), False, hi == 128)
+                tt(R("dv", lo, hi), R("zi", lo, hi), R("pW", 128 + lo, 128 + hi), A.subtract)
+        mm(R("pM", *C), R("blk", *C), R("wz", *C), False, False)
         act(R(vb, *C), R("dv", *C), AF.Abs)
-        if t == 0:
-            fill(R("rz", *C), 1.0)
-            fill(R("rz", 0, 128, 16), 0.0)
-            ts(R("bsj", 0, 8), R("bsi", 0, 8), 255, A.bitwise_and)
-            tt(R("base", 0, 8), R("bsj", 0, 8), R("bsk", 0, 8), A.add)
-            ts(R("odj", 0, 8), R("odi", 0, 8), 15, A.bitwise_and)
-            ts(R("odd", 0, 8), R("odj", 0, 8), 2.0, A.mult, 1.0, A.add)
-            cp(R("kcol", 0, 1), R("mI", 0, 1))
-            cp(R("thf", 0, 1), R("thI", 0, 1))
-        act(R("oz", *C), R("zi", *C), scale=R("odd", 0, 1))
-        scan(R("du", *C), R("rz", *C), R("pU", *C), A.mult, A.max)
-        ts(R("a15", 0, 8), R("du", 15, 128, 16), 15, A.bitwise_and)
-        tt(R("pl", 0, 8), R("a15", 0, 8), R("base", 0, 8), A.add)
-        cp(R(vb, 128, 136), R("a15", 0, 8))
         send(t, vb, lv, "av%d" % t)
-        cp(I(XW, R("pl", 0, 8)), R(vb, *C))
-        act(R("uI", *C), R("pU", *C))
-        if t == 0:
-            act(R("neyeb", *C), R("eyeb", *C), scale=-1.0)
-            for k in range(8):
-                act(R("sel", 16 * k, 16 * k + 129 * 15 + 1, 129), R("blkb", 16 * k, 16 * k + 16))
-        lo = 0
-        while lo < 128:
-            hi = lo + 16
-            while lo not in A_V and hi < 128 and hi not in A_V and hi - lo < 64:
-                hi += 16
-            if lo not in A_V:
-                act(R("xa", 16 * lo, 16 * hi), I(X, R(la, lo, hi)))
-            lo = hi
-        for lo in A_V:
-            cp(R("xa", 16 * lo, 16 * lo + 256), I(X, R(la, lo, lo + 16)))
-        for n, j in enumerate(PE_J):
-            mm(R("y%d" % n, *C), R("eyeb", *C), R("xa", j, 2048, 16), True, False)
-        ts(R("um", *C), R("uI", *C), 4095, A.bitwise_and)
-        tt(R("sq", *C), R("um", *C), R("um", *C), A.mult)
-        ts(R("q5", *C), R("sq", *C), -12.0, A.add, 2.0 ** -5, A.mult)
-        ts(R("pV", 384, 512), R("um", *C), R("kcol", 0, 1), A.mult)
-        tt(R("pV", 384, 512), R("oz", *C), R("pV", 384, 512), A.add)
-        tt(R("r2", *C), R("q5", *C), R("pV", 384, 512), A.add)
-        ts(R("cN", *C), R("r2", *C), 2047, A.bitwise_and)
-        if last:
-            for b in blocks:
-                cp(R("yxb", *b), R("xtab", *b))
-            cp(R("ycb", *C), R("cN", *C))
-            cp(R("yzb", *C), R("zi", *C))
-            for k, (o, b) in enumerate(((T.yc, "ycb"), (T.yz, "yzb"))):
-                need("y", [R(b, *C)], [])
-                g.sync.dma_start(o[:], T[b][:]).then_inc(T.sem["out%d" % k], 16)
-        else:
-            ts(R("kc", *C), R("cN", *C), 3, A.bitwise_and)
-            act(R("T4n", *C), R("kc", *C), scale=-4096.0, bias=float(MID - 2044))
-            mm(R("pT", *C), R("T4n", *C), R("eyeh", *C), True, True)
-            act(R("T4T", *C), R("pT", *C))
-            cp(R("lst", *C), R("cN", *C))
-            ts(R("m4", *C), R("cN", *C), 2044, A.bitwise_and)
-            cp(I(EW, R("pl", 0, 8)), R(cl, 128, 256))
-        tt(R("pb", 0, 8), R(lv, 128, 136), R("base", 0, 8), A.add)
-        mm(R("pV", *C), R("eyeb", *C), R(lv, *C), True, True)
-        for n, j in enumerate(PE_J):
-            mm(R("y%d" % n, *C), R("neyeb", *C), R(lv, *C), False, True)
-        vj = [j for j in range(16) if j not in PE_J]
-        for n, j in enumerate(vj):
-            tt(R("dd", 128 * n, 128 * n + 128), R("xa", j, 2048, 16), R("pV", *C), A.subtract)
-        todo = [(("y%d" % n, 0, 128, 1), [j]) for n, j in enumerate(PE_J)]
-        n = 0
-        for m in ABS_V:
-            todo.append((R("dd", 128 * n, 128 * (n + m)), vj[n:n + m]))
-            n += m
-        n = 0
-        for src, js in todo:
-            act(R("ad", 128 * n, 128 * (n + len(js))), src, AF.Abs)
-            for j in js:
-                mm(R("pD", *C), R("sel", 128 * j, 128 * j + 128), R("ad", 128 * n, 128 * n + 128), n == 0, n == 15)
-                n += 1
-        mm(R("pU", 128, 256), R("eyeb", *C), R("diag", *C), True, False)
-        ts(R("bb", *C), R("pD", *C), R("thf", 0, 1), A.is_lt)
-        mm(R("pU", 128, 256), R("blkb", *C), R("bb", *C), False, True)
+        scan(R("du", *C), R("rz", *C), R("pU", *C), A.mult, A.max)
+        act(R("zf", *C), R("zi", *C), bias=128.0)
+        ts(R("a15", 0, 8), R("du", 15, 128, 16), 15, A.bitwise_and)
+        act(R("qf", *C), R("pU", *C), scale=2.0 ** -12, bias=1025.0 - 2047.5 / 4096)
+        tt(R(pl, 0, 8), R("a15", 0, 8), R("base", 0, 8), A.add)
+        send(t, pl, lp, "ap%d" % t)
+        cp(I(X, R(pl, 0, 8)), R(vb, *C))
+        mm(R("pM", *C), R("n4096", *C), R("qf", *C), False, True)
+        act(R("umh", *C), R("pM", *C), bias=4096.0 * 1025 - 2048)
+        mm(R("pM", 128, 256), R("dodd", *C), R("zf", *C), True, False)
+        mm(R("pM", 128, 256), R("dk", *C), R("umh", *C), False, True)
+        act(R("sq", *C), R("umh", *C), AF.Square, bias=2048.0)
+        act(R("q5", *C), R("sq", *C), scale=2.0 ** -5, bias=-0.375)
+        mm(R("pU", 128, 136), R("eye", *C), R("ci", 0, 8), True, False)
+        mm(R("pU", 128, 136), R("ones", *C), R("c186", 0, 8), False, False)
+        for word in JUDGE:
+            name, lo, hi = (word.split() + [0, 0])[:3]
+            lo, hi = int(lo), int(hi)
+            k = (16 * lo, 16 * hi)
+            if name == "vA":
+                cp(R("xa", *k), I(X, R(la, lo, hi)))
+            elif name == "sA":
+                act(R("xa", *k), I(X, R(la, lo, hi)))
+            elif name == "turn":
+                for c in range(4):
+                    mm(R("pT", 0, 128, 1, (32 * c, 32 * c + 32)), R(lv, c, 128, 4), R("eyeb", *C), True, True)
+                act(R("vT", *C), R("pT", *C), scale=-1.0)
+            elif name == "sub":
+                rows = (32 * lo, 32 * lo + 32)
+                mm(R("y%d" % lo, 0, 512), R("vT", 0, 128, 1, rows), R("exq", 0, 512, 1, rows), True, False)
+                mm(R("y%d" % lo, 0, 512), R("eyeb", *C), R("xa", *blocks[lo]), False, True)
+            elif name == "size":
+                act(R("ad", *blocks[lo]), R("y%d" % lo, 0, 512), AF.Abs)
+            elif name == "sum":
+                for j in range(4):
+                    a = 512 * lo + 128 * j
+                    mm(R("pT", 128 + 4 * j + lo, 256, 16), R("ad", a, a + 128), R("blkb", 0, 128, 16), True, True)
+            elif name == "names":
+                if not last:
+                    cp(I(E, R(pl, 0, 8)), R(cf, 128, 256))
+            elif name == "next":
+                tt(R("r2", *C), R("q5", *C), R("pM", 128, 256), A.add)
+                ts(R("cN", *C), R("r2", *C), 2047, A.bitwise_and)
+                if last:
+                    cp(R("ycb", *C), R("cN", *C))
+                    for n, (o, b) in enumerate(((T.yz, "zf"), (T.yc, "ycb"))):
+                        need("y", [R(b, *C)], [])
+                        g.sync.dma_start(o[:], T[b][:]).then_inc(T.sem["out%d" % n], 16)
+                else:
+                    ts(R("kc", *C), R("r2", *C), 3, A.bitwise_and)
         if not last:
-            for b in BANKS:
-                mm(R("y%d" % b, 0, 512), R("T4T", *C), R("expd", 512 * b, 512 * b + 512), True, False)
-            own()
-        scan(R("st", *C), R("rz", *C), R("pU", 128, 256), A.mult, A.max)
-        ts(R("nb", 0, 8), R("st", 15, 128, 16), BIG + QUO, A.is_lt, 2048.0, A.mult)
-        tt(R("of", 0, 8), R("nb", 0, 8), R("pb", 0, 8), A.add)
+            act(R("K", *C), R("kc", *C), bias=2044.0)
+            lists()
+        tt(R("bb", *C), R("pT", 128, 256), R("lim", *C), A.is_lt)
+        mm(R("pU", 128, 136), R("bb", *C), R("indM", 0, 8), False, True)
+        if not last:
+            mm(R("pT", *C), R("K", *C), R("eye", *C), True, True)
+        tt(R("of", 0, 8), R("pU", 128, 136), R(lp, 0, 8), A.max)
         if last:
-            cp(I(YW, R("of", 0, 8)), R(lv, *C))
+            cp(I(XW, R("of", 0, 8)), R(lv, *C))
         else:
+            act(R("KT", *C), R("pT", *C))
             cp(I(EW, R("of", 0, 8)), R(la, 128, 256))
-            pend.append((lambda l: lambda: cp(I(XW, R("of", 0, 8)), R(l, *C)))(lv))
-    need("y", [R("yxb", 0, 2048)], [])
-    g.sync.dma_start(T.yx[:], T.yxb[:, 0:2048]).then_inc(T.sem.out2, 16)
+            bounds()
+            later()
+    need("y", [X], [])
+    g.sync.dma_start(T.yx[:], T.xtab[:, 0:2048]).then_inc(T.sem.out2, 16)
     g.wait_ge(T.sem.loc, sent[0])
     for k in range(3):
         g.sync.wait_ge(T.sem["out%d" % k], 16)

@@ -2,9 +2,8 @@ from concourse.mybir import AluOpType, ActivationFunctionType as AF
 
 STEPS = 3
 MID = 7168
-BIG = 131072.0
-FAR = 2176
-WIN = 2048 + 128 + 10 * FAR + 16
+EDGE = 61440.0
+WIN = 11 * 2048 + 128
 
 
 def _sb(w, d):
@@ -22,38 +21,42 @@ SCRATCH = {
     "pI": _sb(8, "int32"), "pF": _sb(8, "float32"), "iA": _sb(512, "bfloat16"), "iB": _sb(512, "bfloat16"), "iC": _sb(128, "bfloat16"),
     "iD": _sb(128, "bfloat16"), "iE": _sb(16, "float32"), "exn": _sb(512, "float16"), "exq": _sb(512, "bfloat16"),
     "eye": _sb(128, "float16"), "eyeb": _sb(128, "bfloat16"), "n4096": _sb(128, "float16"), "blk": _sb(128, "float16"), "blkb": _sb(128, "bfloat16"),
-    "diag": _sb(128, "float16"), "ones": _sb(128, "float16"), "indM": _sb(8, "bfloat16"), "c186": _sb(8, "float16"),
-    "ci": _sb(8, "float16"), "base": _sb(8, "float32"), "pq": _sb(8, "uint16"), "w128": _sb(128, "float16"), "dk": _sb(128, "float16"),
-    "dodd": _sb(128, "bfloat16"), "lim": _sb(128, "float32"), "rmin": _sb(512, "float16"), "rmax": _sb(512, "float16"), "rz": _sb(128, "float32"),
+    "blk128": _sb(128, "bfloat16"), "offd": _sb(128, "float16"), "ones": _sb(128, "float16"), "m128": _sb(128, "bfloat16"),
+    "indM": _sb(8, "bfloat16"), "spare": _sb(8, "float16"), "ci": _sb(8, "float16"), "base": _sb(8, "float32"), "pq": _sb(8, "uint16"),
+    "dk": _sb(128, "float16"), "dodd": _sb(128, "bfloat16"), "lim": _sb(128, "float32"),
+    "rmin": _sb(512, "float16"), "rmax": _sb(512, "float16"),
     "cN": _sb(128, "int32"), "kc": _sb(128, "int32"), "lst": _sb(128, "uint16"), "cq": _sb(128, "float16"), "K": _sb(128, "float16"),
     "KT": _sb(128, "float16"), "a32": _sb(128, "int32"), "cl": _sb(128, "uint16"),
     "dg": _sb(2048, "float16"), "ya": _sb(2048, "float16"), "sc": _sb(2048, "float16"), "xh": _sb(2048, "float16"),
     "mx": _sb(2048, "float16"), "mn": _sb(2048, "float16"), "xa": _sb(2048, "bfloat16"), "ad": _sb(2048, "bfloat16"),
     "zi": _sb(128, "int32"), "wz": _sb(128, "float16"), "dv": _sb(128, "bfloat16"), "du": _sb(128, "int32"), "a15": _sb(8, "int32"),
     "zf": _sb(128, "bfloat16"), "qf": _sb(128, "float16"), "umh": _sb(128, "float16"), "sq": _sb(128, "float32"), "q5": _sb(128, "int32"),
-    "r2": _sb(128, "int32"), "vT": _sb(128, "bfloat16"), "bb": _sb(128, "bfloat16"), "of": _sb(8, "uint16"), "ycb": _sb(128, "float32"),
+    "r2": _sb(128, "int32"), "bb": _sb(128, "bfloat16"), "of": _sb(8, "uint16"), "ycb": _sb(128, "float32"),
     "y0": _ps(512), "y1": _ps(512), "y2": _ps(512), "y3": _ps(512),
     "pW": _ps(384),
     "pU": _ps(136),
-    "pM": _ps(256),
+    "pM": _ps(384),
     "pT": _ps(256),
 }
 for _t in range(STEPS):
-    SCRATCH["cf%d" % _t] = _sb(256, "uint16")
-    SCRATCH["la%d" % _t] = _sb(256, "uint16")
-    SCRATCH["vb%d" % _t] = _sb(128, "bfloat16")
-    SCRATCH["lv%d" % _t] = _sb(128, "bfloat16")
-    SCRATCH["pl%d" % _t] = _sb(8, "uint16")
-    SCRATCH["lp%d" % _t] = _sb(8, "uint16")
+    SCRATCH["cf%d" % _t] = _sb(128, "uint16")
+    SCRATCH["la%d" % _t] = _sb(128, "uint16")
+    SCRATCH["vt%d" % _t] = _sb(128, "bfloat16")
+    SCRATCH["lt%d" % _t] = _sb(128, "bfloat16")
+    SCRATCH["vp%d" % _t] = _sb(136 if _t == STEPS - 1 else 264, "uint16")
+    SCRATCH["lv%d" % _t] = SCRATCH["vp%d" % _t]
 PSUM = [k for k in SCRATCH if SCRATCH[k][0] == "psum"]
-SEMAPHORES = ["qv", "qs", "qp", "qg", "loc"] + ["ld%d" % k for k in range(9)] + ["out%d" % k for k in range(3)] + \
+SEMAPHORES = ["qv", "qs", "qp", "qg", "loc"] + ["ld%d" % k for k in range(12)] + ["out%d" % k for k in range(4)] + \
     [a + str(k) for a in ("ac", "av", "ap") for k in range(STEPS)]
 
-READ = ("vD 0 32", "sD 64 96", "vD 32 64", "sD 96 128", "arrived", "abs 0", "abs 1", "need 0", "abs 2", "need 1", "abs 3", "need 2",
-        "sX 0 32", "need 3", "sX 32 64", "codes", "ends 0 32", "sX 64 96", "ends 32 64", "z 0 64", "sX 96 112", "ends 64 96",
-        "sX 112 128", "ends 96 112", "ends 112 128", "z 64 128")
-JUDGE = ("vA 0 32", "sA 96 128", "turn", "vA 32 64", "sub 0", "sub 3", "size 0", "vA 64 96", "sub 1", "size 3", "sum 0", "size 1", "sub 2",
-         "sum 3", "names", "next", "size 2", "sum 1", "sum 2")
+LOADS = (0, 512, 1024, 1536, 2048)
+UNPACK = (0, 512, 1024, 1536, 1792, 2048)
+READ = ("vD 0 32", "sD 32 64", "vD 64 112", "sD 112 128", "abs 0", "abs 1", "near 0 32", "arrived", "abs 2", "need 0 32", "near 32 64",
+        "abs 3", "raise 0 32", "near 64 96", "sX 0 32", "need 32 96", "near 96 128", "raise 32 96", "sX 32 64", "need 96 128", "max 0 32",
+        "raise 96 128", "min 0 32", "sX 64 96", "codes", "max 32 64", "min 32 64", "sX 96 112", "max 64 96", "min 64 96", "sX 112 128",
+        "max 96 112", "min 96 112", "max 112 128", "min 112 128")
+JUDGE = ("vA 0 16", "sA 16 32", "x 0", "vA 32 64", "sA 96 128", "v 0", "v 1", "x 1", "size 0", "vA 64 96", "v 3", "x 3", "v 2", "size 1",
+         "floor", "x 2", "size 3", "sum 0", "next", "sum 1", "names", "size 2", "sum 3", "sum 2", "keys")
 
 
 def R(name, lo, hi, st=1, p=None):
@@ -183,52 +186,58 @@ def rank_program(g, core, T, topo):
         nload[0] += 1
     C = (0, 128)
     ONE = (0, 1)
-    blocks = [(512 * b, 512 * b + 512) for b in range(4)]
+    banks = [(512 * b, 512 * b + 512) for b in range(4)]
     load("s", R("cN", *C), T.req[:])
-    for b, k in enumerate(blocks):
+    for k in zip(LOADS, LOADS[1:]):
         load("y", R("rec0", *k), T.rec[:, k[0]:k[1]])
-    load("y", R("row", 0, 128, 1, ONE), T.mul[:])
-    load("y", R("row", 128, 256, 1, ONE), T.th[:])
+    load("s", R("row", 0, 128, 1, ONE), T.mul[:])
+    load("s", R("row", 128, 256, 1, ONE), T.th[:])
     load("y", R("w", *C), T.wt[:])
     load("y", R("y", *C), T.aim[:])
 
-    P0, P16, P32, PG, PA, PB = [R("pF", k, k + 1) for k in range(6)]
-    iota(R("pI", 0, 1), [[0, 1]], 1)
+    PG, P32, P16, P8, P0, ODD, PQ = [R("pF", k, k + 1) for k in range(7)]
+    for k, m in enumerate((1, 16, 32, 64)):
+        iota(R("pI", k, k + 1), [[0, 1]], m)
+    iota(P0, [[0, 1]], 1)
     iota(R("iC", *C), [[1, 128]])
-    iota(R("iA", 0, 512), [[1, 32], [0, 16]])
-    iota(R("iD", *C), [[0, 8], [1, 16]])
-    iota(R("iE", 0, 8), [[256, 8]])
-    iota(R("iE", 8, 16), [[1, 4], [8, 2]])
-    iota(R("iB", 0, 512), [[1, 4], [4, 8], [0, 16]])
-    fill(R("rmin", 0, 512), -32768.0)
-    fill(R("rmax", 0, 512), 32768.0)
-    fill(R("rz", *C), 1.0)
+    iota(R("iA", 0, 512), [[16, 32], [0, 16]])
+    iota(R("iE", 0, 8), [[512, 8]])
+    iota(R("iE", 8, 16), [[64, 4], [512, 2]])
+    iota(R("iD", *C), [[0, 8], [32, 16]])
+    fill(R("rmin", 0, 512), -EDGE)
     fill(R("ones", *C), 1.0)
-    fill(R("c186", 0, 8), (2048 + 10 * FAR) / 128)
-    fill(R("rmin", 0, 512, 16), 32768.0)
-    fill(R("rmax", 0, 512, 16), -32768.0)
-    fill(R("rz", 0, 128, 16), 0.0)
-    for k, m in ((1, 15), (2, 31), (4, 7)):
-        ts(R("pI", k, k + 1), R("pI", 0, 1), m, A.bitwise_and)
-    ts(R("pI", 3, 4), R("pI", 0, 1), 4, A.arith_shift_right)
-    ts(R("pI", 5, 6), R("pI", 0, 1), 1, A.arith_shift_right, 4, A.bitwise_and)
-    cp(R("pF", 0, 6), R("pI", 0, 6))
+    fill(R("rmin", 0, 512, 16), EDGE)
+    fill(R("m128", *C), -128.0)
+    ts(R("pI", 4, 8), R("pI", 0, 4), 496, A.bitwise_and)
+    fill(R("spare", 0, 8), 11 * 2048 / 128)
+    act(R("rmax", 0, 512), R("rmin", 0, 512), scale=-1.0)
+    cp(R("pF", 0, 4), R("pI", 4, 8))
     ts(R("eye", *C), R("iC", *C), P0, A.is_equal)
-    ts(R("eyeb", *C), R("iC", *C), P0, A.is_equal)
-    ts(R("n4096", *C), R("iC", *C), P0, A.is_equal, -4096.0, A.mult)
-    ts(R("pF", 6, 7), P16, 2.0, A.mult, 1.0, A.add)
-    ts(R("pF", 7, 8), PA, 16.0, A.mult, PB, A.add)
+    ts(ODD, P16, 0.0625, A.mult, 1.0, A.add)
+    ts(PQ, P8, 15.5, A.mult, P16, A.add)
+    act(R("eyeb", *C), R("eye", *C))
+    act(R("n4096", *C), R("eye", *C), scale=-4096.0)
+    ts(R("dodd", *C), R("iC", *C), P0, A.is_equal, ODD, A.mult)
+    ts(R("kc", *C), R("cN", *C), 3, A.bitwise_and)
     ts(R("exn", 0, 512), R("iA", 0, 512), P32, A.is_equal, -4096.0, A.mult)
-    ts(R("dodd", *C), R("iC", *C), P0, A.is_equal, R("pF", 6, 7), A.mult)
     ts(R("blk", *C), R("iA", *C), PG, A.is_equal)
-    ts(R("blkb", *C), R("iA", *C), PG, A.is_equal)
-    ts(R("indM", 0, 8), R("iA", 0, 128, 16), PG, A.is_equal, -float(FAR), A.mult)
+    ts(R("ci", 0, 8), R("iE", 0, 8), P16, A.add, 1 / 32, A.mult)
+    ts(R("base", 0, 8), R("iE", 0, 8), P16, A.add, 0.5, A.mult)
+    ts(R("pq", 0, 8), R("iE", 8, 16), PQ, A.add, 1 / 64, A.mult)
+    ts(R("offd", *C), R("iD", *C), P16, A.not_equal, 32.0, A.mult)
 
-    def lists():
-        act(R("lst", *C), R("cN", *C))
+    def rest():
+        ts(R("rowh", 0, 256, 1, ONE), R("row", 0, 256, 1, ONE), -2048.0, A.add)
+        mm(R("pM", 0, 256), R("ones", 0, 128, 1, ONE), R("rowh", 0, 256, 1, ONE), True, True)
+        ts(R("exq", 0, 512), R("iB", 0, 512), P32, A.is_equal, -1.0, A.mult)
+        tt(R("dk", *C), R("eye", *C), R("pM", *C), A.mult)
+        ts(R("lim", *C), R("pM", 128, 256), 2048.0, A.add)
 
     def keys():
+        recast(R("lst", *C), R("cN", *C))
         act(R("K", *C), R("kc", *C), bias=2044.0)
+
+    def turn():
         mm(R("pT", *C), R("K", *C), R("eye", *C), True, True)
         act(R("KT", *C), R("pT", *C))
 
@@ -236,38 +245,29 @@ def rank_program(g, core, T, topo):
         for b in range(4):
             rows = (32 * b, 32 * b + 32)
             mm(R("y%d" % b, 0, 512), R("KT", 0, 128, 1, rows), R("exn", 0, 512, 1, rows), True, False)
-
-    def later():
         act(R("pW", 256, 384), R("kc", *C), scale=4095.0)
         act(R("cq", *C), I(R("cN", *C), R("pq", 0, 8)))
 
-    ts(R("kc", *C), R("cN", *C), 3, A.bitwise_and)
-    lists()
     keys()
+    iota(R("iB", 0, 512), [[16, 4], [64, 8], [0, 16]])
+    act(R("blkb", *C), R("blk", *C))
+    turn()
+    act(R("blk128", *C), R("blk", *C), scale=128.0)
+    act(R("indM", 0, 8), R("blk", 0, 128, 16), scale=-2048.0)
     bounds()
-    ts(R("diag", *C), R("iD", *C), P16, A.is_equal, -BIG / 4096, A.mult)
-    ts(R("ci", 0, 8), R("iE", 0, 8), 0.0625, A.mult, P16, A.add)
-    ts(R("pq", 0, 8), R("iE", 8, 16), R("pF", 7, 8), A.add)
-    ts(R("base", 0, 8), R("ci", 0, 8), 16.0, A.mult)
-    ts(R("exq", 0, 512), R("iB", 0, 512), P32, A.is_equal)
-    for b, k in enumerate(blocks):
-        ts(R("dI", *k), R("rec0", *k), 2047, A.bitwise_and)
-        act(R("xi", *k), R("rec0", *k), scale=2.0 ** -11, bias=-1023.5 / 2048)
-        act(R("dM", *k), R("dI", *k), scale=4097.0)
-        recast(R("xtab", *k), R("xi", *k))
-        if b:
-            ts(R("etab", *blocks[b - 1]), R("dM", *blocks[b - 1]), 14332, A.bitwise_and)
-    ts(R("etab", *blocks[3]), R("dM", *blocks[3]), 14332, A.bitwise_and)
-    later()
-
-    def rest():
-        ts(R("rowh", 0, 256, 1, ONE), R("row", 0, 256, 1, ONE), -2048.0, A.add)
-        mm(R("pM", 0, 256), R("ones", 0, 128, 1, ONE), R("rowh", 0, 256, 1, ONE), True, True)
-        tt(R("dk", *C), R("eye", *C), R("pM", *C), A.mult)
-        ts(R("lim", *C), R("pM", 128, 256), 2048.0, A.add)
-        ts(R("w128", *C), R("w", *C), 128.0, A.mult)
-        cp(R("pW", *C), R("w", *C))
-        ts(R("pW", 128, 256), R("y", *C), -128.0, A.add)
+    pieces = list(zip(UNPACK, UNPACK[1:]))
+    for n, k in enumerate(pieces + [None]):
+        if k:
+            ts(R("dI", *k), R("rec0", *k), 2047, A.bitwise_and)
+            act(R("dM", *k), R("dI", *k), scale=4097.0)
+            if n < len(pieces) - 2:
+                act(R("xi", *k), R("rec0", *k), scale=2.0 ** -11, bias=-1023.5 / 2048)
+                recast(R("xtab", *k), R("xi", *k))
+        if n:
+            ts(R("etab", *pieces[n - 1]), R("dM", *pieces[n - 1]), 14332, A.bitwise_and)
+    k = (pieces[-2][0], pieces[-1][1])
+    act(R("xi", *k), R("rec0", *k), scale=2.0 ** -11, bias=-1023.5 / 2048)
+    recast(R("xtab", *k), R("xi", *k))
 
     sent = [0]
 
@@ -287,74 +287,76 @@ def rank_program(g, core, T, topo):
     EW, XW = R("etab", 0, WIN), R("xtab", 0, WIN)
     for t in range(STEPS):
         last = t == STEPS - 1
-        cf, la, vb, lv, pl, lp = [a + str(t) for a in ("cf", "la", "vb", "lv", "pl", "lp")]
-        done = [0] * 4
-
-        def sums(o):
-            mm(o, R("n4096", *C), R("diag", *C), True, False)
-            mm(o, R("blk", *C), R("w128", *C), False, False)
-
+        cf, la, vt, lt, vp, lv = [a + str(t) for a in ("cf", "la", "vt", "lt", "vp", "lv")]
+        PL = R(vp, 128, 136)
         for word in READ:
             name, lo, hi = (word.split() + [0, 0])[:3]
             lo, hi = int(lo), int(hi)
             k = (16 * lo, 16 * hi)
-            if name[1:] == "D":
-                if name[0] == "v":
-                    ts(R("dg", *k), I(E, R("lst", lo, hi)), -float(MID), A.add)
-                else:
-                    act(R("dg", *k), I(E, R("lst", lo, hi)), bias=-float(MID))
-                b = lo // 32
-                done[b] += hi - lo
-                mm(R("y%d" % b, k[0] - 512 * b, k[1] - 512 * b), R("eye", *C), R("dg", *k), False, done[b] == 32)
+            if name == "vD":
+                ts(R("dg", *k), I(E, R("lst", lo, hi)), -float(MID), A.add)
+            elif name == "sD":
+                act(R("dg", *k), I(E, R("lst", lo, hi)), bias=-float(MID))
             elif name == "arrived":
                 if t:
                     cp(I(XW, R("of", 0, 8)), R("lv%d" % (t - 1), *C))
                 else:
                     rest()
             elif name == "abs":
-                act(R("ya", *blocks[lo]), R("y%d" % lo, 0, 512), AF.Abs, bias=float(MID + 4095 * 2044))
+                mm(R("y%d" % lo, 0, 512), R("eye", *C), R("dg", *banks[lo]), False, True)
+                act(R("ya", *banks[lo]), R("y%d" % lo, 0, 512), AF.Abs, bias=float(MID + 4095 * 2044))
+            elif name == "near":
+                scan(R("sc", *k), R("rmin", 0, k[1] - k[0]), R("ya", *k), A.max, A.min)
             elif name == "need":
-                c = (32 * lo, 32 * lo + 32)
-                scan(R("sc", *blocks[lo]), R("rmin", 0, 512), R("ya", *blocks[lo]), A.max, A.min)
-                tt(R("a32", *c), R("K", *c), R("sc", 512 * lo + 15, 512 * lo + 512, 16), A.subtract)
-                tt(R("cl", *c), R("a32", *c), R("lst", *c), A.max)
+                tt(R("a32", lo, hi), R("K", lo, hi), R("sc", k[0] + 15, k[1], 16), A.subtract)
+            elif name == "raise":
+                tt(R("cl", lo, hi), R("a32", lo, hi), R("lst", lo, hi), A.max)
             elif name == "codes":
                 tt(R(cf, *C), I(R("a32", *C), R("pq", 0, 8)), R("cq", *C), A.max)
-                tt(R(cf, 128, 256), R("cl", *C), R("pW", 256, 384), A.add)
                 send(t, cf, la, "ac%d" % t)
-                sums(R("pU", *C))
-                sums(R("pM", *C))
-            elif name[1:] == "X":
-                if name[0] == "v":
-                    ts(R("xh", *k), I(X, R("cl", lo, hi)), 0.5, A.mult, -64.125, A.add)
-                else:
-                    act(R("xh", *k), I(X, R("cl", lo, hi)), bias=-64.125, scale=0.5)
-            elif name == "ends":
+                if t == 0:
+                    mm(R("pW", *C), R("eyeb", *C), R("w", *C), True, True)
+                    mm(R("pW", 128, 256), R("eyeb", *C), R("y", *C), True, False)
+                    mm(R("pW", 128, 256), R("eyeb", *C), R("m128", *C), False, True)
+                mm(R("pU", *C), R("n4096", *C), R("offd", *C), True, False)
+                mm(R("pM", *C), R("blk128", *C), R("w", *C), True, False)
+            elif name == "vX":
+                ts(R("xh", *k), I(X, R("cl", lo, hi)), 0.5, A.mult, -64.125, A.add)
+            elif name == "sX":
+                act(R("xh", *k), I(X, R("cl", lo, hi)), bias=-64.125, scale=0.5)
+            elif name == "max":
                 scan(R("mx", *k), R("rmax", 0, k[1] - k[0]), R("xh", *k), A.min, A.max)
+            elif name == "min":
                 scan(R("mn", *k), R("rmin", 0, k[1] - k[0]), R("xh", *k), A.max, A.min)
-            elif name == "z":
-                tt(R("zi", lo, hi), R("mx", k[0] + 15, k[1], 16), R("mn", k[0] + 15, k[1], 16), A.add)
-                tt(R("wz", lo, hi), R("zi", lo, hi), R("pW", lo, hi), A.mult)
-                mm(R("pU", lo, hi), R("blk", *C), R("wz", lo, hi), False, hi == 128)
-                tt(R("dv", lo, hi), R("zi", lo, hi), R("pW", 128 + lo, 128 + hi), A.subtract)
-        mm(R("pM", *C), R("blk", *C), R("wz", *C), False, False)
-        act(R(vb, *C), R("dv", *C), AF.Abs)
-        send(t, vb, lv, "av%d" % t)
-        scan(R("du", *C), R("rz", *C), R("pU", *C), A.mult, A.max)
-        act(R("zf", *C), R("zi", *C), bias=128.0)
+        tt(R("zi", *C), R("mx", 15, 2048, 16), R("mn", 15, 2048, 16), A.add)
+        tt(R("wz", *C), R("zi", *C), R("pW", *C), A.mult)
+        tt(R("dv", *C), R("zi", *C), R("pW", 128, 256), A.subtract)
+        mm(R("pU", *C), R("blk", *C), R("wz", *C), False, True)
+        for c in range(4):
+            mm(R("pT", 0, 128, 1, (32 * c, 32 * c + 32)), R("dv", c, 128, 4), R("eyeb", *C), True, True)
+        mm(R("pM", *C), R("blk", *C), R("wz", *C), False, True)
+        mm(R("pM", 128, 256), R("blk128", *C), R("w", *C), True, False)
+        mm(R("pM", 128, 256), R("blk", *C), R("wz", *C), False, False)
+        act(R(vp, *C), R("dv", *C), AF.Abs)
+        if not last:
+            tt(R(vp, 136, 264), R("cl", *C), R("pW", 256, 384), A.add)
+        scan(R("du", *C), R("rmax", *C), R("pU", *C), A.min, A.max)
+        act(R(vt, *C), R("pT", *C), AF.Abs)
+        send(t, vt, lt, "av%d" % t)
         ts(R("a15", 0, 8), R("du", 15, 128, 16), 15, A.bitwise_and)
-        act(R("qf", *C), R("pU", *C), scale=2.0 ** -12, bias=1025.0 - 2047.5 / 4096)
-        tt(R(pl, 0, 8), R("a15", 0, 8), R("base", 0, 8), A.add)
-        send(t, pl, lp, "ap%d" % t)
-        cp(I(X, R(pl, 0, 8)), R(vb, *C))
-        mm(R("pM", *C), R("n4096", *C), R("qf", *C), False, True)
-        act(R("umh", *C), R("pM", *C), bias=4096.0 * 1025 - 2048)
-        mm(R("pM", 128, 256), R("dodd", *C), R("zf", *C), True, False)
-        mm(R("pM", 128, 256), R("dk", *C), R("umh", *C), False, True)
-        act(R("sq", *C), R("umh", *C), AF.Square, bias=2048.0)
-        act(R("q5", *C), R("sq", *C), scale=2.0 ** -5, bias=-0.375)
+        act(R("qf", *C), R("pM", *C), scale=2.0 ** -12, bias=1025.0 - 2047.5 / 4096)
+        mm(R("pM", 128, 256), R("n4096", *C), R("qf", *C), False, True)
+        tt(PL, R("a15", 0, 8), R("base", 0, 8), A.add)
+        send(t, vp, lv, "ap%d" % t)
+        cp(I(X, PL), R(vp, *C))
+        act(R("umh", *C), R("pM", 128, 256), bias=4096.0 * 1025 - 2048)
+        act(R("sq", *C), R("pM", 128, 256), AF.Square, bias=4096.0 * 1025)
+        mm(R("pM", 256, 384), R("dodd", *C), R("dv", *C), True, False)
+        mm(R("pM", 256, 384), R("dodd", *C), R("y", *C), False, False)
+        mm(R("pM", 256, 384), R("dk", *C), R("umh", *C), False, True)
         mm(R("pU", 128, 136), R("eye", *C), R("ci", 0, 8), True, False)
-        mm(R("pU", 128, 136), R("ones", *C), R("c186", 0, 8), False, False)
+        mm(R("pU", 128, 136), R("ones", *C), R("spare", 0, 8), False, False)
+        begun = set()
         for word in JUDGE:
             name, lo, hi = (word.split() + [0, 0])[:3]
             lo, hi = int(lo), int(hi)
@@ -363,48 +365,49 @@ def rank_program(g, core, T, topo):
                 cp(R("xa", *k), I(X, R(la, lo, hi)))
             elif name == "sA":
                 act(R("xa", *k), I(X, R(la, lo, hi)))
-            elif name == "turn":
-                for c in range(4):
-                    mm(R("pT", 0, 128, 1, (32 * c, 32 * c + 32)), R(lv, c, 128, 4), R("eyeb", *C), True, True)
-                act(R("vT", *C), R("pT", *C), scale=-1.0)
-            elif name == "sub":
+            elif name == "x":
+                mm(R("y%d" % lo, 0, 512), R("eyeb", *C), R("xa", *banks[lo]), lo not in begun, lo in begun)
+                begun.add(lo)
+            elif name == "v":
                 rows = (32 * lo, 32 * lo + 32)
-                mm(R("y%d" % lo, 0, 512), R("vT", 0, 128, 1, rows), R("exq", 0, 512, 1, rows), True, False)
-                mm(R("y%d" % lo, 0, 512), R("eyeb", *C), R("xa", *blocks[lo]), False, True)
+                mm(R("y%d" % lo, 0, 512), R(lt, 0, 128, 1, rows), R("exq", 0, 512, 1, rows), lo not in begun, lo in begun)
+                begun.add(lo)
             elif name == "size":
-                act(R("ad", *blocks[lo]), R("y%d" % lo, 0, 512), AF.Abs)
+                act(R("ad", *banks[lo]), R("y%d" % lo, 0, 512), AF.Abs)
             elif name == "sum":
                 for j in range(4):
                     a = 512 * lo + 128 * j
                     mm(R("pT", 128 + 4 * j + lo, 256, 16), R("ad", a, a + 128), R("blkb", 0, 128, 16), True, True)
+            elif name == "floor":
+                ts(R("q5", *C), R("sq", *C), 2.0 ** -5, A.mult, -0.375, A.add)
             elif name == "names":
                 if not last:
-                    cp(I(E, R(pl, 0, 8)), R(cf, 128, 256))
+                    cp(I(E, PL), R(vp, 136, 264))
             elif name == "next":
-                tt(R("r2", *C), R("q5", *C), R("pM", 128, 256), A.add)
+                tt(R("r2", *C), R("q5", *C), R("pM", 256, 384), A.add)
+                if last:
+                    ts(R("zf", *C), R("zi", *C), 128.0, A.add)
                 ts(R("cN", *C), R("r2", *C), 2047, A.bitwise_and)
                 if last:
-                    cp(R("ycb", *C), R("cN", *C))
+                    recast(R("ycb", *C), R("cN", *C))
                     for n, (o, b) in enumerate(((T.yz, "zf"), (T.yc, "ycb"))):
                         need("y", [R(b, *C)], [])
                         g.sync.dma_start(o[:], T[b][:]).then_inc(T.sem["out%d" % n], 16)
                 else:
                     ts(R("kc", *C), R("r2", *C), 3, A.bitwise_and)
-        if not last:
-            act(R("K", *C), R("kc", *C), bias=2044.0)
-            lists()
+            elif name == "keys":
+                if not last:
+                    keys()
         tt(R("bb", *C), R("pT", 128, 256), R("lim", *C), A.is_lt)
         mm(R("pU", 128, 136), R("bb", *C), R("indM", 0, 8), False, True)
         if not last:
-            mm(R("pT", *C), R("K", *C), R("eye", *C), True, True)
-        tt(R("of", 0, 8), R("pU", 128, 136), R(lp, 0, 8), A.max)
+            turn()
+        tt(R("of", 0, 8), R("pU", 128, 136), R(lv, 128, 136), A.max)
         if last:
             cp(I(XW, R("of", 0, 8)), R(lv, *C))
         else:
-            act(R("KT", *C), R("pT", *C))
-            cp(I(EW, R("of", 0, 8)), R(la, 128, 256))
+            cp(I(EW, R("of", 0, 8)), R(lv, 136, 264))
             bounds()
-            later()
     need("y", [X], [])
     g.sync.dma_start(T.yx[:], T.xtab[:, 0:2048]).then_inc(T.sem.out2, 16)
     g.wait_ge(T.sem.loc, sent[0])

@@ -3,7 +3,11 @@ from concourse.mybir import AluOpType, ActivationFunctionType as AF
 STEPS = 3
 MID = 7168
 EDGE = 61440.0
-WIN = 11 * 2048 + 128
+FAR = 2064.0
+SPARE = 23712
+WIN = 24736
+ROUND = 1.5 * 2 ** 27
+EARLY = 96
 
 
 def _sb(w, d):
@@ -15,48 +19,55 @@ def _ps(w):
 
 
 SCRATCH = {
-    "rec0": _sb(2048, "int32"), "dI": _sb(2048, "int32"), "dM": _sb(2048, "int32"), "xi": _sb(2048, "int32"),
-    "etab": _sb(WIN, "int32"), "xtab": _sb(WIN, "bfloat16"), "y": _sb(128, "bfloat16"), "w": _sb(128, "bfloat16"),
-    "row": _sb(256, "int32"), "rowh": _sb(256, "float16"),
-    "pI": _sb(8, "int32"), "pF": _sb(8, "float32"), "iA": _sb(512, "bfloat16"), "iB": _sb(512, "bfloat16"), "iC": _sb(128, "bfloat16"),
-    "iD": _sb(128, "bfloat16"), "iE": _sb(16, "float32"), "exn": _sb(512, "float16"), "exq": _sb(512, "bfloat16"),
-    "eye": _sb(128, "float16"), "eyeb": _sb(128, "bfloat16"), "n4096": _sb(128, "float16"), "blk": _sb(128, "float16"), "blkb": _sb(128, "bfloat16"),
-    "blk128": _sb(128, "bfloat16"), "offd": _sb(128, "float16"), "ones": _sb(128, "float16"), "m128": _sb(128, "bfloat16"),
-    "indM": _sb(8, "bfloat16"), "spare": _sb(8, "float16"), "ci": _sb(8, "float16"), "base": _sb(8, "float32"), "pq": _sb(8, "uint16"),
-    "dk": _sb(128, "float16"), "dodd": _sb(128, "bfloat16"), "lim": _sb(128, "float32"),
-    "rmin": _sb(512, "float16"), "rmax": _sb(512, "float16"),
-    "cN": _sb(128, "int32"), "kc": _sb(128, "int32"), "lst": _sb(128, "uint16"), "cq": _sb(128, "float16"), "K": _sb(128, "float16"),
-    "KT": _sb(128, "float16"), "a32": _sb(128, "int32"), "cl": _sb(128, "uint16"),
+    "rec0": _sb(2048, "int32"), "dI": _sb(2048, "int32"), "xi": _sb(2048, "int32"),
+    "etab": _sb(WIN, "int32"), "xtab": _sb(WIN + 1024, "bfloat16"),
+    "y": _sb(128, "bfloat16"), "w": _sb(128, "bfloat16"), "row": _sb(256, "int32"), "rowh": _sb(256, "float16"),
+    "pI": _sb(32, "int32"), "pF": _sb(24, "float32"), "iA": _sb(512, "bfloat16"), "iC": _sb(128, "bfloat16"),
+    "iE": _sb(40, "float32"), "exn": _sb(512, "float16"),
+    "eye": _sb(128, "float16"), "neye": _sb(128, "float16"), "eyeb": _sb(128, "bfloat16"), "n4096": _sb(128, "float16"), "p4096": _sb(128, "float16"),
+    "blk": _sb(128, "float16"), "blk128": _sb(128, "bfloat16"), "sel": _sb(288, "float16"), "rnd": _sb(16, "float16"),
+    "ones": _sb(128, "float16"), "m128": _sb(128, "bfloat16"), "indM": _sb(8, "bfloat16"), "spare": _sb(16, "float16"),
+    "base": _sb(8, "float16"), "pm": _sb(8, "uint16"), "dk": _sb(128, "float16"), "dodd": _sb(128, "bfloat16"),
+    "lim": _sb(128, "float32"), "rmin": _sb(512, "float16"), "rmax": _sb(512, "float16"),
+    "cN": _sb(128, "int32"), "kc": _sb(128, "int32"), "lst": _sb(128, "uint16"), "K": _sb(128, "float16"), "KT": _sb(128, "float16"),
+    "F": _sb(128, "int32"),
     "dg": _sb(2048, "float16"), "ya": _sb(2048, "float16"), "sc": _sb(2048, "float16"), "xh": _sb(2048, "float16"),
     "mx": _sb(2048, "float16"), "mn": _sb(2048, "float16"), "xa": _sb(2048, "bfloat16"), "ad": _sb(2048, "bfloat16"),
-    "zi": _sb(128, "int32"), "wz": _sb(128, "float16"), "dv": _sb(128, "bfloat16"), "du": _sb(128, "int32"), "a15": _sb(8, "int32"),
+    "zi": _sb(128, "int32"), "wz": _sb(128, "float16"), "dv": _sb(128, "bfloat16"),
     "zf": _sb(128, "bfloat16"), "qf": _sb(128, "float16"), "umh": _sb(128, "float16"), "sq": _sb(128, "float32"), "q5": _sb(128, "int32"),
-    "r2": _sb(128, "int32"), "bb": _sb(128, "bfloat16"), "of": _sb(8, "uint16"), "ycb": _sb(128, "float32"),
+    "r2": _sb(128, "int32"), "bb": _sb(384, "bfloat16"), "of": _sb(24, "uint16"), "back": _sb(8, "float32"), "ycb": _sb(128, "float32"),
     "y0": _ps(512), "y1": _ps(512), "y2": _ps(512), "y3": _ps(512),
     "pW": _ps(384),
-    "pU": _ps(136),
-    "pM": _ps(384),
+    "pU": _ps(384),
+    "pM": _ps(512),
     "pT": _ps(256),
 }
 for _t in range(STEPS):
-    SCRATCH["cf%d" % _t] = _sb(128, "uint16")
+    SCRATCH["cl%d" % _t] = _sb(128, "uint16")
     SCRATCH["la%d" % _t] = _sb(128, "uint16")
-    SCRATCH["vt%d" % _t] = _sb(128, "bfloat16")
-    SCRATCH["lt%d" % _t] = _sb(128, "bfloat16")
+    for _h in "01":
+        SCRATCH["vt%d%s" % (_t, _h)] = _sb(128, "float16")
+        SCRATCH["lt%d%s" % (_t, _h)] = _sb(128, "float16")
     SCRATCH["vp%d" % _t] = _sb(136 if _t == STEPS - 1 else 264, "uint16")
     SCRATCH["lv%d" % _t] = SCRATCH["vp%d" % _t]
 PSUM = [k for k in SCRATCH if SCRATCH[k][0] == "psum"]
 SEMAPHORES = ["qv", "qs", "qp", "qg", "loc"] + ["ld%d" % k for k in range(12)] + ["out%d" % k for k in range(4)] + \
-    [a + str(k) for a in ("ac", "av", "ap") for k in range(STEPS)]
+    [a + str(k) for a in ("la", "lv") for k in range(STEPS)] + ["lt%d%d" % (k, h) for k in range(STEPS) for h in range(2)]
 
 LOADS = (0, 512, 1024, 1536, 2048)
-UNPACK = (0, 512, 1024, 1536, 1792, 2048)
-READ = ("vD 0 32", "sD 32 64", "vD 64 112", "sD 112 128", "abs 0", "abs 1", "near 0 32", "arrived", "abs 2", "need 0 32", "near 32 64",
-        "abs 3", "raise 0 32", "near 64 96", "sX 0 32", "need 32 96", "near 96 128", "raise 32 96", "sX 32 64", "need 96 128", "max 0 32",
-        "raise 96 128", "min 0 32", "sX 64 96", "codes", "max 32 64", "min 32 64", "sX 96 112", "max 64 96", "min 64 96", "sX 112 128",
-        "max 96 112", "min 96 112", "max 112 128", "min 112 128")
-JUDGE = ("vA 0 16", "sA 16 32", "x 0", "vA 32 64", "sA 96 128", "v 0", "v 1", "x 1", "size 0", "vA 64 96", "v 3", "x 3", "v 2", "size 1",
-         "floor", "x 2", "size 3", "sum 0", "next", "sum 1", "names", "size 2", "sum 3", "sum 2", "keys")
+UNPACK = ("bounds", "value 0 32", "name 0 32", "name 32 64", "twice 0 32", "value 32 64", "coded 0 32", "twice 32 64", "name 64 96",
+          "value 64 96", "coded 32 64", "twice 64 96", "name 96 112", "name 112 128", "twice 96 112", "twice 112 128", "coded 64 96",
+          "coded 96 112", "coded 112 128", "value 96 128")
+READ = ("vD 0 32", "sD 32 64", "vD 64 112", "sD 112 128", "sub 0", "sub 1", "abs 0", "sub 2", "abs 1", "sub 3", "arrived", "near 0 32",
+        "need 0 32", "near 32 64", "raise 0 32", "sums", "abs 2", "abs 3", "near 64 96", "need 32 96", "sX 0 32", "near 96 128", "raise 32 96",
+        "need 96 128", "vX 32 48", "raise 96 128", "send", "min 0 32", "max 0 32", "sX 48 64", "sX 64 96", "min 32 64", "max 32 64",
+        "sX 96 128", "min 64 96", "max 64 96", "late", "code", "z 0 96", "max 96 128", "dv 0 96", "wz 0 96", "turn 0 96", "rows 0 96",
+        "min 96 128", "turned 0 96", "z 96 128", "factor", "wz 96 128", "dv 96 128", "rows 96 128", "whole", "turn 96 128", "order",
+        "values", "place", "quot", "turned 96 128", "give", "own", "rem")
+JUDGE = ("v 0", "vA 0 24", "sA 24 32", "x 0", "sA 64 96", "vA 32 64", "vA 96 128", "v 2", "x 2", "size 0", "v 1", "x 1", "v 3", "size 2", "x 3",
+         "size 1", "size 3", "floor", "names", "sum 0", "sum 2", "sum 1", "next", "mask", "keys", "sum 3")
+LAST = ("v 0", "v 1", "vA 0 32", "sA 32 64", "x 0", "vA 64 96", "x 1", "v 2", "size 0", "x 2", "size 1", "floor", "vA 96 128", "v 3", "sum 0",
+        "size 2", "sum 1", "x 3", "next", "count 0", "size 3", "mask", "let 0", "back", "write 0", "sum 2", "sum 3", "count 1", "let 1", "write 1")
 
 
 def R(name, lo, hi, st=1, p=None):
@@ -65,6 +76,10 @@ def R(name, lo, hi, st=1, p=None):
 
 def I(win, off):
     return ("indirect", win, off)
+
+
+def row(n):
+    return (n >> 3) + 2 * (n & 3) + 8 * ((n >> 2) & 1)
 
 
 def rank_program(g, core, T, topo):
@@ -169,9 +184,8 @@ def rank_program(g, core, T, topo):
     def mm(o, l, r, start, stop):
         op("p", lambda: g.tensor.matmul(ap(o), ap(l), ap(r), start, stop), [o], [l, r])
 
-    def iota(o, pat, cm=0):
-        small = SCRATCH[o[0]][2] != "int32"
-        op("g", lambda: g.iota(ap(o), pat, 0, cm, allow_small_or_imprecise_dtypes=small), [o], [])
+    def iota(o, pat, first=0, cm=0):
+        op("g", lambda: g.iota(ap(o), pat, first, cm, allow_small_or_imprecise_dtypes=True), [o], [])
 
     def recast(o, i):
         n = o[2] - o[1]
@@ -195,43 +209,52 @@ def rank_program(g, core, T, topo):
     load("y", R("w", *C), T.wt[:])
     load("y", R("y", *C), T.aim[:])
 
-    PG, P32, P16, P8, P0, ODD, PQ = [R("pF", k, k + 1) for k in range(7)]
-    for k, m in enumerate((1, 16, 32, 64)):
-        iota(R("pI", k, k + 1), [[0, 1]], m)
-    iota(P0, [[0, 1]], 1)
+    P32, P16, P2 = [R("pF", k, k + 1) for k in (0, 1, 15)]
+    P0, PG, ODD, PM = [R("pF", k, k + 1) for k in range(16, 20)]
+    TOM = R("pm", 0, 8)
+    iota(P0, [[0, 1]], 0, 1)
+    iota(R("iE", 0, 16), [[16, 16]], 16)
     iota(R("iC", *C), [[1, 128]])
+    iota(R("iE", 16, 24), [[8, 8]])
     iota(R("iA", 0, 512), [[16, 32], [0, 16]])
-    iota(R("iE", 0, 8), [[512, 8]])
-    iota(R("iE", 8, 16), [[64, 4], [512, 2]])
-    iota(R("iD", *C), [[0, 8], [32, 16]])
     fill(R("rmin", 0, 512), -EDGE)
     fill(R("ones", *C), 1.0)
+    ts(R("pI", 0, 16), R("iE", 0, 16), P0, A.mult)
     fill(R("rmin", 0, 512, 16), EDGE)
+    ts(R("pI", 16, 32), R("pI", 0, 16), 496, A.bitwise_and)
     fill(R("m128", *C), -128.0)
-    ts(R("pI", 4, 8), R("pI", 0, 4), 496, A.bitwise_and)
-    fill(R("spare", 0, 8), 11 * 2048 / 128)
     act(R("rmax", 0, 512), R("rmin", 0, 512), scale=-1.0)
-    cp(R("pF", 0, 4), R("pI", 4, 8))
+    cp(R("pF", 0, 16), R("pI", 16, 32))
     ts(R("eye", *C), R("iC", *C), P0, A.is_equal)
+    ts(PM, P2, 1.875, A.mult, P16, A.add)
+    ts(PG, P16, -1 / 32, A.mult, P0, A.add)
+    ts(R("iE", 24, 32), R("iE", 16, 24), PM, A.add, 2.0, A.mult)
     ts(ODD, P16, 0.0625, A.mult, 1.0, A.add)
-    ts(PQ, P8, 15.5, A.mult, P16, A.add)
+    act(R("neye", *C), R("eye", *C), scale=-1.0)
     act(R("eyeb", *C), R("eye", *C))
-    act(R("n4096", *C), R("eye", *C), scale=-4096.0)
-    ts(R("dodd", *C), R("iC", *C), P0, A.is_equal, ODD, A.mult)
+    fill(R("spare", 0, 8), SPARE / 128)
+    fill(R("sel", 0, 288), 0.0)
     ts(R("kc", *C), R("cN", *C), 3, A.bitwise_and)
+    act(R("n4096", *C), R("eye", *C), scale=-4096.0)
+    ts(R("base", 0, 8), R("iE", 24, 32), 7.5 - 1024, A.add)
+    ts(TOM, R("iE", 24, 32), 0.0625, A.mult)
+    act(R("p4096", *C), R("eye", *C), scale=4096.0)
     ts(R("exn", 0, 512), R("iA", 0, 512), P32, A.is_equal, -4096.0, A.mult)
     ts(R("blk", *C), R("iA", *C), PG, A.is_equal)
-    ts(R("ci", 0, 8), R("iE", 0, 8), P16, A.add, 1 / 32, A.mult)
-    ts(R("base", 0, 8), R("iE", 0, 8), P16, A.add, 0.5, A.mult)
-    ts(R("pq", 0, 8), R("iE", 8, 16), PQ, A.add, 1 / 64, A.mult)
-    ts(R("offd", *C), R("iD", *C), P16, A.not_equal, 32.0, A.mult)
+    ts(R("dodd", *C), R("iC", *C), P0, A.is_equal, ODD, A.mult)
 
     def rest():
-        ts(R("rowh", 0, 256, 1, ONE), R("row", 0, 256, 1, ONE), -2048.0, A.add)
-        mm(R("pM", 0, 256), R("ones", 0, 128, 1, ONE), R("rowh", 0, 256, 1, ONE), True, True)
-        ts(R("exq", 0, 512), R("iB", 0, 512), P32, A.is_equal, -1.0, A.mult)
-        tt(R("dk", *C), R("eye", *C), R("pM", *C), A.mult)
-        ts(R("lim", *C), R("pM", 128, 256), 2048.0, A.add)
+        ts(R("rnd", 0, 8), R("iE", 24, 32), 16.0 * EARLY, A.is_lt, ROUND / 4096, A.mult)
+        ts(R("rnd", 8, 16), R("iE", 24, 32), 16.0 * EARLY, A.is_ge, ROUND / 4096, A.mult)
+        ts(R("sel", 15, 143, 16), R("iA", 0, 128, 16), PG, A.is_equal, -1.0, A.mult)
+        ts(R("sel", 159, 287, 16), R("iA", 0, 128, 16), PG, A.is_equal)
+
+    def late():
+        act(R("rowh", 0, 256, 1, ONE), R("row", 0, 256, 1, ONE), bias=-2048.0)
+        act(R("blk128", *C), R("blk", *C), scale=128.0)
+        mm(R("pM", 256, 512), R("ones", 0, 128, 1, ONE), R("rowh", 0, 256, 1, ONE), True, True)
+        act(R("indM", 0, 8), R("blk", 0, 128, 16), scale=-FAR)
+        act(R("lim", *C), R("pM", 384, 512), scale=-FAR, bias=-2048 * FAR)
 
     def keys():
         recast(R("lst", *C), R("cN", *C))
@@ -246,32 +269,28 @@ def rank_program(g, core, T, topo):
             rows = (32 * b, 32 * b + 32)
             mm(R("y%d" % b, 0, 512), R("KT", 0, 128, 1, rows), R("exn", 0, 512, 1, rows), True, False)
         act(R("pW", 256, 384), R("kc", *C), scale=4095.0)
-        act(R("cq", *C), I(R("cN", *C), R("pq", 0, 8)))
 
     keys()
-    iota(R("iB", 0, 512), [[16, 4], [64, 8], [0, 16]])
-    act(R("blkb", *C), R("blk", *C))
-    turn()
-    act(R("blk128", *C), R("blk", *C), scale=128.0)
-    act(R("indM", 0, 8), R("blk", 0, 128, 16), scale=-2048.0)
-    bounds()
-    pieces = list(zip(UNPACK, UNPACK[1:]))
-    for n, k in enumerate(pieces + [None]):
-        if k:
+
+    for word in UNPACK:
+        name, lo, hi = (word.split() + [0, 0])[:3]
+        k = (16 * int(lo), 16 * int(hi))
+        if name == "name":
             ts(R("dI", *k), R("rec0", *k), 2047, A.bitwise_and)
-            act(R("dM", *k), R("dI", *k), scale=4097.0)
-            if n < len(pieces) - 2:
-                act(R("xi", *k), R("rec0", *k), scale=2.0 ** -11, bias=-1023.5 / 2048)
-                recast(R("xtab", *k), R("xi", *k))
-        if n:
-            ts(R("etab", *pieces[n - 1]), R("dM", *pieces[n - 1]), 14332, A.bitwise_and)
-    k = (pieces[-2][0], pieces[-1][1])
-    act(R("xi", *k), R("rec0", *k), scale=2.0 ** -11, bias=-1023.5 / 2048)
-    recast(R("xtab", *k), R("xi", *k))
+        elif name == "twice":
+            act(R("dI", *k), R("dI", *k), scale=4097.0)
+        elif name == "coded":
+            ts(R("etab", *k), R("dI", *k), 14332, A.bitwise_and)
+        elif name == "value":
+            act(R("xi", *k), R("rec0", *k), scale=2.0 ** -11, bias=-1023.5 / 2048)
+            recast(R("xtab", *k), R("xi", *k))
+        elif name == "bounds":
+            turn()
+            bounds()
 
     sent = [0]
 
-    def send(t, src, land, sem):
+    def send(t, src, land):
         dst = T.cores[(rank + 1 + t % (N - 1)) % N]
         back = T.cores[(rank - 1 - t % (N - 1)) % N]
         rid, pid = topo.addr(dst, core)
@@ -279,17 +298,26 @@ def rank_program(g, core, T, topo):
         n = len(topo.engines(back, core)[:8])
         width = SCRATCH[src][1][1]
         need("g", [R(src, 0, width)], [])
-        g.remote_dma(T[land][:], T[src][:], T.sem[sem], T.sem.loc, pid, rid, sum(1 << e for e in eng))
+        g.remote_dma(T[land][:], T[src][:], T.sem[land], T.sem.loc, pid, rid, sum(1 << e for e in eng))
         sent[0] += len(eng)
-        event(sem, T.sem[sem], n, [R(land, 0, width)])
+        event(land, T.sem[land], n, [R(land, 0, width)])
+
+    def store(n, out, b):
+        need("y", [b], [])
+        g.sync.dma_start(out, ap(b)).then_inc(T.sem["out%d" % n], 16)
+
+    def spare(h):
+        mm(R("pU", 128 + 8 * h, 136 + 8 * h), R("eye", *C), R("base", 0, 8), True, False)
+        mm(R("pU", 128 + 8 * h, 136 + 8 * h), R("ones", *C), R("spare", 8 * h, 8 * h + 8), False, False)
 
     E, X = R("etab", 0, 2048), R("xtab", 0, 2048)
     EW, XW = R("etab", 0, WIN), R("xtab", 0, WIN)
     for t in range(STEPS):
         last = t == STEPS - 1
-        cf, la, vt, lt, vp, lv = [a + str(t) for a in ("cf", "la", "vt", "lt", "vp", "lv")]
+        cl, la, vt, lt, vp, lv = [a + str(t) for a in ("cl", "la", "vt", "lt", "vp", "lv")]
         PL = R(vp, 128, 136)
-        for word in READ:
+        begun = set()
+        for word in READ + (LAST if last else JUDGE):
             name, lo, hi = (word.split() + [0, 0])[:3]
             lo, hi = int(lo), int(hi)
             k = (16 * lo, 16 * hi)
@@ -302,66 +330,111 @@ def rank_program(g, core, T, topo):
                     cp(I(XW, R("of", 0, 8)), R("lv%d" % (t - 1), *C))
                 else:
                     rest()
-            elif name == "abs":
+            elif name == "sub":
                 mm(R("y%d" % lo, 0, 512), R("eye", *C), R("dg", *banks[lo]), False, True)
+            elif name == "abs":
                 act(R("ya", *banks[lo]), R("y%d" % lo, 0, 512), AF.Abs, bias=float(MID + 4095 * 2044))
             elif name == "near":
                 scan(R("sc", *k), R("rmin", 0, k[1] - k[0]), R("ya", *k), A.max, A.min)
             elif name == "need":
-                tt(R("a32", lo, hi), R("K", lo, hi), R("sc", k[0] + 15, k[1], 16), A.subtract)
+                mm(R("pU", 256 + lo, 256 + hi), R("eye", *C), R("K", lo, hi), True, False)
+                mm(R("pU", 256 + lo, 256 + hi), R("neye", *C), R("sc", k[0] + 15, k[1], 16), False, True)
             elif name == "raise":
-                tt(R("cl", lo, hi), R("a32", lo, hi), R("lst", lo, hi), A.max)
-            elif name == "codes":
-                tt(R(cf, *C), I(R("a32", *C), R("pq", 0, 8)), R("cq", *C), A.max)
-                send(t, cf, la, "ac%d" % t)
-                if t == 0:
-                    mm(R("pW", *C), R("eyeb", *C), R("w", *C), True, True)
-                    mm(R("pW", 128, 256), R("eyeb", *C), R("y", *C), True, False)
-                    mm(R("pW", 128, 256), R("eyeb", *C), R("m128", *C), False, True)
-                mm(R("pU", *C), R("n4096", *C), R("offd", *C), True, False)
-                mm(R("pM", *C), R("blk128", *C), R("w", *C), True, False)
+                tt(R(cl, lo, hi), R("pU", 256 + lo, 256 + hi), R("lst", lo, hi), A.max)
+            elif name == "send":
+                send(t, cl, la)
+            elif name == "code":
+                if last:
+                    fill(R("spare", 8, 16), (SPARE - 1024) / 128)
+                else:
+                    tt(R("F", *C), R(cl, *C), R("pW", 256, 384), A.add)
+            elif name == "order":
+                if last:
+                    ts(R("zf", *C), R("zi", *C), 128.0, A.add)
+                    store(0, T.yz[:], R("zf", *C))
+                    fill(R("bb", 128, 384), 0.0)
+                else:
+                    cp(R(vp, 136, 264), I(R("F", *C), TOM))
             elif name == "vX":
-                ts(R("xh", *k), I(X, R("cl", lo, hi)), 0.5, A.mult, -64.125, A.add)
+                ts(R("xh", *k), I(X if t else R("xi", 0, 2048), R(cl, lo, hi)), 0.5, A.mult, -64.125, A.add)
             elif name == "sX":
-                act(R("xh", *k), I(X, R("cl", lo, hi)), bias=-64.125, scale=0.5)
+                act(R("xh", *k), I(X if t else R("xi", 0, 2048), R(cl, lo, hi)), bias=-64.125, scale=0.5)
             elif name == "max":
                 scan(R("mx", *k), R("rmax", 0, k[1] - k[0]), R("xh", *k), A.min, A.max)
             elif name == "min":
                 scan(R("mn", *k), R("rmin", 0, k[1] - k[0]), R("xh", *k), A.max, A.min)
-        tt(R("zi", *C), R("mx", 15, 2048, 16), R("mn", 15, 2048, 16), A.add)
-        tt(R("wz", *C), R("zi", *C), R("pW", *C), A.mult)
-        tt(R("dv", *C), R("zi", *C), R("pW", 128, 256), A.subtract)
-        mm(R("pU", *C), R("blk", *C), R("wz", *C), False, True)
-        for c in range(4):
-            mm(R("pT", 0, 128, 1, (32 * c, 32 * c + 32)), R("dv", c, 128, 4), R("eyeb", *C), True, True)
-        mm(R("pM", *C), R("blk", *C), R("wz", *C), False, True)
-        mm(R("pM", 128, 256), R("blk128", *C), R("w", *C), True, False)
-        mm(R("pM", 128, 256), R("blk", *C), R("wz", *C), False, False)
-        act(R(vp, *C), R("dv", *C), AF.Abs)
-        if not last:
-            tt(R(vp, 136, 264), R("cl", *C), R("pW", 256, 384), A.add)
-        scan(R("du", *C), R("rmax", *C), R("pU", *C), A.min, A.max)
-        act(R(vt, *C), R("pT", *C), AF.Abs)
-        send(t, vt, lt, "av%d" % t)
-        ts(R("a15", 0, 8), R("du", 15, 128, 16), 15, A.bitwise_and)
-        act(R("qf", *C), R("pM", *C), scale=2.0 ** -12, bias=1025.0 - 2047.5 / 4096)
-        mm(R("pM", 128, 256), R("n4096", *C), R("qf", *C), False, True)
-        tt(PL, R("a15", 0, 8), R("base", 0, 8), A.add)
-        send(t, vp, lv, "ap%d" % t)
-        cp(I(X, PL), R(vp, *C))
-        act(R("umh", *C), R("pM", 128, 256), bias=4096.0 * 1025 - 2048)
-        act(R("sq", *C), R("pM", 128, 256), AF.Square, bias=4096.0 * 1025)
-        mm(R("pM", 256, 384), R("dodd", *C), R("dv", *C), True, False)
-        mm(R("pM", 256, 384), R("dodd", *C), R("y", *C), False, False)
-        mm(R("pM", 256, 384), R("dk", *C), R("umh", *C), False, True)
-        mm(R("pU", 128, 136), R("eye", *C), R("ci", 0, 8), True, False)
-        mm(R("pU", 128, 136), R("ones", *C), R("spare", 0, 8), False, False)
-        begun = set()
-        for word in JUDGE:
-            name, lo, hi = (word.split() + [0, 0])[:3]
-            lo, hi = int(lo), int(hi)
-            k = (16 * lo, 16 * hi)
-            if name == "vA":
+            elif name == "sums":
+                if t == 0:
+                    mm(R("pW", *C), R("eyeb", *C), R("w", *C), True, True)
+                    mm(R("pW", 128, 256), R("eyeb", *C), R("y", *C), True, False)
+                    mm(R("pW", 128, 256), R("eyeb", *C), R("m128", *C), False, True)
+            elif name == "late":
+                if t == 0:
+                    late()
+            elif name == "z":
+                tt(R("zi", lo, hi), R("mx", k[0] + 15, k[1], 16), R("mn", k[0] + 15, k[1], 16), A.add)
+            elif name == "wz":
+                tt(R("wz", lo, hi), R("zi", lo, hi), R("pW", lo, hi), A.mult)
+            elif name == "rows":
+                if lo == 0:
+                    mm(R("pU", 0, 8), R("eye", *C), R("base", 0, 8), True, False)
+                for sign in (0, 144):
+                    for n in range(lo // 8, hi // 8):
+                        a = sign + 15 - row(n)
+                        mm(R("pU", 0, 8), R("sel", a, a + 128), R("wz", 8 * n, 8 * n + 8), False, sign > 0 and n == 15)
+                    for m in ("p4096", "n4096") if sign == 0 else ():
+                        mm(R("pU", 0, 8), R(m, *C), R("rnd", 8, 16) if lo else R("rnd", 0, 8), False, False)
+            elif name == "dv":
+                tt(R("dv", lo, hi), R("zi", lo, hi), R("pW", 128 + lo, 128 + hi), A.subtract)
+            elif name == "turn":
+                mm(R("pT", 0, 128, 1, (lo, hi)), R("dv", lo, hi), R("eyeb", *C), True, True)
+            elif name == "turned":
+                h = str(int(lo > 0))
+                act(R(vt + h, *C), R("pT", *C), AF.Abs, scale=2.0 ** -12)
+                send(t, vt + h, lt + h)
+            elif name == "values":
+                act(R(vp, *C), I(R("dv", *C), TOM), AF.Abs)
+            elif name == "place":
+                ts(PL, R("pU", 0, 8), 1024.0, A.add)
+            elif name == "give":
+                send(t, vp, lv)
+            elif name == "own":
+                cp(I(X, PL), R(vp, *C))
+            elif name == "names":
+                if not last:
+                    cp(I(E, PL), R(vp, 136, 264))
+            elif name == "whole":
+                mm(R("pM", *C), R("blk128", *C), R("w", *C), True, False)
+                mm(R("pM", *C), R("blk", *C), R("wz", *C), False, True)
+            elif name == "factor":
+                if t == 0:
+                    tt(R("dk", *C), R("eye", *C), R("pM", 256, 384), A.mult)
+            elif name == "quot":
+                act(R("qf", *C), R("pM", *C), scale=2.0 ** -12, bias=1025.0 - 2047.5 / 4096)
+                mm(R("pM", 128, 256), R("blk128", *C), R("w", *C), True, False)
+                mm(R("pM", 128, 256), R("blk", *C), R("wz", *C), False, False)
+                mm(R("pM", 128, 256), R("n4096", *C), R("qf", *C), False, True)
+            elif name == "rem":
+                act(R("umh", *C), R("pM", 128, 256), bias=4096.0 * 1025 - 2048)
+                act(R("sq", *C), R("pM", 128, 256), AF.Square, bias=4096.0 * 1025)
+                mm(R("pM", 256, 384), R("dodd", *C), R("dv", *C), True, False)
+                mm(R("pM", 256, 384), R("dodd", *C), R("y", *C), False, False)
+                mm(R("pM", 256, 384), R("dk", *C), R("umh", *C), False, True)
+                spare(0)
+            elif name == "floor":
+                ts(R("q5", *C), R("sq", *C), 2.0 ** -5, A.mult, -0.375, A.add)
+            elif name == "next":
+                tt(R("r2", *C), R("q5", *C), R("pM", 256, 384), A.add)
+            elif name == "mask":
+                ts(R("cN", *C), R("r2", *C), 2047, A.bitwise_and)
+                if last:
+                    recast(R("ycb", *C), R("cN", *C))
+                    store(1, T.yc[:], R("ycb", *C))
+                else:
+                    ts(R("kc", *C), R("r2", *C), 3, A.bitwise_and)
+            elif name == "keys":
+                keys()
+            elif name == "vA":
                 cp(R("xa", *k), I(X, R(la, lo, hi)))
             elif name == "sA":
                 act(R("xa", *k), I(X, R(la, lo, hi)))
@@ -370,48 +443,36 @@ def rank_program(g, core, T, topo):
                 begun.add(lo)
             elif name == "v":
                 rows = (32 * lo, 32 * lo + 32)
-                mm(R("y%d" % lo, 0, 512), R(lt, 0, 128, 1, rows), R("exq", 0, 512, 1, rows), lo not in begun, lo in begun)
+                mm(R("y%d" % lo, 0, 512), R(lt + str(int(rows[0] >= EARLY)), 0, 128, 1, rows), R("exn", 0, 512, 1, rows), lo not in begun, lo in begun)
                 begun.add(lo)
             elif name == "size":
                 act(R("ad", *banks[lo]), R("y%d" % lo, 0, 512), AF.Abs)
             elif name == "sum":
                 for j in range(4):
                     a = 512 * lo + 128 * j
-                    mm(R("pT", 128 + 4 * j + lo, 256, 16), R("ad", a, a + 128), R("blkb", 0, 128, 16), True, True)
-            elif name == "floor":
-                ts(R("q5", *C), R("sq", *C), 2.0 ** -5, A.mult, -0.375, A.add)
-            elif name == "names":
-                if not last:
-                    cp(I(E, PL), R(vp, 136, 264))
-            elif name == "next":
-                tt(R("r2", *C), R("q5", *C), R("pM", 256, 384), A.add)
-                if last:
-                    ts(R("zf", *C), R("zi", *C), 128.0, A.add)
-                ts(R("cN", *C), R("r2", *C), 2047, A.bitwise_and)
-                if last:
-                    recast(R("ycb", *C), R("cN", *C))
-                    for n, (o, b) in enumerate(((T.yz, "zf"), (T.yc, "ycb"))):
-                        need("y", [R(b, *C)], [])
-                        g.sync.dma_start(o[:], T[b][:]).then_inc(T.sem["out%d" % n], 16)
-                else:
-                    ts(R("kc", *C), R("r2", *C), 3, A.bitwise_and)
-            elif name == "keys":
-                if not last:
-                    keys()
-        tt(R("bb", *C), R("pT", 128, 256), R("lim", *C), A.is_lt)
-        mm(R("pU", 128, 136), R("bb", *C), R("indM", 0, 8), False, True)
+                    mm(R("pT", 128 + row(4 * lo + j), 256, 16), R("ad", a, a + 128), R("indM", 0, 8), True, True)
+            elif name == "back":
+                ts(R("back", 0, 8), R(lv, 128, 136), -1024.0, A.add)
+            elif name == "count":
+                b = 128 + 128 * lo
+                tt(R("bb", b + lo, b + 128, 2), R("pT", 128 + lo, 256, 2), R("lim", lo, 128, 2), A.is_gt)
+                mm(R("pU", 128 + 8 * lo, 136 + 8 * lo), R("bb", b, b + 128), R("indM", 0, 8), False, True)
+                if lo == 0:
+                    spare(1)
+            elif name == "let":
+                tt(R("of", 8 + 8 * lo, 16 + 8 * lo), R("pU", 128 + 8 * lo, 136 + 8 * lo), R("back", 0, 8) if lo else R(lv, 128, 136), A.max)
+            elif name == "write":
+                cp(I(R("xtab", 1024 * lo, 1024 * lo + WIN), R("of", 8 + 8 * lo, 16 + 8 * lo)), R(lv, *C))
+                store(2 + lo, T.yx[:, 1024 * lo:1024 * lo + 1024], R("xtab", 1024 * lo, 1024 * lo + 1024))
         if not last:
+            tt(R("bb", *C), R("pT", 128, 256), R("lim", *C), A.is_gt)
+            mm(R("pU", 128, 136), R("bb", *C), R("indM", 0, 8), False, True)
             turn()
-        tt(R("of", 0, 8), R("pU", 128, 136), R(lv, 128, 136), A.max)
-        if last:
-            cp(I(XW, R("of", 0, 8)), R(lv, *C))
-        else:
+            tt(R("of", 0, 8), R("pU", 128, 136), R(lv, 128, 136), A.max)
             cp(I(EW, R("of", 0, 8)), R(lv, 136, 264))
             bounds()
-    need("y", [X], [])
-    g.sync.dma_start(T.yx[:], T.xtab[:, 0:2048]).then_inc(T.sem.out2, 16)
     g.wait_ge(T.sem.loc, sent[0])
-    for k in range(3):
+    for k in range(4):
         g.sync.wait_ge(T.sem["out%d" % k], 16)
     for q in "vspg":
         if seen["y"].get(q, 0) < count[q]:

@@ -1,73 +1,77 @@
-from concourse.mybir import AluOpType, ActivationFunctionType as AF
+from concourse.mybir import AluOpType, AxisListType, ActivationFunctionType as AF
 
 STEPS = 3
-MID = 7168
-EDGE = 61440.0
-FAR = 2064.0
-SPARE = 23712
-WIN = 24736
-ROUND = 1.5 * 2 ** 27
 EARLY = 96
+MID = 6140
+EDGE = 61440.0
+FAR = 2048.0
+PAD = 16
+SPARE = PAD + 11 * 2048
+WIN = SPARE + 2048
 
 
-def _sb(w, d):
-    return ("sbuf", [128, w], d)
+def _sb(w, d, run=None):
+    return ("sbuf", [128, w] if run is None else [128, w // run, run], d)
 
 
-def _ps(w):
-    return ("psum", [128, w], "float32")
+def _ps():
+    return ("psum", [128, 512], "float32")
 
 
+RUNS = ("psum", [128, 32, 16, 1], "float32")
 SCRATCH = {
     "rec0": _sb(2048, "int32"), "dI": _sb(2048, "int32"), "xi": _sb(2048, "int32"),
-    "etab": _sb(WIN, "int32"), "xtab": _sb(WIN + 1024, "bfloat16"),
+    "etab": _sb(WIN, "int32"), "xtab": _sb(WIN + 2048, "bfloat16"),
     "y": _sb(128, "bfloat16"), "w": _sb(128, "bfloat16"), "row": _sb(256, "int32"), "rowh": _sb(256, "float16"),
     "pI": _sb(32, "int32"), "pF": _sb(24, "float32"), "iA": _sb(512, "bfloat16"), "iC": _sb(128, "bfloat16"),
     "iE": _sb(40, "float32"), "exn": _sb(512, "float16"),
-    "eye": _sb(128, "float16"), "neye": _sb(128, "float16"), "eyeb": _sb(128, "bfloat16"), "n4096": _sb(128, "float16"), "p4096": _sb(128, "float16"),
-    "blk": _sb(128, "float16"), "blk128": _sb(128, "bfloat16"), "sel": _sb(288, "float16"), "rnd": _sb(16, "float16"),
-    "ones": _sb(128, "float16"), "m128": _sb(128, "bfloat16"), "indM": _sb(8, "bfloat16"), "spare": _sb(16, "float16"),
-    "base": _sb(8, "float16"), "pm": _sb(8, "uint16"), "dk": _sb(128, "float16"), "dodd": _sb(128, "bfloat16"),
+    "eye": _sb(128, "float16"), "neye": _sb(128, "float16"), "eyeb": _sb(128, "bfloat16"), "neyeb": _sb(128, "bfloat16"), "p4096": _sb(128, "float16"),
+    "blk": _sb(128, "float16"), "nblk": _sb(128, "float16"), "rep": _sb(128, "float16"), "i16": _sb(128, "float32"), "first": _sb(128, "float16"),
+    "num": _sb(1024, "float16"), "m128": _sb(128, "bfloat16"), "ind4": _sb(32, "bfloat16"), "ind2": _sb(2, "bfloat16"), "spare": _sb(16, "float16"), "shift": _sb(8, "float32"),
+    "dk": _sb(128, "float16"), "dodd": _sb(128, "bfloat16"), "wA": _sb(128, "float16"),
     "lim": _sb(128, "float32"), "rmin": _sb(512, "float16"), "rmax": _sb(512, "float16"),
-    "cN": _sb(128, "int32"), "kc": _sb(128, "int32"), "lst": _sb(128, "uint16"), "K": _sb(128, "float16"), "KT": _sb(128, "float16"),
-    "F": _sb(128, "int32"),
-    "dg": _sb(2048, "float16"), "ya": _sb(2048, "float16"), "sc": _sb(2048, "float16"), "xh": _sb(2048, "float16"),
-    "mx": _sb(2048, "float16"), "mn": _sb(2048, "float16"), "xa": _sb(2048, "bfloat16"), "ad": _sb(2048, "bfloat16"),
+    "cN": _sb(128, "int32"), "lst": _sb(128, "uint16"), "ch": _sb(128, "float16"), "KT": _sb(128, "float16"),
+    "dg": _sb(2048, "float16"), "ds": _sb(128, "float16"), "xh": _sb(2048, "float16"),
+    "mx": _sb(2048, "float16"), "mn": _sb(2048, "float16"), "xa": _sb(2048, "bfloat16"), "ad": _sb(2048, "bfloat16", 16),
     "zi": _sb(128, "int32"), "wz": _sb(128, "float16"), "dv": _sb(128, "bfloat16"),
-    "zf": _sb(128, "bfloat16"), "qf": _sb(128, "float16"), "umh": _sb(128, "float16"), "sq": _sb(128, "float32"), "q5": _sb(128, "int32"),
-    "r2": _sb(128, "int32"), "bb": _sb(384, "bfloat16"), "of": _sb(24, "uint16"), "back": _sb(8, "float32"), "ycb": _sb(128, "float32"),
-    "y0": _ps(512), "y1": _ps(512), "y2": _ps(512), "y3": _ps(512),
-    "pW": _ps(384),
-    "pU": _ps(384),
-    "pM": _ps(512),
-    "pT": _ps(256),
+    "zf": _sb(128, "bfloat16"), "umh": _sb(128, "float16"), "sq": _sb(128, "float32"),
+    "r2": _sb(128, "int32"), "q5": _sb(128, "int32"), "bb": _sb(512, "bfloat16"), "of": _sb(8, "uint16"), "back": _sb(8, "float32"), "ycb": _sb(128, "float32"),
+    "y0": RUNS, "y1": RUNS, "y2": RUNS, "y3": RUNS,
+    "pW": _ps(),
+    "pA": _ps(),
+    "pB": _ps(),
+    "pT": _ps(),
 }
 for _t in range(STEPS):
     SCRATCH["cl%d" % _t] = _sb(128, "uint16")
     SCRATCH["la%d" % _t] = _sb(128, "uint16")
-    for _h in "01":
+    for _h in "ab":
         SCRATCH["vt%d%s" % (_t, _h)] = _sb(128, "float16")
         SCRATCH["lt%d%s" % (_t, _h)] = _sb(128, "float16")
     SCRATCH["vp%d" % _t] = _sb(136 if _t == STEPS - 1 else 264, "uint16")
     SCRATCH["lv%d" % _t] = SCRATCH["vp%d" % _t]
 PSUM = [k for k in SCRATCH if SCRATCH[k][0] == "psum"]
-SEMAPHORES = ["qv", "qs", "qp", "qg", "loc"] + ["ld%d" % k for k in range(12)] + ["out%d" % k for k in range(4)] + \
-    [a + str(k) for a in ("la", "lv") for k in range(STEPS)] + ["lt%d%d" % (k, h) for k in range(STEPS) for h in range(2)]
+SEMAPHORES = ["qv", "qs", "qp", "qg", "loc"] + ["ld%d" % k for k in range(12)] + ["out%d" % k for k in range(6)] + \
+    [a + str(k) for a in ("la", "lv") for k in range(STEPS)] + ["lt%d%s" % (k, h) for k in range(STEPS) for h in "ab"]
+NUM = {"1": 1.0, "3/8": 0.375, "341.25": 341.25, "2045": 2045.0, "2^8": 256.0, "2^15": 32768.0, "+": 49152.0, "-": -49152.0}
 
 LOADS = (0, 512, 1024, 1536, 2048)
-UNPACK = ("bounds", "value 0 32", "name 0 32", "name 32 64", "twice 0 32", "value 32 64", "coded 0 32", "twice 32 64", "name 64 96",
-          "value 64 96", "coded 32 64", "twice 64 96", "name 96 112", "name 112 128", "twice 96 112", "twice 112 128", "coded 64 96",
-          "coded 96 112", "coded 112 128", "value 96 128")
-READ = ("vD 0 32", "sD 32 64", "vD 64 112", "sD 112 128", "sub 0", "sub 1", "abs 0", "sub 2", "abs 1", "sub 3", "arrived", "near 0 32",
-        "need 0 32", "near 32 64", "raise 0 32", "sums", "abs 2", "abs 3", "near 64 96", "need 32 96", "sX 0 32", "near 96 128", "raise 32 96",
-        "need 96 128", "vX 32 48", "raise 96 128", "send", "min 0 32", "max 0 32", "sX 48 64", "sX 64 96", "min 32 64", "max 32 64",
-        "sX 96 128", "min 64 96", "max 64 96", "late", "code", "z 0 96", "max 96 128", "dv 0 96", "wz 0 96", "turn 0 96", "rows 0 96",
-        "min 96 128", "turned 0 96", "z 96 128", "factor", "wz 96 128", "dv 96 128", "rows 96 128", "whole", "turn 96 128", "order",
-        "values", "place", "quot", "turned 96 128", "give", "own", "rem")
-JUDGE = ("v 0", "vA 0 24", "sA 24 32", "x 0", "sA 64 96", "vA 32 64", "vA 96 128", "v 2", "x 2", "size 0", "v 1", "x 1", "v 3", "size 2", "x 3",
-         "size 1", "size 3", "floor", "names", "sum 0", "sum 2", "sum 1", "next", "mask", "keys", "sum 3")
-LAST = ("v 0", "v 1", "vA 0 32", "sA 32 64", "x 0", "vA 64 96", "x 1", "v 2", "size 0", "x 2", "size 1", "floor", "vA 96 128", "v 3", "sum 0",
-        "size 2", "sum 1", "x 3", "next", "count 0", "size 3", "mask", "let 0", "back", "write 0", "sum 2", "sum 3", "count 1", "let 1", "write 1")
+UNPACK = """iC, p, p16, -, +, pI, 341.25, eye, 1, 3/8, pF, PH, 2045, PG, 2^8, p4096, neye, value 0 32, eyeb, iA, first, iE, keys, table 0 32, ODD,
+    name 0 32, 2^15, exn, name 32 64, twice 0 32, value 32 64, twice 32 64, value 64 96, rep, table 64 96, coded 0 32, name 64 96, key,
+    twice 64 96, keep, coded 32 64, name 96 112, twice 96 112, name 112 128, coded 64 96, coded 96 112, twice 112 128, bounds 0 4,
+    value 96 128, coded 112 128, table 96 128, table 32 64""".split(",")
+READ = """mul, th, rhigh, vD 32 64, m128, along, dk, rlow, spare, sD 0 32, sub 0, arrived, blk, least 0, sD 64 96, sub 1, least 1, sub 2, lim,
+    need 0 32, sD 96 128, own4, raise 0 32, sub 3, need 32 64, least 2, rmax, rmin, raise 32 64, need 64 96, pW, least 3, raise 64 96,
+    need 96 128, nblk, sX 0 32, max 0 32, min 0 32, sX 32 64, raise 96 128, pT, max 32 64, min 32 64, neyeb, sX 64 96, max 64 96, min 64 96,
+    ind4, sX 96 128, pturn 0 96, pz 0 96, pdv 0 96, send, pturned, wide, dodd, min 96 128, max 96 128, pwz 0 96, z 96 128, rows 0 96,
+    wz 96 128, dv 96 128, PA, place 0 96, ind2, rows 96 128, turn 96 128, pvalues 0 96, wA, pzs 0 96, zs 96 128, values 96 128,
+    place 96 128, own 0 96, turned, own 96 128, whole, keyed, code, give""".split(",")
+JUDGE = """vA 0 16, sA 16 32, x 0, rem, square, vA 64 96, v 1, v 0, lin, x 2, sA 32 64, floor, size 0, x 1, v 2, vA 96 128, next, mask, gwide, list,
+    size 1, v 3, x 3, sum 0, vsize 2, names, sum 1, less 1, less 0, key, sum 2, size 3, sum 3, less 2, keep, less 3, count 1, count 0, count 2,
+    count 3, bounds 0 1, let 0 4, named 0 4, bounds 1 4""".split(",")
+LAST = """vA 0 16, sA 16 32, vA 32 64, sA 64 96, x 0, v 0, size 0, vA 96 128, v 1, x 1, v 2, x 2, sum 0, x 3, vsize 1, v 3, sum 1, less 0, back,
+    square, rem, less 1, count 0, let 0 1, zout, floor, size 2, size 3, sum 2, less 2, write 0 1, lin, count 1, next, let 1 2, sum 3, less 3,
+    write 1 2, count 2, count 3, mask, let 2 3, write 2 3, let 3 4, write 3 4""".split(",")
 
 
 def R(name, lo, hi, st=1, p=None):
@@ -76,10 +80,6 @@ def R(name, lo, hi, st=1, p=None):
 
 def I(win, off):
     return ("indirect", win, off)
-
-
-def row(n):
-    return (n >> 3) + 2 * (n & 3) + 8 * ((n >> 2) & 1)
 
 
 def rank_program(g, core, T, topo):
@@ -103,8 +103,13 @@ def rank_program(g, core, T, topo):
     def ap(x):
         if x[0] == "indirect":
             return ap(x[1]).indirect(ap(x[2]))
-        rows = slice(None) if x[4] is None else slice(*x[4])
-        return T[x[0]][rows, x[1]:x[2]] if x[3] == 1 else T[x[0]][rows, x[1]:x[2]:x[3]]
+        name, lo, hi, st, p = x
+        rows = slice(None) if p is None else slice(*p)
+        if len(SCRATCH[name][1]) == 4:
+            return T[name][:, lo // 16:hi // 16:st, :, 0] if isinstance(st, int) else T[name][:, lo // 16:hi // 16, st[0]:st[1], 0]
+        if len(SCRATCH[name][1]) == 3:
+            return T[name][:, lo // 16:hi // 16, :]
+        return T[name][rows, lo:hi] if st == 1 else T[name][rows, lo:hi:st]
 
     def need(q, reads, writes):
         want = {}
@@ -148,7 +153,15 @@ def rank_program(g, core, T, topo):
         for x in outs:
             writes.append(flat(x)[0])
             reads += flat(x)[1:]
+        if q == "g":
+            if (writes[0][4] or ONE)[0]:
+                reads.append(R("any call", 0, 1))
+                writes.append(R("lone call", 0, 1))
+            else:
+                reads.append(R("lone call", 0, 1))
         need(q, reads, writes)
+        if q == "g":
+            writes.append(R("any call", 0, 1))
         i = call()
         count[q] += 1
         i.then_inc(T.sem["q" + q], 1)
@@ -175,21 +188,35 @@ def rank_program(g, core, T, topo):
     def scan(o, a, b, f0, f1):
         op("v", lambda: g.vector.tensor_tensor_scan(ap(o), ap(a), ap(b), 0.0, f0, f1), [o], [a, b])
 
+    def fold(o, i, f, size=False):
+        op("v", lambda: g.vector.tensor_reduce(ap(o), ap(i), AxisListType.X, f, apply_absolute_value=size), [o], [i])
+
     def fill(o, c):
         op("v", lambda: g.vector.memset(ap(o), c), [o], [])
 
     def act(o, i, f=AF.Identity, bias=0.0, scale=1.0):
         op("s", lambda: g.scalar.activation(ap(o), ap(i), f, bias=bias, scale=scale), [o], [i])
 
-    def mm(o, l, r, start, stop):
+    def mm(o, l, r, start=False, stop=False):
         op("p", lambda: g.tensor.matmul(ap(o), ap(l), ap(r), start, stop), [o], [l, r])
+
+    def plus(o, a, b, k, start=False, stop=False):
+        at = {n: 128 * j for j, n in enumerate(NUM)}
+        m = 128 if o[4] is None else o[4][1] - o[4][0]
+        mm(o, R("num", at[a], at[a] + m, 1, (0, k)), R("num", at[b], at[b] + o[2] - o[1], 1, (0, k)), start, stop)
+
+    def rounded(o, bits, stop=False):
+        for sign in "+-":
+            plus(o, "2^8" if bits < 7 else "2^15", sign, 2 ** bits if bits < 7 else 2 ** (bits - 7), False, stop and sign == "-")
 
     def iota(o, pat, first=0, cm=0):
         op("g", lambda: g.iota(ap(o), pat, first, cm, allow_small_or_imprecise_dtypes=True), [o], [])
 
+    def select(o, i, pat, cm=0, first=0, other=0.0):
+        op("g", lambda: g.affine_select(ap(o), ap(i), pat, A.is_equal, other, first, cm), [o], [i])
+
     def recast(o, i):
-        n = o[2] - o[1]
-        op("g", lambda: g.affine_select(ap(o), ap(i), [[0, n]], A.is_equal, 0.0, 0, 0), [o], [i])
+        select(o, i, [[0, o[2] - o[1]]])
 
     nload = [0]
 
@@ -209,68 +236,75 @@ def rank_program(g, core, T, topo):
     load("y", R("w", *C), T.wt[:])
     load("y", R("y", *C), T.aim[:])
 
-    P32, P16, P2 = [R("pF", k, k + 1) for k in (0, 1, 15)]
-    P0, PG, ODD, PM = [R("pF", k, k + 1) for k in range(16, 20)]
-    TOM = R("pm", 0, 8)
-    iota(P0, [[0, 1]], 0, 1)
-    iota(R("iE", 0, 16), [[16, 16]], 16)
-    iota(R("iC", *C), [[1, 128]])
-    iota(R("iE", 16, 24), [[8, 8]])
-    iota(R("iA", 0, 512), [[16, 32], [0, 16]])
-    fill(R("rmin", 0, 512), -EDGE)
-    fill(R("ones", *C), 1.0)
-    ts(R("pI", 0, 16), R("iE", 0, 16), P0, A.mult)
-    fill(R("rmin", 0, 512, 16), EDGE)
-    ts(R("pI", 16, 32), R("pI", 0, 16), 496, A.bitwise_and)
-    fill(R("m128", *C), -128.0)
-    act(R("rmax", 0, 512), R("rmin", 0, 512), scale=-1.0)
-    cp(R("pF", 0, 16), R("pI", 16, 32))
-    ts(R("eye", *C), R("iC", *C), P0, A.is_equal)
-    ts(PM, P2, 1.875, A.mult, P16, A.add)
-    ts(PG, P16, -1 / 32, A.mult, P0, A.add)
-    ts(R("iE", 24, 32), R("iE", 16, 24), PM, A.add, 2.0, A.mult)
-    ts(ODD, P16, 0.0625, A.mult, 1.0, A.add)
-    act(R("neye", *C), R("eye", *C), scale=-1.0)
-    act(R("eyeb", *C), R("eye", *C))
-    fill(R("spare", 0, 8), SPARE / 128)
-    fill(R("sel", 0, 288), 0.0)
-    ts(R("kc", *C), R("cN", *C), 3, A.bitwise_and)
-    act(R("n4096", *C), R("eye", *C), scale=-4096.0)
-    ts(R("base", 0, 8), R("iE", 24, 32), 7.5 - 1024, A.add)
-    ts(TOM, R("iE", 24, 32), 0.0625, A.mult)
-    act(R("p4096", *C), R("eye", *C), scale=4096.0)
-    ts(R("exn", 0, 512), R("iA", 0, 512), P32, A.is_equal, -4096.0, A.mult)
-    ts(R("blk", *C), R("iA", *C), PG, A.is_equal)
-    ts(R("dodd", *C), R("iC", *C), P0, A.is_equal, ODD, A.mult)
-
-    def rest():
-        ts(R("rnd", 0, 8), R("iE", 24, 32), 16.0 * EARLY, A.is_lt, ROUND / 4096, A.mult)
-        ts(R("rnd", 8, 16), R("iE", 24, 32), 16.0 * EARLY, A.is_ge, ROUND / 4096, A.mult)
-        ts(R("sel", 15, 143, 16), R("iA", 0, 128, 16), PG, A.is_equal, -1.0, A.mult)
-        ts(R("sel", 159, 287, 16), R("iA", 0, 128, 16), PG, A.is_equal)
-
-    def late():
-        act(R("rowh", 0, 256, 1, ONE), R("row", 0, 256, 1, ONE), bias=-2048.0)
-        act(R("blk128", *C), R("blk", *C), scale=128.0)
-        mm(R("pM", 256, 512), R("ones", 0, 128, 1, ONE), R("rowh", 0, 256, 1, ONE), True, True)
-        act(R("indM", 0, 8), R("blk", 0, 128, 16), scale=-FAR)
-        act(R("lim", *C), R("pM", 384, 512), scale=-FAR, bias=-2048 * FAR)
-
     def keys():
+        recast(R("ch", *C), R("cN", *C))
         recast(R("lst", *C), R("cN", *C))
-        act(R("K", *C), R("kc", *C), bias=2044.0)
 
-    def turn():
-        mm(R("pT", *C), R("K", *C), R("eye", *C), True, True)
-        act(R("KT", *C), R("pT", *C))
+    P32, P16 = [R("pF", k, k + 1) for k in (0, 1)]
+    P0, PG, ODD, PH, PA = [R("pF", k, k + 1) for k in range(16, 21)]
+    ROWS = (0, 16)
+    ONCE = {
+        "p": lambda: iota(P0, [[0, 1]], 0, 1),
+        "p16": lambda: (iota(R("pI", 0, 1), [[0, 1]], 0, 16), iota(R("pI", 1, 2), [[0, 1]], 0, 32)),
+        "iC": lambda: iota(R("iC", *C), [[1, 128]]),
+        "iA": lambda: iota(R("iA", 0, 512), [[16, 32], [0, 16]]),
+        "pI": lambda: ts(R("pI", 16, 18), R("pI", 0, 2), 496, A.bitwise_and),
+        "pF": lambda: cp(R("pF", 0, 2), R("pI", 16, 18)),
+        "PG": lambda: ts(PG, P16, -1 / 32, A.mult, P0, A.add),
+        "ODD": lambda: ts(ODD, P16, 0.0625, A.mult, 1.0, A.add),
+        "PH": lambda: ts(PH, P16, 0.5, A.mult),
+        "rlow": lambda: fill(R("rmin", 0, 512), -EDGE),
+        "rmin": lambda: fill(R("rmin", 0, 512, 16), EDGE),
+        "rhigh": lambda: fill(R("rmax", 0, 512), EDGE),
+        "rmax": lambda: fill(R("rmax", 0, 512, 16), -EDGE),
+        "m128": lambda: fill(R("m128", *C), -128.0),
+        "pT": lambda: fill(R("pT", *C), 0.0),
+        "eye": lambda: ts(R("eye", *C), R("iC", *C), P0, A.is_equal),
+        "neye": lambda: act(R("neye", *C), R("eye", *C), scale=-1.0),
+        "eyeb": lambda: act(R("eyeb", *C), R("eye", *C)),
+        "neyeb": lambda: act(R("neyeb", *C), R("eye", *C), scale=-1.0),
+        "p4096": lambda: act(R("p4096", *C), R("eye", *C), scale=4096.0),
+        "exn": lambda: ts(R("exn", 0, 512), R("iA", 0, 512), P32, A.is_equal, -4096.0, A.mult),
+        "blk": lambda: ts(R("blk", *C), R("iA", *C), PG, A.is_equal),
+        "dodd": lambda: ts(R("dodd", *C), R("iC", *C), P0, A.is_equal, ODD, A.mult),
+        "nblk": lambda: act(R("nblk", *C), R("blk", *C), scale=-1.0),
+        "ind4": lambda: act(R("ind4", 0, 32), R("blk", 0, 128, 4), scale=-FAR),
+        "PA": lambda: ts(PA, P32, 256.0, A.is_ge),
+        "ind2": lambda: ts(R("ind2", 0, 2), R("iC", 0, 2), PA, A.is_equal, -FAR, A.mult),
+        "own4": lambda: [select(R("lim", 0, 128, 1, (32 * k, 32 * k + 32)), R("lim", 0, 128, 1, (32 * k, 32 * k + 32)), [[0, 32], [1, 4]], 0, -k, 1.0)
+                         for k in range(4)],
+        "rep": lambda: select(R("rep", 0, 128, 1, ROWS), R("num", 0, 128, 1, ROWS), [[0, 8], [1, 16]], -1),
+        "first": lambda: (iota(R("i16", 0, 128, 1, ROWS), [[16, 128]], PAD),
+                          select(R("first", 0, 128, 1, ROWS), R("i16", 0, 128, 1, ROWS), [[0, 8], [1, 16]], -1)),
+        "iE": lambda: (iota(R("iE", 8, 16), [[256, 8]], SPARE), iota(R("iE", 16, 24), [[0, 4], [256, 2]], SPARE - PAD),
+                       iota(R("shift", 0, 8), [[512, 4], [0, 2]], PAD)),
+        "spare": lambda: ts(R("spare", 0, 16), R("iE", 8, 24), PH, A.add),
+        "mul": lambda: act(R("rowh", 0, 128, 1, ONE), R("row", 0, 128, 1, ONE), bias=-1920.0),
+        "th": lambda: act(R("rowh", 128, 256, 1, ONE), R("row", 128, 256, 1, ONE), bias=-2048.0),
+        "along": lambda: mm(R("pA", 256, 512), R("num", 0, 128, 1, ONE), R("rowh", 0, 256, 1, ONE), True, True),
+        "lim": lambda: act(R("lim", *C), R("pA", 384, 512), scale=-FAR, bias=-2048 * FAR),
+        "dk": lambda: tt(R("dk", *C), R("eye", *C), R("pA", 256, 384), A.mult),
+        "wA": lambda: act(R("wA", *C), R("w", *C), scale=128.0, bias=-128.0),
+        "pW": lambda: (mm(R("pW", *C), R("eyeb", *C), R("w", *C), True, True), mm(R("pW", 128, 256), R("eyeb", *C), R("y", *C), True),
+                       mm(R("pW", 128, 256), R("eyeb", *C), R("m128", *C), False, True)),
+    }
+    for j, n in enumerate(NUM):
+        ONCE[n] = (lambda j, n: lambda: fill(R("num", 128 * j, 128 * j + 128), NUM[n]))(j, n)
 
-    def bounds():
-        for b in range(4):
+    def key():
+        o = R("pB", 256, 384)
+        mm(o, R("ch", *C), R("neye", *C), True)
+        plus(o, "1", "3/8", 4)
+        rounded(o, 2)
+        mm(o, R("ch", *C), R("eye", *C), False, True)
+
+    def keep():
+        act(R("KT", *C), R("pB", 256, 384), bias=-1.0)
+
+    def bounds(lo, hi):
+        for b in range(lo, hi):
             rows = (32 * b, 32 * b + 32)
             mm(R("y%d" % b, 0, 512), R("KT", 0, 128, 1, rows), R("exn", 0, 512, 1, rows), True, False)
-        act(R("pW", 256, 384), R("kc", *C), scale=4095.0)
-
-    keys()
 
     for word in UNPACK:
         name, lo, hi = (word.split() + [0, 0])[:3]
@@ -280,15 +314,18 @@ def rank_program(g, core, T, topo):
         elif name == "twice":
             act(R("dI", *k), R("dI", *k), scale=4097.0)
         elif name == "coded":
-            ts(R("etab", *k), R("dI", *k), 14332, A.bitwise_and)
+            ts(R("etab", PAD + k[0], PAD + k[1]), R("dI", *k), 14332, A.bitwise_and)
         elif name == "value":
             act(R("xi", *k), R("rec0", *k), scale=2.0 ** -11, bias=-1023.5 / 2048)
-            recast(R("xtab", *k), R("xi", *k))
+        elif name == "table":
+            recast(R("xtab", PAD + k[0], PAD + k[1]), R("xi", *k))
         elif name == "bounds":
-            turn()
-            bounds()
+            bounds(int(lo), int(hi))
+        else:
+            dict(ONCE, keys=keys, key=key, keep=keep)[name]()
 
     sent = [0]
+    stored = [0]
 
     def send(t, src, land):
         dst = T.cores[(rank + 1 + t % (N - 1)) % N]
@@ -302,59 +339,71 @@ def rank_program(g, core, T, topo):
         sent[0] += len(eng)
         event(land, T.sem[land], n, [R(land, 0, width)])
 
-    def store(n, out, b):
+    def store(out, b):
         need("y", [b], [])
-        g.sync.dma_start(out, ap(b)).then_inc(T.sem["out%d" % n], 16)
+        g.sync.dma_start(out, ap(b)).then_inc(T.sem["out%d" % stored[0]], 16)
+        stored[0] += 1
 
-    def spare(h):
-        mm(R("pU", 128 + 8 * h, 136 + 8 * h), R("eye", *C), R("base", 0, 8), True, False)
-        mm(R("pU", 128 + 8 * h, 136 + 8 * h), R("ones", *C), R("spare", 8 * h, 8 * h + 8), False, False)
-
-    E, X = R("etab", 0, 2048), R("xtab", 0, 2048)
+    E, X = R("etab", PAD, PAD + 2048), R("xtab", PAD, PAD + 2048)
+    EP, XP = R("etab", 0, PAD + 2048), R("xtab", 0, PAD + 2048)
     EW, XW = R("etab", 0, WIN), R("xtab", 0, WIN)
     for t in range(STEPS):
         last = t == STEPS - 1
         cl, la, vt, lt, vp, lv = [a + str(t) for a in ("cl", "la", "vt", "lt", "vp", "lv")]
-        PL = R(vp, 128, 136)
-        begun = set()
+        terms = [0] * 4
+
+        def term(m, l, r):
+            mm(R("y%d" % (m // 2), 16 * (m % 2), 512, 2), l, r, terms[m // 2] == 0, terms[m // 2] == 3)
+            terms[m // 2] += 1
+
+        def midst(o, lo, hi, turned=False, less=None):
+            for b in ("mx", "mn"):
+                ends = R(b, 16 * lo + 15, 16 * hi, 16)
+                mm(o, *((ends, R("eye", *C)) if turned else (R("eye", *C), ends)), b == "mx")
+            rounded(o, 0, less is None)
+            if less:
+                mm(o, *((less, R("neyeb", *C)) if turned else (R("neyeb", *C), less)), False, True)
         for word in READ + (LAST if last else JUDGE):
             name, lo, hi = (word.split() + [0, 0])[:3]
             lo, hi = int(lo), int(hi)
             k = (16 * lo, 16 * hi)
-            if name == "vD":
+            rows, cols = (32 * lo, 32 * hi), (2 * lo, 2 * hi)
+            if name in ONCE:
+                if t == 0:
+                    ONCE[name]()
+            elif name == "vD":
                 ts(R("dg", *k), I(E, R("lst", lo, hi)), -float(MID), A.add)
             elif name == "sD":
                 act(R("dg", *k), I(E, R("lst", lo, hi)), bias=-float(MID))
             elif name == "arrived":
                 if t:
                     cp(I(XW, R("of", 0, 8)), R("lv%d" % (t - 1), *C))
-                else:
-                    rest()
             elif name == "sub":
                 mm(R("y%d" % lo, 0, 512), R("eye", *C), R("dg", *banks[lo]), False, True)
-            elif name == "abs":
-                act(R("ya", *banks[lo]), R("y%d" % lo, 0, 512), AF.Abs, bias=float(MID + 4095 * 2044))
-            elif name == "near":
-                scan(R("sc", *k), R("rmin", 0, k[1] - k[0]), R("ya", *k), A.max, A.min)
+            elif name == "least":
+                fold(R("ds", 32 * lo, 32 * lo + 32), R("y%d" % lo, 0, 512), A.min, True)
             elif name == "need":
-                mm(R("pU", 256 + lo, 256 + hi), R("eye", *C), R("K", lo, hi), True, False)
-                mm(R("pU", 256 + lo, 256 + hi), R("neye", *C), R("sc", k[0] + 15, k[1], 16), False, True)
+                o = R("pA", 128 + lo, 128 + hi)
+                mm(o, R("KT", *C), R("eye", lo, hi), True)
+                plus(o, "1", "2045", 1)
+                mm(o, R("neye", *C), R("ds", lo, hi), False, True)
             elif name == "raise":
-                tt(R(cl, lo, hi), R("pU", 256 + lo, 256 + hi), R("lst", lo, hi), A.max)
+                tt(R(cl, lo, hi), R("pA", 128 + lo, 128 + hi), R("lst", lo, hi), A.max)
             elif name == "send":
                 send(t, cl, la)
+            elif name == "wide":
+                if not last:
+                    recast(R("ch", *C), R(cl, *C))
+            elif name == "keyed":
+                if not last:
+                    o = R("pB", 128, 256)
+                    mm(o, R("KT", *C), R("p4096", *C), True)
+                    mm(o, R("KT", *C), R("neye", *C))
+                    plus(o, "1", "341.25", 12)
+                    mm(o, R("eye", *C), R("ch", *C), False, True)
             elif name == "code":
-                if last:
-                    fill(R("spare", 8, 16), (SPARE - 1024) / 128)
-                else:
-                    tt(R("F", *C), R(cl, *C), R("pW", 256, 384), A.add)
-            elif name == "order":
-                if last:
-                    ts(R("zf", *C), R("zi", *C), 128.0, A.add)
-                    store(0, T.yz[:], R("zf", *C))
-                    fill(R("bb", 128, 384), 0.0)
-                else:
-                    cp(R(vp, 136, 264), I(R("F", *C), TOM))
+                if not last:
+                    act(R(vp, 136, 264), R("pB", 128, 256))
             elif name == "vX":
                 ts(R("xh", *k), I(X if t else R("xi", 0, 2048), R(cl, lo, hi)), 0.5, A.mult, -64.125, A.add)
             elif name == "sX":
@@ -363,116 +412,130 @@ def rank_program(g, core, T, topo):
                 scan(R("mx", *k), R("rmax", 0, k[1] - k[0]), R("xh", *k), A.min, A.max)
             elif name == "min":
                 scan(R("mn", *k), R("rmin", 0, k[1] - k[0]), R("xh", *k), A.max, A.min)
-            elif name == "sums":
-                if t == 0:
-                    mm(R("pW", *C), R("eyeb", *C), R("w", *C), True, True)
-                    mm(R("pW", 128, 256), R("eyeb", *C), R("y", *C), True, False)
-                    mm(R("pW", 128, 256), R("eyeb", *C), R("m128", *C), False, True)
-            elif name == "late":
-                if t == 0:
-                    late()
             elif name == "z":
                 tt(R("zi", lo, hi), R("mx", k[0] + 15, k[1], 16), R("mn", k[0] + 15, k[1], 16), A.add)
             elif name == "wz":
                 tt(R("wz", lo, hi), R("zi", lo, hi), R("pW", lo, hi), A.mult)
-            elif name == "rows":
-                if lo == 0:
-                    mm(R("pU", 0, 8), R("eye", *C), R("base", 0, 8), True, False)
-                for sign in (0, 144):
-                    for n in range(lo // 8, hi // 8):
-                        a = sign + 15 - row(n)
-                        mm(R("pU", 0, 8), R("sel", a, a + 128), R("wz", 8 * n, 8 * n + 8), False, sign > 0 and n == 15)
-                    for m in ("p4096", "n4096") if sign == 0 else ():
-                        mm(R("pU", 0, 8), R(m, *C), R("rnd", 8, 16) if lo else R("rnd", 0, 8), False, False)
             elif name == "dv":
                 tt(R("dv", lo, hi), R("zi", lo, hi), R("pW", 128 + lo, 128 + hi), A.subtract)
             elif name == "turn":
                 mm(R("pT", 0, 128, 1, (lo, hi)), R("dv", lo, hi), R("eyeb", *C), True, True)
             elif name == "turned":
-                h = str(int(lo > 0))
-                act(R(vt + h, *C), R("pT", *C), AF.Abs, scale=2.0 ** -12)
-                send(t, vt + h, lt + h)
+                act(R(vt + "b", *C), R("pT", *C), AF.Abs, scale=2.0 ** -12)
+                send(t, vt + "b", lt + "b")
             elif name == "values":
-                act(R(vp, *C), I(R("dv", *C), TOM), AF.Abs)
+                act(R(vp, lo, hi), R("dv", lo, hi), AF.Abs)
+            elif name == "zs":
+                act(R("zf", lo, hi), R("zi", lo, hi), bias=128.0)
+            elif name == "zout":
+                store(T.yz[:], R("zf", *C))
+            elif name == "pz":
+                midst(R("pA", lo, hi), lo, hi)
+            elif name == "pwz":
+                tt(R("wz", lo, hi), R("pA", lo, hi), R("w", lo, hi), A.mult)
+            elif name == "pzs":
+                act(R("zf", lo, hi), R("pA", lo, hi), bias=128.0)
+            elif name == "pturn":
+                midst(R("pT", 0, 128, 1, (lo, hi)), lo, hi, True, R("y", lo, hi))
+            elif name == "pturned":
+                act(R(vt + "a", *C), R("pT", *C), AF.Abs, scale=2.0 ** -12, bias=2.0 ** -5)
+                send(t, vt + "a", lt + "a")
+            elif name == "pdv":
+                midst(R("pB", 384 + lo, 384 + hi), lo, hi, False, R("y", lo, hi))
+            elif name == "pvalues":
+                act(R(vp, lo, hi), R("pB", 384 + lo, 384 + hi), AF.Abs, bias=128.0)
+            elif name == "rows":
+                o = R("y3" if lo else "y2", lo, hi)
+                mm(o, R("rep", 0, 128, 1, ROWS), R("first", lo, hi, 1, ROWS), True)
+                plus(o, "1", "3/8", 20)
+                mm(o, R("nblk", *C), R("wz", lo, hi))
+                rounded(o, 4)
+                mm(o, R("blk", *C), R("wz", lo, hi), False, True)
             elif name == "place":
-                ts(PL, R("pU", 0, 8), 1024.0, A.add)
+                fold(R(vp, 128 + lo // 16, 128 + hi // 16), R("y3" if lo else "y2", lo, hi), A.max)
             elif name == "give":
                 send(t, vp, lv)
             elif name == "own":
-                cp(I(X, PL), R(vp, *C))
+                cp(I(XP, R(vp, 128 + lo // 16, 128 + hi // 16)), R(vp, lo, hi))
             elif name == "names":
-                if not last:
-                    cp(I(E, PL), R(vp, 136, 264))
+                cp(I(EP, R(vp, 128, 136)), R(vp, 136, 264))
             elif name == "whole":
-                mm(R("pM", *C), R("blk128", *C), R("w", *C), True, False)
-                mm(R("pM", *C), R("blk", *C), R("wz", *C), False, True)
-            elif name == "factor":
-                if t == 0:
-                    tt(R("dk", *C), R("eye", *C), R("pM", 256, 384), A.mult)
-            elif name == "quot":
-                act(R("qf", *C), R("pM", *C), scale=2.0 ** -12, bias=1025.0 - 2047.5 / 4096)
-                mm(R("pM", 128, 256), R("blk128", *C), R("w", *C), True, False)
-                mm(R("pM", 128, 256), R("blk", *C), R("wz", *C), False, False)
-                mm(R("pM", 128, 256), R("n4096", *C), R("qf", *C), False, True)
+                o = R("pB", *C)
+                mm(o, R("nblk", *C), R("wA", *C), True)
+                mm(o, R("nblk", *C), R("wz", *C))
+                rounded(o, 12)
+                mm(o, R("blk", *C), R("wA", *C))
+                mm(o, R("blk", *C), R("wz", *C), False, True)
+            elif name == "square":
+                act(R("sq", *C), R("pB", *C), AF.Square)
             elif name == "rem":
-                act(R("umh", *C), R("pM", 128, 256), bias=4096.0 * 1025 - 2048)
-                act(R("sq", *C), R("pM", 128, 256), AF.Square, bias=4096.0 * 1025)
-                mm(R("pM", 256, 384), R("dodd", *C), R("dv", *C), True, False)
-                mm(R("pM", 256, 384), R("dodd", *C), R("y", *C), False, False)
-                mm(R("pM", 256, 384), R("dk", *C), R("umh", *C), False, True)
-                spare(0)
+                act(R("umh", *C), R("pB", *C))
+            elif name == "lin":
+                o = R("pB", 128, 256)
+                mm(o, R("dodd", *C), R("zf", *C), True)
+                mm(o, R("dk", *C), R("umh", *C), False, True)
             elif name == "floor":
+                act(R("q5", *C), R("sq", *C), scale=2.0 ** -5, bias=-0.375)
+            elif name == "vfloor":
                 ts(R("q5", *C), R("sq", *C), 2.0 ** -5, A.mult, -0.375, A.add)
             elif name == "next":
-                tt(R("r2", *C), R("q5", *C), R("pM", 256, 384), A.add)
+                tt(R("r2", *C), R("q5", *C), R("pB", 128, 256), A.add)
+            elif name == "swide":
+                act(R("ch", *C), R("cN", *C))
+            elif name == "gwide":
+                recast(R("ch", *C), R("cN", *C))
+            elif name == "list":
+                recast(R("lst", *C), R("cN", *C))
             elif name == "mask":
                 ts(R("cN", *C), R("r2", *C), 2047, A.bitwise_and)
                 if last:
                     recast(R("ycb", *C), R("cN", *C))
-                    store(1, T.yc[:], R("ycb", *C))
-                else:
-                    ts(R("kc", *C), R("r2", *C), 3, A.bitwise_and)
-            elif name == "keys":
-                keys()
+                    store(T.yc[:], R("ycb", *C))
+            elif name == "key":
+                key()
+            elif name == "keep":
+                keep()
+            elif name == "bounds":
+                bounds(lo, hi)
             elif name == "vA":
                 cp(R("xa", *k), I(X, R(la, lo, hi)))
             elif name == "sA":
                 act(R("xa", *k), I(X, R(la, lo, hi)))
             elif name == "x":
-                mm(R("y%d" % lo, 0, 512), R("eyeb", *C), R("xa", *banks[lo]), lo not in begun, lo in begun)
-                begun.add(lo)
+                for m in (2 * lo, 2 * lo + 1):
+                    term(m, R("eyeb", *C), R("xa", 256 * m, 256 * m + 256))
             elif name == "v":
-                rows = (32 * lo, 32 * lo + 32)
-                mm(R("y%d" % lo, 0, 512), R(lt + str(int(rows[0] >= EARLY)), 0, 128, 1, rows), R("exn", 0, 512, 1, rows), lo not in begun, lo in begun)
-                begun.add(lo)
+                part = (32 * lo, 32 * lo + 32)
+                for a in range(2):
+                    term(2 * lo + a, R(lt + "ab"[part[0] >= EARLY], 0, 128, 1, part), R("exn", 256 * a, 256 * a + 256, 1, part))
             elif name == "size":
                 act(R("ad", *banks[lo]), R("y%d" % lo, 0, 512), AF.Abs)
+            elif name == "vsize":
+                op("v", lambda: g.vector.tensor_reduce(ap(R("ad", *banks[lo])), T["y%d" % lo][:], AxisListType.X, A.max, apply_absolute_value=True),
+                   [R("ad", *banks[lo])], [R("y%d" % lo, 0, 512)])
             elif name == "sum":
-                for j in range(4):
-                    a = 512 * lo + 128 * j
-                    mm(R("pT", 128 + row(4 * lo + j), 256, 16), R("ad", a, a + 128), R("indM", 0, 8), True, True)
-            elif name == "back":
-                ts(R("back", 0, 8), R(lv, 128, 136), -1024.0, A.add)
+                for q in range(4):
+                    mm(R("y%d" % lo, 0, 128, (4 * q, 4 * q + 4)), R("ad", 512 * lo + 128 * q, 512 * lo + 128 * q + 128), R("ind4", 0, 32), True, True)
+            elif name == "less":
+                tt(R("bb", 128 * lo, 128 * lo + 128), R("y%d" % lo, 0, 128), R("lim", *C), A.is_gt)
             elif name == "count":
-                b = 128 + 128 * lo
-                tt(R("bb", b + lo, b + 128, 2), R("pT", 128 + lo, 256, 2), R("lim", lo, 128, 2), A.is_gt)
-                mm(R("pU", 128 + 8 * lo, 136 + 8 * lo), R("bb", b, b + 128), R("indM", 0, 8), False, True)
-                if lo == 0:
-                    spare(1)
+                o = R("pA", 256 + 2 * lo, 258 + 2 * lo)
+                mm(o, R("eye", *C), R("spare", 8 * last + 2 * lo, 8 * last + 2 * lo + 2), True)
+                mm(o, R("bb", 128 * lo, 128 * lo + 128), R("ind2", 0, 2), False, True)
+            elif name == "back":
+                tt(R("back", 0, 8), R(lv, 128, 136), R("shift", 0, 8), A.subtract)
             elif name == "let":
-                tt(R("of", 8 + 8 * lo, 16 + 8 * lo), R("pU", 128 + 8 * lo, 136 + 8 * lo), R("back", 0, 8) if lo else R(lv, 128, 136), A.max)
+                tt(R("of", *cols), R("pA", 256 + cols[0], 256 + cols[1]), R("back", *cols) if last else R(lv, 128 + cols[0], 128 + cols[1]), A.max)
+            elif name == "named":
+                cp(I(EW, R("of", *cols)), R(lv, 136 + rows[0], 136 + rows[1]))
             elif name == "write":
-                cp(I(R("xtab", 1024 * lo, 1024 * lo + WIN), R("of", 8 + 8 * lo, 16 + 8 * lo)), R(lv, *C))
-                store(2 + lo, T.yx[:, 1024 * lo:1024 * lo + 1024], R("xtab", 1024 * lo, 1024 * lo + 1024))
-        if not last:
-            tt(R("bb", *C), R("pT", 128, 256), R("lim", *C), A.is_gt)
-            mm(R("pU", 128, 136), R("bb", *C), R("indM", 0, 8), False, True)
-            turn()
-            tt(R("of", 0, 8), R("pU", 128, 136), R(lv, 128, 136), A.max)
-            cp(I(EW, R("of", 0, 8)), R(lv, 136, 264))
-            bounds()
+                a = PAD + 512 * lo
+                cp(I(R("xtab", a, a + WIN), R("of", *cols)), R(lv, *rows))
+                store(T.yx[:, 512 * lo:512 * hi], R("xtab", a, a + 512))
+            else:
+                raise ValueError(word)
     g.wait_ge(T.sem.loc, sent[0])
-    for k in range(4):
+    for k in range(stored[0]):
         g.sync.wait_ge(T.sem["out%d" % k], 16)
     for q in "vspg":
         if seen["y"].get(q, 0) < count[q]:

@@ -55,23 +55,24 @@ SEMAPHORES = ["qv", "qs", "qp", "qg", "loc"] + ["ld%d" % k for k in range(12)] +
     [a + str(k) for a in ("la", "lv") for k in range(STEPS)] + ["lt%d%s" % (k, h) for k in range(STEPS) for h in "ab"]
 NUM = {"1": 1.0, "3/8": 0.375, "341.25": 341.25, "2045": 2045.0, "2^8": 256.0, "2^15": 32768.0, "+": 49152.0, "-": -49152.0}
 
-LOADS = (0, 512, 1024, 1536, 2048)
-UNPACK = """iC, p, p16, -, +, pI, 341.25, eye, 1, 3/8, pF, PH, 2045, PG, 2^8, p4096, neye, value 0 32, eyeb, iA, first, iE, keys, table 0 32, ODD,
-    name 0 32, 2^15, exn, name 32 64, twice 0 32, value 32 64, twice 32 64, value 64 96, rep, table 64 96, coded 0 32, name 64 96, key,
-    twice 64 96, keep, coded 32 64, name 96 112, twice 96 112, name 112 128, coded 64 96, coded 96 112, twice 112 128, bounds 0 4,
-    value 96 128, coded 112 128, table 96 128, table 32 64""".split(",")
-READ = """mul, th, rhigh, vD 32 64, m128, along, dk, rlow, spare, sD 0 32, sub 0, arrived, blk, least 0, sD 64 96, sub 1, least 1, sub 2, lim,
-    need 0 32, sD 96 128, own4, raise 0 32, sub 3, need 32 64, least 2, rmax, rmin, raise 32 64, need 64 96, pW, least 3, raise 64 96,
-    need 96 128, nblk, sX 0 32, max 0 32, min 0 32, sX 32 64, raise 96 128, pT, max 32 64, min 32 64, neyeb, sX 64 96, max 64 96, min 64 96,
-    ind4, sX 96 128, pturn 0 96, pz 0 96, pdv 0 96, send, pturned, wide, dodd, min 96 128, max 96 128, pwz 0 96, z 96 128, rows 0 96,
-    wz 96 128, dv 96 128, PA, place 0 96, ind2, rows 96 128, turn 96 128, pvalues 0 96, wA, pzs 0 96, zs 96 128, values 96 128,
-    place 96 128, own 0 96, turned, own 96 128, whole, keyed, code, give""".split(",")
-JUDGE = """vA 0 16, sA 16 32, x 0, rem, square, vA 64 96, v 1, v 0, lin, x 2, sA 32 64, floor, size 0, x 1, v 2, vA 96 128, next, mask, gwide, list,
-    size 1, v 3, x 3, sum 0, vsize 2, names, sum 1, less 1, less 0, key, sum 2, size 3, sum 3, less 2, keep, less 3, count 1, count 0, count 2,
-    count 3, bounds 0 1, let 0 4, named 0 4, bounds 1 4""".split(",")
-LAST = """vA 0 16, sA 16 32, vA 32 64, sA 64 96, x 0, v 0, size 0, vA 96 128, v 1, x 1, v 2, x 2, sum 0, x 3, vsize 1, v 3, sum 1, less 0, back,
-    square, rem, less 1, count 0, let 0 1, zout, floor, size 2, size 3, sum 2, less 2, write 0 1, lin, count 1, next, let 1 2, sum 3, less 3,
-    write 1 2, count 2, count 3, mask, let 2 3, write 2 3, let 3 4, write 3 4""".split(",")
+LOADS = (0, 256, 768, 1280, 1792, 2048)
+UNPACK = """p16, iC, p, m128, pI, rlow, eye, rmin, pF, ODD, rhigh, PG, +, -, 2045, 2^8, 2^15, 1, 3/8, 341.25, name 0 16, iA, rmax, exn, eyeb, neye,
+    p4096, neyeb, keys, value 0 16, twice 0 16, blk, name 16 48, PH, coded 0 16, name 48 80, key, value 16 48, name 80 112, ind4, keep,
+    twice 16 48, value 48 80, twice 48 80, twice 80 112, name 112 128, coded 16 48, twice 112 128, value 112 128, mul, coded 48 80,
+    bounds 0 4, coded 80 112, coded 112 128, value 80 112, nblk, th, along, rep, iE, first, table 112 128, table 16 48, table 0 16,
+    table 48 80, table 80 112""".split(",")
+READ = """sD 0 16, arrived, vD 16 32, vD 32 64, sD 64 96, sub 0, sub 1, sub 2, least 0, least 1, need 0 32, PA, raise 0 32, least 2, sD 96 128,
+    sub 3, need 32 64, need 64 96, raise 32 64, least 3, sX 0 32, raise 64 96, min 0 32, vX 32 40, need 96 128, raise 96 128, sX 40 64,
+    sX 64 96, max 0 32, min 32 64, max 32 64, sX 96 112, pT, max 64 96, min 64 96, pW, pz 0 64, pdv 0 64, pturn 0 96, min 96 112, pwz 0 64,
+    max 96 112, sX 112 128, max 112 128, min 112 128, dk, z 64 128, rows 0 64, place 0 64, send, wide, wA, pvalues 0 64, pturned, keyed,
+    wz 64 128, rows 64 128, code, dv 64 128, ind2, own 0 64, values 64 128, zs 64 128, pzs 0 64, place 64 128, dodd, own 64 128, spare,
+    turn 96 128, turned, lim, ahead, whole, give, own4""".split(",")
+JUDGE = """vA 0 16, square, rem, sA 16 32, lin, x 0, sA 48 64, sA 64 96, vA 32 48, vfloor, vA 96 128, next, names, x 1, v 0, v 1, v 2, x 2, size 0,
+    size 1, x 3, v 3, sum 0, sum 1, mask, vsize 2, less 0, gwide, list, less 1, size 3, sum 2, less 2, count 0, sum 3, count 1, count 2, less 3,
+    let 0 3, named 0 3, key, count 3, keep, let 3 4, named 3 4, bounds 0 4""".split(",")
+LAST = """vA 0 32, rem, square, sA 32 64, lin, x 0, x 1, sA 96 128, vfloor, vA 64 96, next, v 0, size 0, v 1, v 2, x 2, zout, mask, vsize 1, size 2,
+    v 3, sum 0, x 3, sum 1, less 0, back 0 4, less 1, count 0, sum 2, size 3, let 0 1, count 1, less 2, write 0 1, out 0 1, let 1 2, sum 3,
+    count 2, write 1 2, out 1 2, less 3, let 2 3, count 3, write 2 3, out 2 3, let 3 4, write 3 4, out 3 4""".split(",")
 
 
 def R(name, lo, hi, st=1, p=None):
@@ -289,7 +290,7 @@ def rank_program(g, core, T, topo):
                        mm(R("pW", 128, 256), R("eyeb", *C), R("m128", *C), False, True)),
     }
     for j, n in enumerate(NUM):
-        ONCE[n] = (lambda j, n: lambda: fill(R("num", 128 * j, 128 * j + 128), NUM[n]))(j, n)
+        ONCE[n] = (lambda j, n: lambda: act(R("num", 128 * j, 128 * j + 128), R("m128", *C), scale=NUM[n] / -128))(j, n)
 
     def key():
         o = R("pB", 256, 384)
@@ -352,6 +353,9 @@ def rank_program(g, core, T, topo):
         cl, la, vt, lt, vp, lv = [a + str(t) for a in ("cl", "la", "vt", "lt", "vp", "lv")]
         terms = [0] * 4
 
+        def places(b, lo, hi):
+            return R(b, 128 + lo // 16, 128 + hi // 16)
+
         def term(m, l, r):
             mm(R("y%d" % (m // 2), 16 * (m % 2), 512, 2), l, r, terms[m // 2] == 0, terms[m // 2] == 3)
             terms[m // 2] += 1
@@ -368,6 +372,7 @@ def rank_program(g, core, T, topo):
             lo, hi = int(lo), int(hi)
             k = (16 * lo, 16 * hi)
             rows, cols = (32 * lo, 32 * hi), (2 * lo, 2 * hi)
+            counts = "pT" if lo == 3 or last and lo == 1 else "pA"
             if name in ONCE:
                 if t == 0:
                     ONCE[name]()
@@ -383,12 +388,12 @@ def rank_program(g, core, T, topo):
             elif name == "least":
                 fold(R("ds", 32 * lo, 32 * lo + 32), R("y%d" % lo, 0, 512), A.min, True)
             elif name == "need":
-                o = R("pA", 128 + lo, 128 + hi)
+                o = R(("pA", "pT")[lo // 32 % 2], 128 + lo, 128 + hi)
                 mm(o, R("KT", *C), R("eye", lo, hi), True)
                 plus(o, "1", "2045", 1)
                 mm(o, R("neye", *C), R("ds", lo, hi), False, True)
             elif name == "raise":
-                tt(R(cl, lo, hi), R("pA", 128 + lo, 128 + hi), R("lst", lo, hi), A.max)
+                tt(R(cl, lo, hi), R(("pA", "pT")[lo // 32 % 2], 128 + lo, 128 + hi), R("lst", lo, hi), A.max)
             elif name == "send":
                 send(t, cl, la)
             elif name == "wide":
@@ -445,18 +450,22 @@ def rank_program(g, core, T, topo):
             elif name == "pvalues":
                 act(R(vp, lo, hi), R("pB", 384 + lo, 384 + hi), AF.Abs, bias=128.0)
             elif name == "rows":
-                o = R("y3" if lo else "y2", lo, hi)
+                o = R("y%d" % (hi // 32 - 1), lo, hi)
                 mm(o, R("rep", 0, 128, 1, ROWS), R("first", lo, hi, 1, ROWS), True)
                 plus(o, "1", "3/8", 20)
                 mm(o, R("nblk", *C), R("wz", lo, hi))
                 rounded(o, 4)
                 mm(o, R("blk", *C), R("wz", lo, hi), False, True)
             elif name == "place":
-                fold(R(vp, 128 + lo // 16, 128 + hi // 16), R("y3" if lo else "y2", lo, hi), A.max)
+                fold(places(vp, lo, hi), R("y%d" % (hi // 32 - 1), lo, hi), A.max)
             elif name == "give":
-                send(t, vp, lv)
+                if not last:
+                    send(t, vp, lv)
+            elif name == "ahead":
+                if last:
+                    send(t, vp, lv)
             elif name == "own":
-                cp(I(XP, R(vp, 128 + lo // 16, 128 + hi // 16)), R(vp, lo, hi))
+                cp(I(XP, places(vp, lo, hi)), R(vp, lo, hi))
             elif name == "names":
                 cp(I(EP, R(vp, 128, 136)), R(vp, 136, 264))
             elif name == "whole":
@@ -471,7 +480,7 @@ def rank_program(g, core, T, topo):
             elif name == "rem":
                 act(R("umh", *C), R("pB", *C))
             elif name == "lin":
-                o = R("pB", 128, 256)
+                o = R("pW", 256, 384)
                 mm(o, R("dodd", *C), R("zf", *C), True)
                 mm(o, R("dk", *C), R("umh", *C), False, True)
             elif name == "floor":
@@ -479,7 +488,7 @@ def rank_program(g, core, T, topo):
             elif name == "vfloor":
                 ts(R("q5", *C), R("sq", *C), 2.0 ** -5, A.mult, -0.375, A.add)
             elif name == "next":
-                tt(R("r2", *C), R("q5", *C), R("pB", 128, 256), A.add)
+                tt(R("r2", *C), R("q5", *C), R("pW", 256, 384), A.add)
             elif name == "swide":
                 act(R("ch", *C), R("cN", *C))
             elif name == "gwide":
@@ -519,19 +528,20 @@ def rank_program(g, core, T, topo):
             elif name == "less":
                 tt(R("bb", 128 * lo, 128 * lo + 128), R("y%d" % lo, 0, 128), R("lim", *C), A.is_gt)
             elif name == "count":
-                o = R("pA", 256 + 2 * lo, 258 + 2 * lo)
+                o = R(counts, 256 + 2 * lo, 258 + 2 * lo)
                 mm(o, R("eye", *C), R("spare", 8 * last + 2 * lo, 8 * last + 2 * lo + 2), True)
                 mm(o, R("bb", 128 * lo, 128 * lo + 128), R("ind2", 0, 2), False, True)
             elif name == "back":
-                tt(R("back", 0, 8), R(lv, 128, 136), R("shift", 0, 8), A.subtract)
+                tt(R("back", *cols), places(lv, *rows), R("shift", *cols), A.subtract)
             elif name == "let":
-                tt(R("of", *cols), R("pA", 256 + cols[0], 256 + cols[1]), R("back", *cols) if last else R(lv, 128 + cols[0], 128 + cols[1]), A.max)
+                tt(R("of", *cols), R(counts, 256 + cols[0], 256 + cols[1]), R("back", *cols) if last else places(lv, *rows), A.max)
             elif name == "named":
                 cp(I(EW, R("of", *cols)), R(lv, 136 + rows[0], 136 + rows[1]))
             elif name == "write":
                 a = PAD + 512 * lo
                 cp(I(R("xtab", a, a + WIN), R("of", *cols)), R(lv, *rows))
-                store(T.yx[:, 512 * lo:512 * hi], R("xtab", a, a + 512))
+            elif name == "out":
+                store(T.yx[:, 512 * lo:512 * hi], R("xtab", PAD + 512 * lo, PAD + 512 * hi))
             else:
                 raise ValueError(word)
     g.wait_ge(T.sem.loc, sent[0])

from concourse.mybir import AluOpType, AxisListType, ActivationFunctionType as AF

STEPS = 3
EARLY = 96
MID = 6140
EDGE = 61440.0
FAR = 2048.0
PAD = 16
SPARE = PAD + 11 * 2048
WIN = SPARE + 2048


def _sb(w, d, run=None):
    return ("sbuf", [128, w] if run is None else [128, w // run, run], d)


def _ps():
    return ("psum", [128, 512], "float32")


RUNS = ("psum", [128, 32, 16, 1], "float32")
SCRATCH = {
    "rec0": _sb(2048, "int32"), "dI": _sb(2048, "int32"), "xi": _sb(2048, "int32"),
    "etab": _sb(WIN, "int32"), "xtab": _sb(WIN + 2048, "bfloat16"),
    "y": _sb(128, "bfloat16"), "w": _sb(128, "bfloat16"), "row": _sb(256, "int32"), "rowh": _sb(256, "float16"),
    "pI": _sb(32, "int32"), "pF": _sb(24, "float32"), "iA": _sb(512, "bfloat16"), "iC": _sb(128, "bfloat16"),
    "iE": _sb(40, "float32"), "exn": _sb(512, "float16"),
    "eye": _sb(128, "float16"), "neye": _sb(128, "float16"), "eyeb": _sb(128, "bfloat16"), "neyeb": _sb(128, "bfloat16"), "p4096": _sb(128, "float16"),
    "blk": _sb(128, "float16"), "nblk": _sb(128, "float16"), "rep": _sb(128, "float16"), "i16": _sb(128, "float32"), "first": _sb(128, "float16"),
    "num": _sb(1024, "float16"), "m128": _sb(128, "bfloat16"), "ind4": _sb(32, "bfloat16"), "ind2": _sb(2, "bfloat16"), "spare": _sb(16, "float16"), "shift": _sb(8, "float32"),
    "dk": _sb(128, "float16"), "dodd": _sb(128, "bfloat16"), "wA": _sb(128, "float16"),
    "lim": _sb(128, "float32"), "rmin": _sb(512, "float16"), "rmax": _sb(512, "float16"),
    "cN": _sb(128, "int32"), "lst": _sb(128, "uint16"), "ch": _sb(128, "float16"), "KT": _sb(128, "float16"),
    "dg": _sb(2048, "float16"), "ds": _sb(128, "float16"), "xh": _sb(2048, "float16"),
    "mx": _sb(2048, "float16"), "mn": _sb(2048, "float16"), "xa": _sb(2048, "bfloat16"), "ad": _sb(2048, "bfloat16", 16),
    "zi": _sb(128, "int32"), "wz": _sb(128, "float16"), "dv": _sb(128, "bfloat16"),
    "zf": _sb(128, "bfloat16"), "umh": _sb(128, "float16"), "sq": _sb(128, "float32"),
    "r2": _sb(128, "int32"), "q5": _sb(128, "int32"), "bb": _sb(512, "bfloat16"), "of": _sb(8, "uint16"), "back": _sb(8, "float32"), "ycb": _sb(128, "float32"),
    "y0": RUNS, "y1": RUNS, "y2": RUNS, "y3": RUNS,
    "pW": _ps(),
    "pA": _ps(),
    "pB": _ps(),
    "pT": _ps(),
}
for _t in range(STEPS):
    SCRATCH["cl%d" % _t] = _sb(128, "uint16")
    SCRATCH["la%d" % _t] = _sb(128, "uint16")
    for _h in "ab":
        SCRATCH["vt%d%s" % (_t, _h)] = _sb(128, "float16")
        SCRATCH["lt%d%s" % (_t, _h)] = _sb(128, "float16")
    SCRATCH["vp%d" % _t] = _sb(136 if _t == STEPS - 1 else 264, "uint16")
    SCRATCH["lv%d" % _t] = SCRATCH["vp%d" % _t]
PSUM = [k for k in SCRATCH if SCRATCH[k][0] == "psum"]
SEMAPHORES = ["qv", "qs", "qp", "qg", "loc"] + ["ld%d" % k for k in range(12)] + ["out%d" % k for k in range(6)] + \
    [a + str(k) for a in ("la", "lv") for k in range(STEPS)] + ["lt%d%s" % (k, h) for k in range(STEPS) for h in "ab"]
NUM = {"1": 1.0, "3/8": 0.375, "341.25": 341.25, "2045": 2045.0, "2^8": 256.0, "2^15": 32768.0, "+": 49152.0, "-": -49152.0}

LOADS = (0, 256, 768, 1280, 1792, 2048)
UNPACK = """p16, iC, p, m128, pI, rlow, eye, rmin, pF, ODD, rhigh, PG, +, -, 2045, 2^8, 2^15, 1, 3/8, 341.25, name 0 16, iA, rmax, exn, eyeb, neye,
    p4096, neyeb, keys, value 0 16, twice 0 16, blk, name 16 48, PH, coded 0 16, name 48 80, key, value 16 48, name 80 112, ind4, keep,
    twice 16 48, value 48 80, twice 48 80, twice 80 112, name 112 128, coded 16 48, twice 112 128, value 112 128, mul, coded 48 80,
    bounds 0 4, coded 80 112, coded 112 128, value 80 112, nblk, th, along, rep, iE, first, table 112 128, table 16 48, table 0 16,
    table 48 80, table 80 112""".split(",")
READ = """sD 0 16, arrived, vD 16 32, vD 32 64, sD 64 96, sub 0, sub 1, sub 2, least 0, least 1, need 0 32, PA, raise 0 32, least 2, sD 96 128,
    sub 3, need 32 64, need 64 96, raise 32 64, least 3, sX 0 32, raise 64 96, min 0 32, vX 32 40, need 96 128, raise 96 128, sX 40 64,
    sX 64 96, max 0 32, min 32 64, max 32 64, sX 96 112, pT, max 64 96, min 64 96, pW, pz 0 64, pdv 0 64, pturn 0 96, min 96 112, pwz 0 64,
    max 96 112, sX 112 128, max 112 128, min 112 128, dk, z 64 128, rows 0 64, place 0 64, send, wide, wA, pvalues 0 64, pturned, keyed,
    wz 64 128, rows 64 128, code, dv 64 128, ind2, own 0 64, values 64 128, zs 64 128, pzs 0 64, place 64 128, dodd, own 64 128, spare,
    turn 96 128, turned, lim, ahead, whole, give, own4""".split(",")
JUDGE = """vA 0 16, square, rem, sA 16 32, lin, x 0, sA 48 64, sA 64 96, vA 32 48, vfloor, vA 96 128, next, names, x 1, v 0, v 1, v 2, x 2, size 0,
    size 1, x 3, v 3, sum 0, sum 1, mask, vsize 2, less 0, gwide, list, less 1, size 3, sum 2, less 2, count 0, sum 3, count 1, count 2, less 3,
    let 0 3, named 0 3, key, count 3, keep, let 3 4, named 3 4, bounds 0 4""".split(",")
LAST = """vA 0 32, rem, square, sA 32 64, lin, x 0, x 1, sA 96 128, vfloor, vA 64 96, next, v 0, size 0, v 1, v 2, x 2, zout, mask, vsize 1, size 2,
    v 3, sum 0, x 3, sum 1, less 0, back 0 4, less 1, count 0, sum 2, size 3, let 0 1, count 1, less 2, write 0 1, out 0 1, let 1 2, sum 3,
    count 2, write 1 2, out 1 2, less 3, let 2 3, count 3, write 2 3, out 2 3, let 3 4, write 3 4, out 3 4""".split(",")


def R(name, lo, hi, st=1, p=None):
    return (name, lo, hi, st, p)


def I(win, off):
    return ("indirect", win, off)


def rank_program(g, core, T, topo):
    rank = T.rank_of(core)
    if rank is None:
        return
    A = AluOpType
    N = len(T.cores)
    queues = {"v": g.vector, "s": g.scalar, "p": g.tensor, "g": g, "y": g.sync}
    count = {q: 0 for q in "vspg"}
    seen = {q: {} for q in queues}
    clock = {}
    last_w, last_r = {}, {}
    target = {}
    for q in "vspg":
        target[q] = (lambda s: lambda n: (s, n))(T.sem["q" + q])

    def flat(x):
        return [x[1], x[2]] if x[0] == "indirect" else [x]

    def ap(x):
        if x[0] == "indirect":
            return ap(x[1]).indirect(ap(x[2]))
        name, lo, hi, st, p = x
        rows = slice(None) if p is None else slice(*p)
        if len(SCRATCH[name][1]) == 4:
            return T[name][:, lo // 16:hi // 16:st, :, 0] if isinstance(st, int) else T[name][:, lo // 16:hi // 16, st[0]:st[1], 0]
        if len(SCRATCH[name][1]) == 3:
            return T[name][:, lo // 16:hi // 16, :]
        return T[name][rows, lo:hi] if st == 1 else T[name][rows, lo:hi:st]

    def need(q, reads, writes):
        want = {}

        def add(src, n):
            want[src] = max(want.get(src, 0), n)
        for (b, lo, hi, _s, _p), wr in [(r, False) for r in reads] + [(w, True) for w in writes]:
            ps = b in PSUM
            for (l, h, src, n) in last_w.get(b, []):
                if ((ps and src != q) or (l < hi and lo < h)) and not (ps and q == "p" and src == "p"):
                    add(src, n)
            for (l, h, src, n) in last_r.get(b, []):
                if src != q and (ps or (wr and l < hi and lo < h)):
                    add(src, n)
        while want:
            src = max(want, key=lambda s: (s in "vspg", want[s]))
            n = want.pop(src)
            if seen[q].get(src, 0) >= n:
                continue
            sem, val = target[src](n)
            queues[q].wait_ge(sem, val)
            seen[q][src] = n
            for k, m in clock.get((src, n), {}).items():
                if seen[q].get(k, 0) < m:
                    seen[q][k] = m

    def record(src, n, reads, writes):
        for (b, lo, hi, st, p) in writes:
            whole = st == 1 and p is None
            keep = [e for e in last_w.get(b, []) if not (lo <= e[0] and e[1] <= hi and (e[2] == src or (whole and b not in PSUM)))]
            last_w[b] = keep + [(lo, hi, src, n)]
            if whole and b not in PSUM:
                last_r[b] = [e for e in last_r.get(b, []) if not (lo <= e[0] and e[1] <= hi)]
        for (b, lo, hi, _s, _p) in reads:
            keep = [e for e in last_r.get(b, []) if not (lo <= e[0] and e[1] <= hi and e[2] == src)]
            last_r[b] = keep + [(lo, hi, src, n)]

    def op(q, call, outs, ins):
        reads = [r for x in ins if isinstance(x, tuple) for r in flat(x)]
        writes = []
        for x in outs:
            writes.append(flat(x)[0])
            reads += flat(x)[1:]
        if q == "g":
            if (writes[0][4] or ONE)[0]:
                reads.append(R("any call", 0, 1))
                writes.append(R("lone call", 0, 1))
            else:
                reads.append(R("lone call", 0, 1))
        need(q, reads, writes)
        if q == "g":
            writes.append(R("any call", 0, 1))
        i = call()
        count[q] += 1
        i.then_inc(T.sem["q" + q], 1)
        clock[(q, count[q])] = dict(seen[q])
        record(q, count[q], reads, writes)

    def event(name, sem, val, writes):
        target[name] = lambda n: (sem, val)
        record(name, 1, [], writes)

    def val(x):
        return ap(x) if isinstance(x, tuple) else x

    def cp(o, i):
        op("v", lambda: g.vector.tensor_copy(ap(o), ap(i)), [o], [i])

    def tt(o, a, b, f):
        op("v", lambda: g.vector.tensor_tensor(ap(o), ap(a), ap(b), f), [o], [a, b])

    def ts(o, a, s1, f1, s2=None, f2=None):
        more = () if f2 is None else (f2,)
        op("v", lambda: g.vector.tensor_scalar(ap(o), ap(a), val(s1), val(s2), f1, *more), [o], [a, s1, s2])

    def scan(o, a, b, f0, f1):
        op("v", lambda: g.vector.tensor_tensor_scan(ap(o), ap(a), ap(b), 0.0, f0, f1), [o], [a, b])

    def fold(o, i, f, size=False):
        op("v", lambda: g.vector.tensor_reduce(ap(o), ap(i), AxisListType.X, f, apply_absolute_value=size), [o], [i])

    def fill(o, c):
        op("v", lambda: g.vector.memset(ap(o), c), [o], [])

    def act(o, i, f=AF.Identity, bias=0.0, scale=1.0):
        op("s", lambda: g.scalar.activation(ap(o), ap(i), f, bias=bias, scale=scale), [o], [i])

    def mm(o, l, r, start=False, stop=False):
        op("p", lambda: g.tensor.matmul(ap(o), ap(l), ap(r), start, stop), [o], [l, r])

    def plus(o, a, b, k, start=False, stop=False):
        at = {n: 128 * j for j, n in enumerate(NUM)}
        m = 128 if o[4] is None else o[4][1] - o[4][0]
        mm(o, R("num", at[a], at[a] + m, 1, (0, k)), R("num", at[b], at[b] + o[2] - o[1], 1, (0, k)), start, stop)

    def rounded(o, bits, stop=False):
        for sign in "+-":
            plus(o, "2^8" if bits < 7 else "2^15", sign, 2 ** bits if bits < 7 else 2 ** (bits - 7), False, stop and sign == "-")

    def iota(o, pat, first=0, cm=0):
        op("g", lambda: g.iota(ap(o), pat, first, cm, allow_small_or_imprecise_dtypes=True), [o], [])

    def select(o, i, pat, cm=0, first=0, other=0.0):
        op("g", lambda: g.affine_select(ap(o), ap(i), pat, A.is_equal, other, first, cm), [o], [i])

    def recast(o, i):
        select(o, i, [[0, o[2] - o[1]]])

    nload = [0]

    def load(q, out, src):
        sem = T.sem["ld%d" % nload[0]]
        queues[q].dma_start(ap(out), src).then_inc(sem, 16)
        event("ld%d" % nload[0], sem, 16, [out])
        nload[0] += 1
    C = (0, 128)
    ONE = (0, 1)
    banks = [(512 * b, 512 * b + 512) for b in range(4)]
    load("s", R("cN", *C), T.req[:])
    for k in zip(LOADS, LOADS[1:]):
        load("y", R("rec0", *k), T.rec[:, k[0]:k[1]])
    load("s", R("row", 0, 128, 1, ONE), T.mul[:])
    load("s", R("row", 128, 256, 1, ONE), T.th[:])
    load("y", R("w", *C), T.wt[:])
    load("y", R("y", *C), T.aim[:])

    def keys():
        recast(R("ch", *C), R("cN", *C))
        recast(R("lst", *C), R("cN", *C))

    P32, P16 = [R("pF", k, k + 1) for k in (0, 1)]
    P0, PG, ODD, PH, PA = [R("pF", k, k + 1) for k in range(16, 21)]
    ROWS = (0, 16)
    ONCE = {
        "p": lambda: iota(P0, [[0, 1]], 0, 1),
        "p16": lambda: (iota(R("pI", 0, 1), [[0, 1]], 0, 16), iota(R("pI", 1, 2), [[0, 1]], 0, 32)),
        "iC": lambda: iota(R("iC", *C), [[1, 128]]),
        "iA": lambda: iota(R("iA", 0, 512), [[16, 32], [0, 16]]),
        "pI": lambda: ts(R("pI", 16, 18), R("pI", 0, 2), 496, A.bitwise_and),
        "pF": lambda: cp(R("pF", 0, 2), R("pI", 16, 18)),
        "PG": lambda: ts(PG, P16, -1 / 32, A.mult, P0, A.add),
        "ODD": lambda: ts(ODD, P16, 0.0625, A.mult, 1.0, A.add),
        "PH": lambda: ts(PH, P16, 0.5, A.mult),
        "rlow": lambda: fill(R("rmin", 0, 512), -EDGE),
        "rmin": lambda: fill(R("rmin", 0, 512, 16), EDGE),
        "rhigh": lambda: fill(R("rmax", 0, 512), EDGE),
        "rmax": lambda: fill(R("rmax", 0, 512, 16), -EDGE),
        "m128": lambda: fill(R("m128", *C), -128.0),
        "pT": lambda: fill(R("pT", *C), 0.0),
        "eye": lambda: ts(R("eye", *C), R("iC", *C), P0, A.is_equal),
        "neye": lambda: act(R("neye", *C), R("eye", *C), scale=-1.0),
        "eyeb": lambda: act(R("eyeb", *C), R("eye", *C)),
        "neyeb": lambda: act(R("neyeb", *C), R("eye", *C), scale=-1.0),
        "p4096": lambda: act(R("p4096", *C), R("eye", *C), scale=4096.0),
        "exn": lambda: ts(R("exn", 0, 512), R("iA", 0, 512), P32, A.is_equal, -4096.0, A.mult),
        "blk": lambda: ts(R("blk", *C), R("iA", *C), PG, A.is_equal),
        "dodd": lambda: ts(R("dodd", *C), R("iC", *C), P0, A.is_equal, ODD, A.mult),
        "nblk": lambda: act(R("nblk", *C), R("blk", *C), scale=-1.0),
        "ind4": lambda: act(R("ind4", 0, 32), R("blk", 0, 128, 4), scale=-FAR),
        "PA": lambda: ts(PA, P32, 256.0, A.is_ge),
        "ind2": lambda: ts(R("ind2", 0, 2), R("iC", 0, 2), PA, A.is_equal, -FAR, A.mult),
        "own4": lambda: [select(R("lim", 0, 128, 1, (32 * k, 32 * k + 32)), R("lim", 0, 128, 1, (32 * k, 32 * k + 32)), [[0, 32], [1, 4]], 0, -k, 1.0)
                         for k in range(4)],
        "rep": lambda: select(R("rep", 0, 128, 1, ROWS), R("num", 0, 128, 1, ROWS), [[0, 8], [1, 16]], -1),
        "first": lambda: (iota(R("i16", 0, 128, 1, ROWS), [[16, 128]], PAD),
                          select(R("first", 0, 128, 1, ROWS), R("i16", 0, 128, 1, ROWS), [[0, 8], [1, 16]], -1)),
        "iE": lambda: (iota(R("iE", 8, 16), [[256, 8]], SPARE), iota(R("iE", 16, 24), [[0, 4], [256, 2]], SPARE - PAD),
                       iota(R("shift", 0, 8), [[512, 4], [0, 2]], PAD)),
        "spare": lambda: ts(R("spare", 0, 16), R("iE", 8, 24), PH, A.add),
        "mul": lambda: act(R("rowh", 0, 128, 1, ONE), R("row", 0, 128, 1, ONE), bias=-1920.0),
        "th": lambda: act(R("rowh", 128, 256, 1, ONE), R("row", 128, 256, 1, ONE), bias=-2048.0),
        "along": lambda: mm(R("pA", 256, 512), R("num", 0, 128, 1, ONE), R("rowh", 0, 256, 1, ONE), True, True),
        "lim": lambda: act(R("lim", *C), R("pA", 384, 512), scale=-FAR, bias=-2048 * FAR),
        "dk": lambda: tt(R("dk", *C), R("eye", *C), R("pA", 256, 384), A.mult),
        "wA": lambda: act(R("wA", *C), R("w", *C), scale=128.0, bias=-128.0),
        "pW": lambda: (mm(R("pW", *C), R("eyeb", *C), R("w", *C), True, True), mm(R("pW", 128, 256), R("eyeb", *C), R("y", *C), True),
                       mm(R("pW", 128, 256), R("eyeb", *C), R("m128", *C), False, True)),
    }
    for j, n in enumerate(NUM):
        ONCE[n] = (lambda j, n: lambda: act(R("num", 128 * j, 128 * j + 128), R("m128", *C), scale=NUM[n] / -128))(j, n)

    def key():
        o = R("pB", 256, 384)
        mm(o, R("ch", *C), R("neye", *C), True)
        plus(o, "1", "3/8", 4)
        rounded(o, 2)
        mm(o, R("ch", *C), R("eye", *C), False, True)

    def keep():
        act(R("KT", *C), R("pB", 256, 384), bias=-1.0)

    def bounds(lo, hi):
        for b in range(lo, hi):
            rows = (32 * b, 32 * b + 32)
            mm(R("y%d" % b, 0, 512), R("KT", 0, 128, 1, rows), R("exn", 0, 512, 1, rows), True, False)

    for word in UNPACK:
        name, lo, hi = (word.split() + [0, 0])[:3]
        k = (16 * int(lo), 16 * int(hi))
        if name == "name":
            ts(R("dI", *k), R("rec0", *k), 2047, A.bitwise_and)
        elif name == "twice":
            act(R("dI", *k), R("dI", *k), scale=4097.0)
        elif name == "coded":
            ts(R("etab", PAD + k[0], PAD + k[1]), R("dI", *k), 14332, A.bitwise_and)
        elif name == "value":
            act(R("xi", *k), R("rec0", *k), scale=2.0 ** -11, bias=-1023.5 / 2048)
        elif name == "table":
            recast(R("xtab", PAD + k[0], PAD + k[1]), R("xi", *k))
        elif name == "bounds":
            bounds(int(lo), int(hi))
        else:
            dict(ONCE, keys=keys, key=key, keep=keep)[name]()

    sent = [0]
    stored = [0]

    def send(t, src, land):
        dst = T.cores[(rank + 1 + t % (N - 1)) % N]
        back = T.cores[(rank - 1 - t % (N - 1)) % N]
        rid, pid = topo.addr(dst, core)
        eng = topo.engines(core, dst)[:8]
        n = len(topo.engines(back, core)[:8])
        width = SCRATCH[src][1][1]
        need("g", [R(src, 0, width)], [])
        g.remote_dma(T[land][:], T[src][:], T.sem[land], T.sem.loc, pid, rid, sum(1 << e for e in eng))
        sent[0] += len(eng)
        event(land, T.sem[land], n, [R(land, 0, width)])

    def store(out, b):
        need("y", [b], [])
        g.sync.dma_start(out, ap(b)).then_inc(T.sem["out%d" % stored[0]], 16)
        stored[0] += 1

    E, X = R("etab", PAD, PAD + 2048), R("xtab", PAD, PAD + 2048)
    EP, XP = R("etab", 0, PAD + 2048), R("xtab", 0, PAD + 2048)
    EW, XW = R("etab", 0, WIN), R("xtab", 0, WIN)
    for t in range(STEPS):
        last = t == STEPS - 1
        cl, la, vt, lt, vp, lv = [a + str(t) for a in ("cl", "la", "vt", "lt", "vp", "lv")]
        terms = [0] * 4

        def places(b, lo, hi):
            return R(b, 128 + lo // 16, 128 + hi // 16)

        def term(m, l, r):
            mm(R("y%d" % (m // 2), 16 * (m % 2), 512, 2), l, r, terms[m // 2] == 0, terms[m // 2] == 3)
            terms[m // 2] += 1

        def midst(o, lo, hi, turned=False, less=None):
            for b in ("mx", "mn"):
                ends = R(b, 16 * lo + 15, 16 * hi, 16)
                mm(o, *((ends, R("eye", *C)) if turned else (R("eye", *C), ends)), b == "mx")
            rounded(o, 0, less is None)
            if less:
                mm(o, *((less, R("neyeb", *C)) if turned else (R("neyeb", *C), less)), False, True)
        for word in READ + (LAST if last else JUDGE):
            name, lo, hi = (word.split() + [0, 0])[:3]
            lo, hi = int(lo), int(hi)
            k = (16 * lo, 16 * hi)
            rows, cols = (32 * lo, 32 * hi), (2 * lo, 2 * hi)
            counts = "pT" if lo == 3 or last and lo == 1 else "pA"
            if name in ONCE:
                if t == 0:
                    ONCE[name]()
            elif name == "vD":
                ts(R("dg", *k), I(E, R("lst", lo, hi)), -float(MID), A.add)
            elif name == "sD":
                act(R("dg", *k), I(E, R("lst", lo, hi)), bias=-float(MID))
            elif name == "arrived":
                if t:
                    cp(I(XW, R("of", 0, 8)), R("lv%d" % (t - 1), *C))
            elif name == "sub":
                mm(R("y%d" % lo, 0, 512), R("eye", *C), R("dg", *banks[lo]), False, True)
            elif name == "least":
                fold(R("ds", 32 * lo, 32 * lo + 32), R("y%d" % lo, 0, 512), A.min, True)
            elif name == "need":
                o = R(("pA", "pT")[lo // 32 % 2], 128 + lo, 128 + hi)
                mm(o, R("KT", *C), R("eye", lo, hi), True)
                plus(o, "1", "2045", 1)
                mm(o, R("neye", *C), R("ds", lo, hi), False, True)
            elif name == "raise":
                tt(R(cl, lo, hi), R(("pA", "pT")[lo // 32 % 2], 128 + lo, 128 + hi), R("lst", lo, hi), A.max)
            elif name == "send":
                send(t, cl, la)
            elif name == "wide":
                if not last:
                    recast(R("ch", *C), R(cl, *C))
            elif name == "keyed":
                if not last:
                    o = R("pB", 128, 256)
                    mm(o, R("KT", *C), R("p4096", *C), True)
                    mm(o, R("KT", *C), R("neye", *C))
                    plus(o, "1", "341.25", 12)
                    mm(o, R("eye", *C), R("ch", *C), False, True)
            elif name == "code":
                if not last:
                    act(R(vp, 136, 264), R("pB", 128, 256))
            elif name == "vX":
                ts(R("xh", *k), I(X if t else R("xi", 0, 2048), R(cl, lo, hi)), 0.5, A.mult, -64.125, A.add)
            elif name == "sX":
                act(R("xh", *k), I(X if t else R("xi", 0, 2048), R(cl, lo, hi)), bias=-64.125, scale=0.5)
            elif name == "max":
                scan(R("mx", *k), R("rmax", 0, k[1] - k[0]), R("xh", *k), A.min, A.max)
            elif name == "min":
                scan(R("mn", *k), R("rmin", 0, k[1] - k[0]), R("xh", *k), A.max, A.min)
            elif name == "z":
                tt(R("zi", lo, hi), R("mx", k[0] + 15, k[1], 16), R("mn", k[0] + 15, k[1], 16), A.add)
            elif name == "wz":
                tt(R("wz", lo, hi), R("zi", lo, hi), R("pW", lo, hi), A.mult)
            elif name == "dv":
                tt(R("dv", lo, hi), R("zi", lo, hi), R("pW", 128 + lo, 128 + hi), A.subtract)
            elif name == "turn":
                mm(R("pT", 0, 128, 1, (lo, hi)), R("dv", lo, hi), R("eyeb", *C), True, True)
            elif name == "turned":
                act(R(vt + "b", *C), R("pT", *C), AF.Abs, scale=2.0 ** -12)
                send(t, vt + "b", lt + "b")
            elif name == "values":
                act(R(vp, lo, hi), R("dv", lo, hi), AF.Abs)
            elif name == "zs":
                act(R("zf", lo, hi), R("zi", lo, hi), bias=128.0)
            elif name == "zout":
                store(T.yz[:], R("zf", *C))
            elif name == "pz":
                midst(R("pA", lo, hi), lo, hi)
            elif name == "pwz":
                tt(R("wz", lo, hi), R("pA", lo, hi), R("w", lo, hi), A.mult)
            elif name == "pzs":
                act(R("zf", lo, hi), R("pA", lo, hi), bias=128.0)
            elif name == "pturn":
                midst(R("pT", 0, 128, 1, (lo, hi)), lo, hi, True, R("y", lo, hi))
            elif name == "pturned":
                act(R(vt + "a", *C), R("pT", *C), AF.Abs, scale=2.0 ** -12, bias=2.0 ** -5)
                send(t, vt + "a", lt + "a")
            elif name == "pdv":
                midst(R("pB", 384 + lo, 384 + hi), lo, hi, False, R("y", lo, hi))
            elif name == "pvalues":
                act(R(vp, lo, hi), R("pB", 384 + lo, 384 + hi), AF.Abs, bias=128.0)
            elif name == "rows":
                o = R("y%d" % (hi // 32 - 1), lo, hi)
                mm(o, R("rep", 0, 128, 1, ROWS), R("first", lo, hi, 1, ROWS), True)
                plus(o, "1", "3/8", 20)
                mm(o, R("nblk", *C), R("wz", lo, hi))
                rounded(o, 4)
                mm(o, R("blk", *C), R("wz", lo, hi), False, True)
            elif name == "place":
                fold(places(vp, lo, hi), R("y%d" % (hi // 32 - 1), lo, hi), A.max)
            elif name == "give":
                if not last:
                    send(t, vp, lv)
            elif name == "ahead":
                if last:
                    send(t, vp, lv)
            elif name == "own":
                cp(I(XP, places(vp, lo, hi)), R(vp, lo, hi))
            elif name == "names":
                cp(I(EP, R(vp, 128, 136)), R(vp, 136, 264))
            elif name == "whole":
                o = R("pB", *C)
                mm(o, R("nblk", *C), R("wA", *C), True)
                mm(o, R("nblk", *C), R("wz", *C))
                rounded(o, 12)
                mm(o, R("blk", *C), R("wA", *C))
                mm(o, R("blk", *C), R("wz", *C), False, True)
            elif name == "square":
                act(R("sq", *C), R("pB", *C), AF.Square)
            elif name == "rem":
                act(R("umh", *C), R("pB", *C))
            elif name == "lin":
                o = R("pW", 256, 384)
                mm(o, R("dodd", *C), R("zf", *C), True)
                mm(o, R("dk", *C), R("umh", *C), False, True)
            elif name == "floor":
                act(R("q5", *C), R("sq", *C), scale=2.0 ** -5, bias=-0.375)
            elif name == "vfloor":
                ts(R("q5", *C), R("sq", *C), 2.0 ** -5, A.mult, -0.375, A.add)
            elif name == "next":
                tt(R("r2", *C), R("q5", *C), R("pW", 256, 384), A.add)
            elif name == "swide":
                act(R("ch", *C), R("cN", *C))
            elif name == "gwide":
                recast(R("ch", *C), R("cN", *C))
            elif name == "list":
                recast(R("lst", *C), R("cN", *C))
            elif name == "mask":
                ts(R("cN", *C), R("r2", *C), 2047, A.bitwise_and)
                if last:
                    recast(R("ycb", *C), R("cN", *C))
                    store(T.yc[:], R("ycb", *C))
            elif name == "key":
                key()
            elif name == "keep":
                keep()
            elif name == "bounds":
                bounds(lo, hi)
            elif name == "vA":
                cp(R("xa", *k), I(X, R(la, lo, hi)))
            elif name == "sA":
                act(R("xa", *k), I(X, R(la, lo, hi)))
            elif name == "x":
                for m in (2 * lo, 2 * lo + 1):
                    term(m, R("eyeb", *C), R("xa", 256 * m, 256 * m + 256))
            elif name == "v":
                part = (32 * lo, 32 * lo + 32)
                for a in range(2):
                    term(2 * lo + a, R(lt + "ab"[part[0] >= EARLY], 0, 128, 1, part), R("exn", 256 * a, 256 * a + 256, 1, part))
            elif name == "size":
                act(R("ad", *banks[lo]), R("y%d" % lo, 0, 512), AF.Abs)
            elif name == "vsize":
                op("v", lambda: g.vector.tensor_reduce(ap(R("ad", *banks[lo])), T["y%d" % lo][:], AxisListType.X, A.max, apply_absolute_value=True),
                   [R("ad", *banks[lo])], [R("y%d" % lo, 0, 512)])
            elif name == "sum":
                for q in range(4):
                    mm(R("y%d" % lo, 0, 128, (4 * q, 4 * q + 4)), R("ad", 512 * lo + 128 * q, 512 * lo + 128 * q + 128), R("ind4", 0, 32), True, True)
            elif name == "less":
                tt(R("bb", 128 * lo, 128 * lo + 128), R("y%d" % lo, 0, 128), R("lim", *C), A.is_gt)
            elif name == "count":
                o = R(counts, 256 + 2 * lo, 258 + 2 * lo)
                mm(o, R("eye", *C), R("spare", 8 * last + 2 * lo, 8 * last + 2 * lo + 2), True)
                mm(o, R("bb", 128 * lo, 128 * lo + 128), R("ind2", 0, 2), False, True)
            elif name == "back":
                tt(R("back", *cols), places(lv, *rows), R("shift", *cols), A.subtract)
            elif name == "let":
                tt(R("of", *cols), R(counts, 256 + cols[0], 256 + cols[1]), R("back", *cols) if last else places(lv, *rows), A.max)
            elif name == "named":
                cp(I(EW, R("of", *cols)), R(lv, 136 + rows[0], 136 + rows[1]))
            elif name == "write":
                a = PAD + 512 * lo
                cp(I(R("xtab", a, a + WIN), R("of", *cols)), R(lv, *rows))
            elif name == "out":
                store(T.yx[:, 512 * lo:512 * hi], R("xtab", PAD + 512 * lo, PAD + 512 * hi))
            else:
                raise ValueError(word)
    g.wait_ge(T.sem.loc, sent[0])
    for k in range(stored[0]):
        g.sync.wait_ge(T.sem["out%d" % k], 16)
    for q in "vspg":
        if seen["y"].get(q, 0) < count[q]:
            g.sync.wait_ge(T.sem["q" + q], count[q])
